import numpy as np, ml_dtypes
CORES = [9,25,41,57]
N = 4
BF = ml_dtypes.bfloat16
def gentries(a):
    return np.ascontiguousarray(a.reshape(8, 16, -1).transpose(0, 2, 1)).reshape(8, -1)
def gtable(e):
    e = np.asarray(e); return np.ascontiguousarray(e.reshape(8, -1, 16).transpose(0, 2, 1)).reshape(128, -1).astype(np.int32)
W, NW, P, RO, F = 4096, 256, 16, 4, 1
S = W // NW
def parts(rng):
    x = rng.integers(0, 16, (N, 8, 16, W)); l = rng.integers(0, W, (N, 8, NW, P))
    n = np.where(rng.random((N, 8, NW)) < 0.12, rng.integers(0, P + 1, (N, 8, NW)), rng.integers(P // 2, P + 1, (N, 8, NW)))
    return x, l, n, rng.integers(0, 256, (N, 8, 16)), rng.integers(68, 100, (N, 8))
def pack(x, l, n, w, t):
    return {"xv": np.ascontiguousarray(x.reshape(N, 128, W)).astype(np.float32).astype(BF), "wl": np.stack([gtable(a.reshape(8, NW * P)) for a in l]),
            "wn": np.ascontiguousarray(n).astype(np.int32), "wt": np.ascontiguousarray(w.reshape(N, 128, 1)).astype(np.int32), "th": np.ascontiguousarray(t.reshape(N, 8, 1)).astype(np.int32)}
def setup_inputs(rng):
    return pack(*parts(rng))
def setup_inputs_alike(rng):
    x, l, n, w, t = parts(rng)
    l[:, ::2] = rng.choice(np.array([0, W - 1, W // 2, 3]), (N, 4, NW, P))
    l[:, 1] = l[:, 1, :, :1]; x[:, 3] = x[:, 3, :, :1]; w[:, 5] = 0; n[:, 6] = P; t[:, 7] = 0
    return pack(x, l, n, w, t)
def setup_inputs_corners(rng):
    x, l, n, w, t = parts(rng); k = np.arange(P)
    x = rng.integers(0, 4, (N, 8, 16, W)) + 12 * (np.arange(W) & 1); t = rng.integers(48, 144, (N, 8)); t[:, 0] = 48; t[:, 7] = 143
    w = np.where(rng.random((N, 8, 1)) < 0.3, 255 * rng.integers(0, 2, (N, 8, 1)), w)
    n = rng.choice(np.array([0, 1, 2, P - 1, P, P, P, P]), (N, 8, NW)); m = np.minimum(n, rng.choice(np.array([1, 2, P // 2, P // 2 + 1, P - 1, P]), (N, 8, NW)))
    pick = rng.random((8, NW)) < 0.4; a = rng.integers(P // 2, P + 1, (8, NW)); a[:, 0] = P // 2 + 1; a[:, NW - 1] = P; pick[:, 0] = True; pick[:, NW - 1] = True
    for q in range(0, N - 1, 2):
        m[q] = np.where(pick, a, m[q]); n[q] = np.where(pick, np.maximum(a, rng.integers(0, P + 1, (8, NW))), n[q])
        m[q + 1] = np.where(pick, P - a, m[q + 1]); n[q + 1] = np.where(pick, np.where(a == P, 0, np.maximum(P - a, rng.integers(1, P + 1, (8, NW)))), n[q + 1])
    m[0, 5] = P; n[0, 5] = P; m[1, 4] = 0; n[1, 4] = 0
    m[N - 2] = P; n[N - 2] = P; m[N - 1] = 0; n[N - 1] = 0
    for q in (0, 1):
        fr = np.where(pick, 0, m[q]); fr[5] = 0; fr = fr.reshape(-1); o = rng.permutation(8 * NW); b = fr[o]; cut = np.zeros_like(b)
        cut[o] = np.clip((int(np.sum(m[q])) - 256) % 512 - (np.add.accumulate(b) - b), 0, b)
        m[q] = m[q] - cut.reshape(8, NW); n[q] = np.where(m[q] == 0, 0, n[q])
    sc = np.where((k == 0) | (k >= n[..., None]), 2.0, rng.random((N, 8, NW, P)))
    brk = np.argsort(np.argsort(sc, axis=-1), axis=-1) < (m - 1)[..., None]
    cl = (rng.integers(0, 2, (N, 8, NW, 1)) + np.add.accumulate(brk.astype(np.int64), axis=-1)) & 1
    l = np.where(rng.random((N, 8, NW, P)) < 0.1, cl * (W - 1), 2 * rng.integers(0, W // 2, (N, 8, NW, P)) + cl)
    return pack(x, l, n, w, t)
def setup_inputs_ends(rng):
    kind = rng.integers(0, 3, (N, 8, 1, W)); k = np.arange(P); c = np.arange(1, P + 1)
    x = np.where(kind == 0, 0, np.where(kind == 1, 15, 15 * rng.integers(0, 2, (N, 8, 16, W))))
    for u, v in ((0, 15), ((240 * 255) & (W - 1), 0)):
        hh = ((u * u >> 5) + 37 * u + 611 * c) & (W - 1)
        for g in (0, 7): x[:, g][..., hh] = v
    x[..., 0] = 0; x[..., W - 1] = 15
    w = 255 * rng.integers(0, 2, (N, 8, 16)); w[:, 0] = 255; w[:, 7] = 255; w[:, 3, 0] = 0; w[:, 4] = 0
    t = 239 * rng.integers(0, 2, (N, 8)); t[:, 0] = 0; t[:, 1] = 239; t[:, 7] = 239
    kd = rng.integers(0, 4, (N, 8, NW, 1)); s = rng.integers(0, 2, (N, 8, NW, 1)); em = np.where(np.arange(N) == N - 1, 0.05, 0.25).reshape(N, 1, 1)
    kd[N - 1] = np.where(rng.random((8, NW, 1)) < 0.9, 1, kd[N - 1]); kd[:, :, 0] = 1; kd[:, 7, NW - 1] = 1; kd[:, 7, NW - 2] = 0; s[:, 7, NW - 2] = 1
    b = np.where(kd == 0, s, np.where(kd == 1, (k + s) & 1, rng.integers(0, 2, (N, 8, NW, P))))
    n = P * (rng.random((N, 8, NW)) > em).astype(np.int64); n[:, :, 0] = P; n[:, :, 1] = 0; n[:, :, NW - 2] = P; n[:, :, NW - 1] = P
    return pack(x, (W - 1) * b, n, w, t)
def setup_inputs_spread(rng):
    x, l, n, w, t = parts(rng)
    x = (rng.random((N, 8, 16, W)) * np.exp2(rng.integers(0, 5, (N, 8, 1, W)))).astype(np.int64)
    l = np.minimum((W * rng.random((N, 8, NW, P)) ** rng.choice(np.array([0.3, 1.0, 3.0]), (N, 8, 1, 1))).astype(np.int64), W - 1)
    n = rng.integers(0, P + 1, (N, 8, NW)); w = (256 * rng.random((N, 8, 16)) ** 2).astype(np.int64)
    t = np.exp2(7.9 * rng.random((N, 8))).astype(np.int64) - 1
    return pack(x, l, n, w, t)
def setup_inputs_ties(rng):
    x, l, n, w, t = parts(rng)
    lane = np.argsort(rng.random((N, 8, 16)), axis=-1); pm = np.argsort(rng.random((N, 8, W)), axis=-1)
    lev = np.zeros((N, 8, W), np.int64); np.put_along_axis(lev, pm, np.broadcast_to(np.arange(W) % 241, (N, 8, W)), 2)
    x = np.clip(lev[:, :, None, :] - 15 * lane[..., None], 0, 15)
    t = rng.choice(np.array([0, 1, 15, 16, 47, 80, 100]), (N, 8)); s = rng.integers(0, 241, (N, 8, NW))
    for k in range(P):
        l[..., k] = np.take_along_axis(pm, s + 241 * rng.integers(0, W // 241, (N, 8, NW)), 2)
        st = np.abs(t[:, :, None] + rng.integers(-1, 2, (N, 8, NW))); up = ((rng.random((N, 8, NW)) < 0.5) & (s + st <= 240)) | (s - st < 0)
        s = np.where(up, s + st, s - st)
    t[:, 7] = 239
    hl = 239 * ((np.arange(P) + rng.integers(0, 2, (N, NW, 1))) & 1) + rng.integers(0, 2, (N, NW, P)) + 241 * rng.integers(0, W // 241, (N, NW, P))
    l[:, 7] = np.take_along_axis(pm[:, 7], hl.reshape(N, NW * P), 1).reshape(N, NW, P)
    return pack(x, l, n, w, t)
def check_inputs(d):
    bad = []
    for k, lo, hi in (("xv", 0, 15), ("wl", 0, W - 1), ("wn", 0, P), ("wt", 0, 255), ("th", 0, 239)):
        v = np.asarray(d[k]).astype(np.float64)
        if not (np.min(v) >= lo and np.max(v) <= hi): bad.append("range of " + k)
        elif np.any(v != np.floor(v)): bad.append("whole numbers of " + k)
    return bad
def reference(xv, wl, wn, wt, th):
    x = xv.astype(np.int32).reshape(N, 8, 16, W); w = wt.astype(np.int32).reshape(N, 8, 16, 1, 1); lim = th.astype(np.int64).reshape(N, 8, 1, 1)
    l = np.stack([gentries(a) for a in wl]).astype(np.int64).reshape(N, 8, NW, P); n = wn.astype(np.int64)
    last = np.zeros((N, 1, 1, 1), np.int64); k = np.arange(P); M = W - 1
    for t in range(RO):
        if t > 0:
            l = np.roll(l, (1, 1), axis=(0, 1)); n = np.roll(n, (1, 1), axis=(0, 1))
        live = k < n[..., None]
        v = np.take_along_axis(x, l.reshape(N, 8, 1, NW * P), 3).reshape(N, 8, 16, NW, P)
        dist = np.add.reduce(np.abs(v[..., 1:] - v[..., :-1]), axis=2)
        start = live.copy(); start[..., 1:] &= dist > lim
        end = live.copy(); end[..., :-1] &= start[..., 1:] | ~live[..., 1:]
        num = np.add.accumulate(start.astype(np.int64), axis=-1) - 1; m = np.add.reduce(start.astype(np.int64), axis=-1)
        z = v.copy(); c = np.ones((N, 8, NW, P), np.int64); f = l.copy()
        for j in range(1, P):
            s = start[..., j]
            z[..., j] = np.where(s[:, :, None], v[..., j], np.maximum(z[..., j - 1], v[..., j]))
            c[..., j] = np.where(s, 1, c[..., j - 1] + 1); f[..., j] = np.where(s, l[..., j], f[..., j - 1])
        u = np.add.reduce(w * z, axis=2).astype(np.int64) & M
        h = ((u * u >> 5) + 37 * u + 611 * c) & M
        xh = np.take_along_axis(x, h.reshape(N, 8, 1, NW * P), 3).reshape(N, 8, 16, NW, P)
        dd = np.add.reduce(np.abs(xh - z), axis=2).astype(np.int64)
        y = np.zeros((N, 8, NW, 2 * P + 2), np.int64)
        np.put_along_axis(y, np.where(end, 2 * num, 2 * P), ((f * (2 * c + 1) >> 2) + last) & M, 3)
        np.put_along_axis(y, np.where(end, 2 * num + 1, 2 * P + 1), (h + dd * (2 * c + 1)) & M, 3)
        own = np.minimum(2 * m, P); over = np.roll(2 * m - own, 1, axis=0); oy = np.roll(y[..., P:2 * P], 1, axis=0)
        n = np.minimum(own + over, P); o = own[..., None]
        l = np.where(k < o, y[..., :P], np.where(k < n[..., None], np.take_along_axis(oy, np.clip(k - o, 0, P - 1), 3), 0))
        e = np.argmax(end, axis=-1)[..., None]; e5 = e[:, :, None]
        val = ((np.take_along_axis(z, e5, 4) + np.take_along_axis(xh, e5, 4)) >> 1)[..., 0]
        at = (S * np.arange(NW) + (np.take_along_axis(u, e, 3)[..., 0] & (S - 1)))[:, :, None]
        np.put_along_axis(x, at, np.where((m > 0)[:, :, None], val, np.take_along_axis(x, at, 3)), 3)
        last = np.add.reduce(m.reshape(N, 8 * NW), axis=1).reshape(N, 1, 1, 1) & 255
    return {"yx": np.add.reduce(x.reshape(N, 128, W // F, F), axis=3).astype(np.float32).astype(BF), "yl": np.stack([gtable(a.reshape(8, NW * P)) for a in l]).astype(np.float32), "yn": n.astype(np.float32)}

@@ -1,0 +1,613 @@
+from concourse.bass import DstId, RemoteDMATransfer
+from concourse.mybir import dt, AluOpType, AxisListType, ActivationFunctionType
+
+A = AluOpType
+F = ActivationFunctionType
+VISITS = 4
+SCRATCH = {
+    "X": ("sbuf", [128, 8192], "bfloat16"),
+    "ZZ": ("sbuf", [128, 4096], "bfloat16"), "XD": ("sbuf", [128, 4096], "bfloat16"),
+    "QE": ("sbuf", [128, 256], "bfloat16"), "QU": ("sbuf", [128, 256], "bfloat16"), "M0": ("sbuf", [128, 256], "bfloat16"),
+    "WL": ("sbuf", [128, 256], "int32"), "WN": ("sbuf", [8, 256], "int32"), "WT": ("sbuf", [128, 1], "int32"), "TH": ("sbuf", [8, 1], "int32"),
+    "WLF": ("sbuf", [128, 256], "float32"), "WNB": ("sbuf", [8, 256], "bfloat16"), "THB": ("sbuf", [8, 8], "bfloat16"),
+    "CI": ("sbuf", [128, 144], "int32"), "CG": ("sbuf", [128, 144], "int32"), "KI": ("sbuf", [128, 128], "int32"), "CS": ("sbuf", [128, 16], "int32"),
+    "PI": ("sbuf", [128, 4], "int32"), "PQ": ("sbuf", [128, 4], "int32"), "PR_": ("sbuf", [128, 4], "int32"),
+    "KF": ("sbuf", [128, 16], "float32"),
+    "IDB": ("sbuf", [128, 128], "bfloat16"), "NIB": ("sbuf", [128, 128], "bfloat16"), "IDF": ("sbuf", [128, 128], "float32"),
+    "BO": ("sbuf", [128, 128], "bfloat16"), "ZO": ("sbuf", [128, 144], "bfloat16"), "ZW": ("sbuf", [128, 144], "bfloat16"),
+    "SF": ("sbuf", [128, 8], "bfloat16"), "SGF": ("sbuf", [128, 16], "float32"), "SGB": ("sbuf", [128, 8], "bfloat16"), "SGT": ("sbuf", [8, 128], "bfloat16"),
+    "ON": ("sbuf", [128, 128], "bfloat16"), "BIG": ("sbuf", [128, 32], "bfloat16"), "C4K": ("sbuf", [128, 16], "bfloat16"), "ZN": ("sbuf", [128, 144], "bfloat16"), "RS": ("sbuf", [128, 128], "bfloat16"),
+    "BS": ("sbuf", [128, 16], "bfloat16"),
+    "FE": ("sbuf", [128, 16], "uint16"), "TG": ("sbuf", [128, 16], "uint16"),
+    "ZF": ("sbuf", [128, 256], "bfloat16"), "SU": ("sbuf", [128, 256], "int32"), "SV": ("sbuf", [128, 256], "int32"),
+    "AI": ("sbuf", [128, 8], "int32"), "AF": ("sbuf", [128, 8], "float32"),
+    "YL": ("sbuf", [128, 256], "float32"), "YN": ("sbuf", [8, 256], "float32"),
+}
+for _h in (0, 1):
+    SCRATCH["V%d" % _h] = ("sbuf", [128, 2064], "bfloat16")
+    for _n in ("AD", "MK", "AE", "MO"):
+        SCRATCH["%s%d" % (_n, _h)] = ("sbuf", [128, 2048], "bfloat16")
+    SCRATCH["PD%d" % _h] = ("sbuf", [128, 2048], "float32")
+    SCRATCH["OF%d" % _h] = ("sbuf", [128, 128], "uint16")
+    SCRATCH["HU%d" % _h] = ("sbuf", [128, 128], "uint16")
+    SCRATCH["CT%d" % _h] = ("sbuf", [128, 144], "bfloat16")
+    SCRATCH["HB%d" % _h] = ("sbuf", [128, 128 * 16], "bfloat16")
+    SCRATCH["HF%d" % _h] = ("sbuf", [128, 128 * 6], "float32")
+    SCRATCH["HI%d" % _h] = ("sbuf", [128, 128 * 12], "int32")
+for _t in range(VISITS):
+    for _h in (0, 1):
+        SCRATCH["SN%d%d" % (_t, _h)] = ("sbuf", [128, 128], "float32")
+        SCRATCH["SM%d%d" % (_t, _h)] = ("sbuf", [128, 128], "bfloat16")
+        SCRATCH["RO%d%d" % (_t, _h)] = ("sbuf", [128, 64], "float32")
+        SCRATCH["RV%d%d" % (_t, _h)] = ("sbuf", [128, 64], "float32")
+        SCRATCH["RM%d%d" % (_t, _h)] = ("sbuf", [128, 128], "bfloat16")
+for _b in range(8):
+    SCRATCH["pb%d" % _b] = ("psum", [128, 512], "float32")
+ENGS = "VSTG"
+SEMAPHORES = ["e" + e for e in ENGS] + ["sent"] + ["rx%d%d" % (t, h) for t in range(VISITS) for h in (0, 1)] \
+    + ["rm%d%d" % (t, h) for t in range(VISITS) for h in (0, 1)] + ["dm%d" % i for i in range(12)]
+
+CYC, FIX, GAT, SCA, PE, HOP, OWN, NET = 1.0, 30.0, 1.6, 4.0, 0.5, 110.0, 40.0, 2800.0
+
+
+def R(b, c0, c1, step=1, p=128):
+    return (b, c0, c1, step, p)
+
+
+def _n(r):
+    return (r[2] - r[1] + r[3] - 1) // r[3]
+
+
+def _over(a, b):
+    if a[2] <= b[1] or b[2] <= a[1]:
+        return False
+    if a[3] == b[3] and a[3] > 1 and (a[1] - b[1]) % a[3]:
+        return False
+    return True
+
+
+def _wide(b):
+    return 4 if SCRATCH[b][2] in ("float32", "int32") else 2
+
+
+PLAN = {"gv": {0: (), 1: (0, 1, 2, 3)}, "xs": {0: (), 1: (2, 3)}, "bias": {}}
+
+
+def build(g, T, topo, core):
+    ops = []
+    hist = {}
+    banks = {}
+    ndma = [0]
+    stage = [("load", 0, 0)]
+    blast = {}
+
+    def ap(r):
+        if r is None or isinstance(r, (int, float)):
+            return r
+        if len(r) == 2:
+            w, o = r
+            if o is None:
+                return T[w][:]
+            return ap(w).indirect(ap(o))
+        b, c0, c1, st, p = r
+        full = SCRATCH[b][1][1]
+        if st == 1:
+            return T[b][0:p, c0:c1]
+        return T[b][0:p, c0:min(c1, full):st]
+
+    def regs(r):
+        if r is None or isinstance(r, (int, float)):
+            return []
+        if len(r) == 2:
+            return [] if r[1] is None else [r[0], r[1]]
+        return [r]
+
+    def add(eng, fn, reads, writes, cost, grp=None, dma=False, waits=(), after=(), lat=None):
+        i = len(ops)
+        deps = {}
+
+        def dep(j, hard):
+            if j != i:
+                deps[j] = deps.get(j, False) or hard
+        for r in reads:
+            for (q, j, w) in hist.get(r[0], ()):
+                if w and _over(q, r) and not (grp is not None and ops[j]["grp"] == grp):
+                    dep(j, True)
+        for r in writes:
+            for (q, j, w) in hist.get(r[0], ()):
+                if _over(q, r) and not (grp is not None and ops[j]["grp"] == grp):
+                    dep(j, w or ops[j]["eng"] != eng or ops[j]["dma"])
+        for b in set(r[0] for r in list(reads) + list(writes) if r[0][:2] == "pb"):
+            ph = banks.setdefault(b, [None, [], []])
+            if ph[0] != eng:
+                ph[2] = ph[1]
+                ph[0], ph[1] = eng, []
+            ph[1].append(i)
+            for j in ph[2]:
+                dep(j, True)
+        if eng == "T":
+            for b in set(r[0] for r in writes):
+                if b in blast and ops[blast[b]]["grp"] != grp:
+                    dep(blast[b], False)
+                blast[b] = i
+        if grp is not None:
+            for j in range(i - 1, -1, -1):
+                if ops[j]["grp"] == grp:
+                    dep(j, False)
+                    break
+        for j in after:
+            dep(j, False)
+        for r in writes:
+            lst = hist.setdefault(r[0], [])
+            if r[3] == 1:
+                lst[:] = [e for e in lst if not (e[0][1] >= r[1] and e[0][2] <= r[2] and e[0][4] <= r[4])]
+            lst.append((r, i, True))
+        for r in reads:
+            hist.setdefault(r[0], []).append((r, i, False))
+        ops.append({"stage": stage[0], "eng": eng, "fn": fn, "deps": deps, "cost": cost, "grp": grp, "dma": dma, "waits": waits, "lat": lat, "after": after})
+        return i
+
+    def vcost(out, ins, two=False):
+        n = _n(out)
+        w = max(_wide(r[0]) for q in [out] + list(ins) for r in regs(q)[:1])
+        ps = any(r[0][:2] == "pb" for q in ins for r in regs(q))
+        f = (1 if ps else 2) if two else (0.5 if w == 2 and not ps and out[0][:2] != "pb" else 1)
+        for q in ins:
+            if not isinstance(q, (int, float)) and q is not None and len(q) == 2:
+                f = max(f if two is False else 1, GAT)
+        return FIX + CYC * max(64, n * f)
+
+    def tt(out, a, b, op, **kw):
+        return add("V", lambda: g.vector.tensor_tensor(ap(out), ap(a), ap(b), op), regs(a) + regs(b), regs(out), vcost(out, [a, b], True), **kw)
+
+    def ts(out, a, s1, s2, op0, op1=None, **kw):
+        if op1 is None:
+            fn = lambda: g.vector.tensor_scalar(ap(out), ap(a), ap(s1), None, op0)
+        else:
+            fn = lambda: g.vector.tensor_scalar(ap(out), ap(a), ap(s1), ap(s2), op0, op1)
+        return add("V", fn, regs(a) + regs(s1) + regs(s2), regs(out), vcost(out, [a]), **kw)
+
+    def cp(out, a, **kw):
+        if len(out) == 2:
+            return add("V", lambda: g.vector.tensor_copy(ap(out), ap(a)), regs(a) + [out[1]], [out[0]], FIX + CYC * SCA * _n(a), **kw)
+        return add("V", lambda: g.vector.tensor_copy(ap(out), ap(a)), regs(a), regs(out), vcost(out, [a]), **kw)
+
+    def scan(out, d0, d1, op0, op1):
+        return add("V", lambda: g.vector.tensor_tensor_scan(ap(out), ap(d0), ap(d1), 0.0, op0, op1), regs(d0) + regs(d1), regs(out), vcost(out, [d0, d1]))
+
+    def ms(out, val):
+        return add("V", lambda: g.vector.memset(ap(out), val), [], regs(out), vcost(out, []))
+
+    def act(out, a, func, bias=0.0, scale=1.0):
+        n = _n(out) * (GAT if len(a) == 2 else 1)
+        return add("S", lambda: g.scalar.activation(ap(out), ap(a), func, bias=ap(bias), scale=scale), regs(a) + regs(bias), regs(out), FIX + 20 + CYC * max(64, n))
+
+    def mm(out, lhsT, rhs, start=True, stop=True, grp=None, **kw):
+        f = 4 if SCRATCH[lhsT[0]][2] == "float32" else 1
+        return add("T", lambda: g.tensor.matmul(ap(out), ap(lhsT), ap(rhs), start, stop), regs(lhsT) + regs(rhs), regs(out), 8 + PE * f * max(64, _n(rhs)), grp=grp, **kw)
+
+    def dma(q, out, a, cost=2500.0):
+        i = ndma[0]
+        ndma[0] += 1
+        eng = g.sync if q == "Q" else g.scalar
+        return add(q, lambda: eng.dma_start(ap(out), ap(a)), regs(a), regs(out), 100.0, dma="dm%d" % i, lat=cost)
+
+    def io(name, c0=None, c1=None):
+        return (name, None)
+
+    dma("Q", R("WL", 0, 256), ("wl", None))
+    dma("Q", R("X", 0, 4096), ("xv", None), 6000.0)
+    dma("S", R("TH", 0, 1, 1, 8), ("th", None))
+    dma("S", R("WN", 0, 256, 1, 8), ("wn", None))
+    dma("S", R("WT", 0, 1), ("wt", None))
+    add("G", lambda: g.iota(ap(R("CI", 0, 144)), [[1, 144]], 0, 0), [], [R("CI", 0, 144)], 400.0)
+    add("G", lambda: g.iota(ap(R("PI", 0, 1)), [[1, 1]], 0, 1), [], [R("PI", 0, 1)], 150.0)
+    PI = R("PI", 0, 1)
+    PF, PG, T15, KC_, L16, WC, TB, PL = [R("KF", c, c + 1) for c in range(8)]
+    C128 = R("CI", 0, 128)
+    for h in (0, 1):
+        ms(R("V%d" % h, 0, 16), 0.0)
+        ms(R("CT%d" % h, 128, 144), 0.0)
+    ms(R("BIG", 0, 32), 512.0)
+    ms(R("C4K", 0, 16), 4096.0)
+    ms(R("ON", 0, 128), 1.0)
+    cp(PF, PI)
+    ts(R("PQ", 0, 1), PI, 4, None, A.logical_shift_right)
+    ts(R("PR_", 0, 1), PI, 15, None, A.bitwise_and)
+    cp(PG, R("PQ", 0, 1))
+    ts(T15, R("PQ", 0, 1), 16, 15, A.mult, A.add)
+    cp(KC_, R("PR_", 0, 1))
+    ts(L16, R("PR_", 0, 1), 16, None, A.mult)
+    ts(R("CG", 0, 144), R("CI", 0, 144), 4, None, A.logical_shift_right)
+    ts(R("SGT", 0, 128, 1, 8), R("CG", 0, 128, 1, 8), R("KF", 0, 1, 1, 8), None, A.is_equal)
+    ts(R("IDB", 0, 128), C128, PF, None, A.is_equal)
+    ts(R("NIB", 0, 128), C128, PF, -1, A.is_equal, A.mult)
+    ts(R("IDF", 0, 128), C128, PF, None, A.is_equal)
+    ts(R("BO", 0, 128), R("CG", 0, 128), PG, None, A.is_equal)
+    ts(R("ZO", 0, 144), R("CI", 0, 144), T15, None, A.is_equal)
+    ts(R("ZN", 0, 144), R("CI", 0, 144), T15, -4096, A.is_equal, A.mult)
+    ts(R("SF", 0, 8), R("CI", 0, 8), 16, PF, A.mult, A.is_equal)
+    ts(R("CS", 0, 16), R("CI", 0, 16), 7, None, A.bitwise_and)
+    ts(R("SGF", 0, 16), R("CS", 0, 16), PG, None, A.is_equal)
+    ts(R("SGB", 0, 8), R("CI", 0, 8), PG, None, A.is_equal)
+    ts(R("KI", 0, 128), C128, 15, None, A.bitwise_and)
+    ts(R("RS", 0, 128), R("KI", 0, 128), 0, None, A.is_gt)
+    ts(R("BS", 0, 16), R("CI", 0, 16), 256, L16, A.mult, A.add)
+    cp(R("THB", 0, 1, 1, 8), R("TH", 0, 1, 1, 8))
+    cp(R("WNB", 0, 256, 1, 8), R("WN", 0, 256, 1, 8))
+    cp(WC, R("WT", 0, 1))
+    ts(R("ZW", 0, 144), R("CI", 0, 144), T15, WC, A.is_equal, A.mult)
+    mm(R("pb3", 0, 1), R("SGT", 0, 128, 1, 8), R("THB", 0, 1, 1, 8))
+    ts(TB, R("pb3", 0, 1), 0.5, None, A.add)
+
+    def H(kind, h, s, c0=0, c1=128, step=1):
+        return R("%s%d" % (kind, h), 128 * s + c0, 128 * s + c1, step)
+
+    def hb(h, s, *a):
+        return H("HB", h, s, *a)
+
+    def hf(h, s, *a):
+        return H("HF", h, s, *a)
+
+    def hi(h, s, *a):
+        return H("HI", h, s, *a)
+    NL_, LV, EN, CU, CC, S1, G2, CD, CL, EL, E9, T1, OV, GL, UK = range(15)
+    NM, SNM, AA, PP, KC, FN = range(6)
+    JI, NMI, AG, AG2, P1, P1M, UI, U, Y, HH, Q2, Q3 = range(12)
+
+    def pA(h, r):
+        return R("pb%d" % (4 + 2 * h), 128 * r, 128 * r + 128)
+
+    def pB(h, r):
+        return R("pb%d" % (5 + 2 * h), 128 * r, 128 * r + 128)
+    rank = T.rank_of(core)
+    sends = [0]
+
+    def addr(d):
+        dst = T.cores[(rank + d) % 4]
+        rid, pid, _s = topo.addr(dst)
+        return dst, rid, pid
+
+    def start_words(h):
+        w = R("WL", 128 * h, 128 * h + 128)
+        cp(R("OF%d" % h, 0, 128), w)
+        cp(R("WLF", 128 * h, 128 * h + 128), w)
+        mm(pA(h, 0), R("WLF", 128 * h, 128 * h + 128), R("IDF", 0, 128))
+        act(hf(h, NM), pA(h, 0), F.Copy)
+        mm(pB(h, 0), R("WNB", 128 * h, 128 * h + 128, 1, 8), R("SGT", 0, 128, 1, 8))
+        tt(pA(h, 1), pB(h, 0), R("KI", 0, 128), A.is_gt)
+        ts(hb(h, NL_), pA(h, 1), -1, 1, A.mult, A.add)
+
+    def join(h, own, ov, waits, after):
+        tt(hi(h, JI, 0, 64), own, ov, A.add, waits=waits, after=after)
+        ts(hi(h, NMI, 0, 128, 2), hi(h, JI, 0, 64), 12, 4095, A.logical_shift_right, A.bitwise_and)
+        ts(hi(h, NMI, 1, 128, 2), hi(h, JI, 0, 64), 4095, None, A.bitwise_and)
+        cp(hf(h, NM), hi(h, NMI))
+        ts(hb(h, NL_, 0, 128, 2), hi(h, JI, 0, 64), 0, None, A.is_lt)
+        ts(hb(h, NL_, 1, 128, 2), hi(h, JI, 0, 64), 0, None, A.is_lt)
+        act(pA(h, 1), hb(h, NL_), F.Copy, 1.0, -1.0)
+
+    def offsets(h):
+        mm(pB(h, 0), hf(h, NM), R("IDF", 0, 128))
+        cp(R("OF%d" % h, 0, 128), pB(h, 0))
+
+    def mask(h, s):
+        return R("M0", 128 * h, 128 * h + 128) if s == 0 else R("MO%d" % h, 128 * s, 128 * s + 128)
+
+    def front(t, h):
+        stage[0] = ("front", t, h)
+        v, ad, mk = "V%d" % h, "AD%d" % h, "MK%d" % h
+        for c in range(4):
+            o, i = R(v, 16 + 512 * c, 528 + 512 * c), (R("X", 0, 4096), R("OF%d" % h, 32 * c, 32 * c + 32))
+            if c in PLAN["gv"][h]:
+                cp(o, i)
+            else:
+                act(o, i, F.Copy)
+        for c in range(4):
+            b = R("pb%d" % c, 0, 512)
+            gr = ("df", t, h, c)
+            mm(b, R("IDB", 0, 128), R(v, 16 + 512 * c, 528 + 512 * c), True, False, gr)
+            mm(b, R("NIB", 0, 128), R(v, 15 + 512 * c, 527 + 512 * c), False, False, gr)
+            mm(R("pb%d" % c, 0, 512, 16), R("IDB", 0, 128), R("BIG", 0, 32), False, True, gr)
+            act(R(ad, 512 * c, 512 * c + 512), b, F.Abs)
+            mm(b, R("BO", 0, 128), R(ad, 512 * c, 512 * c + 512))
+            act(R(mk, 512 * c, 512 * c + 512), b, F.Sign, TB, -1.0)
+            scan(R("ZZ", 2048 * h + 512 * c, 2048 * h + 512 * c + 512), R(mk, 512 * c, 512 * c + 512), R(v, 16 + 512 * c, 528 + 512 * c), A.mult, A.max)
+        for k in range(16):
+            mm(R("pb%d" % (4 + 2 * h), k, 128, 16), R(mk, k, 2048, 16), R("SF", 0, 8))
+        ct = R("CT%d" % h, 0, 128)
+        tt(ct, pA(h, 0), hb(h, NL_), A.is_gt)
+        tt(hb(h, EN), pA(h, 1), R("CT%d" % h, 1, 129), A.subtract)
+        scan(pA(h, 0), R("RS", 0, 128), hb(h, EN), A.mult, A.add)
+        scan(hb(h, CC), ct, R("ON", 0, 128), A.mult, A.add)
+        tt(hb(h, CD), pA(h, 0), hb(h, EN), A.mult)
+        mm(pA(h, 1), hb(h, CC), R("IDB", 0, 128))
+        mm(pA(h, 2), hb(h, CD), R("IDB", 0, 128))
+        act(hf(h, KC), pA(h, 1), F.Copy, 0.0, 19552.0)
+        act(hb(h, GL), pA(h, 1), F.Copy, 1.0, 2.0)
+        act(hb(h, CL), pA(h, 2), F.Copy)
+        act(hb(h, EL), hb(h, CL), F.Sign)
+        mm(pA(h, 0), R("BO", 0, 128), hb(h, EL))
+        sm = R("SM%d%d" % (t, h), 0, 128)
+        act(sm, pA(h, 0), F.Copy)
+        dst, rid, pid = addr(-1)
+        es = topo.engines(core, dst)
+        m = 0
+        for e in es[:8]:
+            m |= 1 << e
+        rm = "RM%d%d" % (t, h)
+        snd = add("G", lambda: g.remote_dma(out_ap=T[rm][:], in_ap=ap(sm), remote_sem=T.sem["rm%d%d" % (t, h)], local_sem=T.sem["sent"], pid=pid, routing_id=rid, dma_engine_mask=m),
+                  [sm], [], 1000.0, dma="sent", lat=NET)
+        sends[0] += 8
+        for s in range(8):
+            ts(mask(h, s), hb(h, CL), s + 1, None, A.is_equal)
+        ts(hb(h, E9), hb(h, CL), 9, 100, A.is_lt, A.mult)
+        gr = ("ov", t, h)
+        mm(pA(h, 1), R("IDB", 0, 128), hb(h, CL), True, False, gr)
+        mm(pA(h, 1), R("NIB", 0, 128), hb(h, E9), False, False, gr)
+        mm(pA(h, 1), R("IDB", 0, 128), R(rm, 0, 128), False, True, gr, waits=[("rm%d%d" % (t, h), 8)], after=[snd])
+        act(hb(h, OV), pA(h, 1), F.Copy)
+        for s in range(8):
+            ts(R("MO%d" % h, 1024 + 128 * s, 1152 + 128 * s), hb(h, OV), s + 9, None, A.is_equal)
+
+    def middle(t, h):
+        stage[0] = ("middle", t, h)
+        gr = ("u", t, h)
+        for k in range(16):
+            mm(pB(h, 0), R("ZW", 15 - k, 143 - k), R("ZZ", 2048 * h + k, 2048 * h + 2048, 16), k == 0, k == 15, gr)
+        cp(hi(h, UI), pB(h, 0))
+        ts(hi(h, U), hi(h, UI), 4095, None, A.bitwise_and)
+        ts(pB(h, 1), hi(h, U), 1184, None, A.add)
+        tt(pB(h, 2), pB(h, 1), hi(h, U), A.mult)
+        tt(hi(h, Y), pB(h, 2), hf(h, KC), A.add)
+        ts(hi(h, HH), hi(h, Y), 5, 4095, A.logical_shift_right, A.bitwise_and)
+        cp(R("HU%d" % h, 0, 128), hi(h, HH))
+        for c in range(4):
+            a, b = 2048 * h + 512 * c, 2048 * h + 512 * c + 512
+            x = (R("X", 0, 4096), R("HU%d" % h, 32 * c, 32 * c + 32))
+            ae = R("AE%d" % h, 512 * c, 512 * c + 512)
+            if c in PLAN["xs"][h]:
+                act(R("XD", a, b), x, F.Copy)
+                pb, gr = R("pb%d" % c, 0, 512), ("xd", t, h, c)
+                mm(pb, R("IDB", 0, 128), R("XD", a, b), True, False, gr)
+                mm(pb, R("NIB", 0, 128), R("ZZ", a, b), False, True, gr)
+                act(ae, pb, F.Abs)
+            else:
+                tt(R("XD", a, b), x, R("ZZ", a, b), A.subtract)
+                act(ae, R("XD", a, b), F.Abs)
+        stage[0] = ("first", t, h)
+        ts(hi(h, UI), hi(h, U), 15, None, A.bitwise_and)
+        tt(R("QU", 128 * h, 128 * h + 128), hi(h, UI), mask(h, 0), A.mult)
+        ts(R("QE", 128 * h, 128 * h + 128), mask(h, 0), KC_, None, A.mult)
+        stage[0] = ("names", t, h)
+        ct = R("CT%d" % h, 0, 128)
+        act(pB(h, 2), ct, F.Copy, 1.0, -1.0)
+        tt(hf(h, SNM), pB(h, 2), hf(h, NM), A.mult)
+        scan(pB(h, 3), ct, hf(h, SNM), A.mult, A.add)
+        act(hb(h, G2), hb(h, CC), F.Copy, 1.0, 2.0)
+        tt(hi(h, AG), pB(h, 3), hb(h, G2), A.mult)
+        if t == 0:
+            ts(hi(h, P1M), hi(h, AG), 2, 4095, A.logical_shift_right, A.bitwise_and)
+        else:
+            ts(hi(h, AG2), hi(h, AG), 2, None, A.logical_shift_right)
+            ts(hi(h, P1), hi(h, AG2), R("AF", t, t + 1), None, A.add)
+            ts(hi(h, P1M), hi(h, P1), 4095, None, A.bitwise_and)
+        ts(hf(h, PP), hi(h, P1M), 4096, 1, A.mult, A.add)
+        mm(pA(h, 3), hf(h, PP), R("IDF", 0, 128))
+
+    def write(t):
+        stage[0] = ("write", t, 0)
+        fe, tg = R("pb3", 0, 16), R("pb2", 0, 16)
+        g1, g2 = ("fe", t), ("tg", t)
+        for k in range(16):
+            mm(fe, R("ZO", 15 - k, 143 - k), R("QE", k, 256, 16), k == 0, False, g1)
+        mm(fe, R("IDB", 0, 128), R("BS", 0, 16), False, True, g1)
+        for k in range(16):
+            mm(tg, R("ZO", 15 - k, 143 - k), R("QU", k, 256, 16), k == 0, False, g2)
+            mm(tg, R("ZN", 15 - k, 143 - k), R("M0", k, 256, 16), False, False, g2)
+        mm(tg, R("IDB", 0, 128), R("BS", 0, 16), False, False, g2)
+        mm(tg, R("IDB", 0, 128), R("C4K", 0, 16), False, True, g2)
+        cp(R("FE", 0, 16), fe)
+        cp(R("TG", 0, 16), tg)
+        seg = [1.0 if c % 4 in PLAN["xs"][c // 4] else 2.0 for c in range(8)]
+        c0 = 0
+        for c in range(1, 9):
+            if c == 8 or seg[c] != seg[c0]:
+                act(R("ZF", 32 * c0, 32 * c), (R("ZZ", 0, 4096), R("FE", 2 * c0, 2 * c)), F.Copy, 0.0, seg[c0])
+                c0 = c
+        tt(R("SU", 0, 256), (R("XD", 0, 4096), R("FE", 0, 16)), R("ZF", 0, 256), A.add)
+        ts(R("SV", 0, 256), R("SU", 0, 256), 1, None, A.arith_shift_right)
+        cp((R("X", 0, 8192), R("TG", 0, 16)), R("SV", 0, 256))
+        if t < VISITS - 1:
+            for h in (0, 1):
+                mm(R("pb1", 0, 128), R("ON", 0, 128), hb(h, EN), h == 0, h == 1, ("a", t))
+            add("V", lambda: g.vector.tensor_reduce(ap(R("AF", 4 + t, 5 + t)), ap(R("pb1", 0, 128)), axis=AxisListType.X, op=A.add), [R("pb1", 0, 128)], [R("AF", 4 + t, 5 + t)], FIX + 128)
+            cp(R("AI", 0, 1), R("AF", 4 + t, 5 + t))
+            ts(R("AI", 1, 2), R("AI", 0, 1), 255, None, A.bitwise_and)
+            cp(R("AF", t + 1, t + 2), R("AI", 1, 2))
+
+    def back(t, h):
+        stage[0] = ("back", t, h)
+        gr = ("d", t, h)
+        for k in range(16):
+            mm(pB(h, 3), R("ZO", 15 - k, 143 - k), R("AE%d" % h, k, 2048, 16), k == 0, k == 15, gr)
+        tt(pB(h, 1), pB(h, 3), hb(h, GL), A.mult)
+        tt(hi(h, Q2), pB(h, 1), hi(h, HH), A.add)
+        ts(hi(h, Q3), hi(h, Q2), 4095, None, A.bitwise_and)
+        tt(pB(h, 2), pA(h, 3), hi(h, Q3), A.add)
+        last = t == VISITS - 1
+        sg = R("SGF", 0, 8) if last else R("SGF", 7, 15)
+        bank = "pb%d" % (4 + 2 * h)
+        for s in (list(range(8, 16)) + list(range(8)) if last else range(16)):
+            pr = R("PD%d" % h, 128 * s, 128 * s + 128)
+            tt(pr, pB(h, 2), mask(h, s), A.mult)
+            o = 64 * (s // 8)
+            mm(R(bank, o + s % 8, o + 64, 8), pr, sg)
+        sn = "SN%d%d" % (t, h)
+        act(R(sn, 0, 64), R(bank, 0, 64), F.Copy, -1.0)
+        act(R(sn, 64, 128), R(bank, 64, 128), F.Copy)
+        ro, rv, rx = "RO%d%d" % (t, h), "RV%d%d" % (t, h), "rx%d%d" % (t, h)
+        d1, r1, p1 = addr(1)
+        d2, r2, p2 = addr(2)
+        e1, e2 = topo.engines(core, d1), topo.engines(core, d2)
+        if last:
+            m = 0
+            for e in e1[:8]:
+                m |= 1 << e
+            sends[0] += 8
+            return add("G", lambda: g.remote_dma(out_ap=T[rv][:], in_ap=ap(R(sn, 64, 128)), remote_sem=T.sem[rx], local_sem=T.sem["sent"], pid=p1, routing_id=r1, dma_engine_mask=m),
+                       [R(sn, 64, 128)], [], 1000.0, dma="sent", lat=NET)
+        m1 = m2 = 0
+        for e in e1[:4]:
+            m1 |= 1 << e
+        for e in [e for e in e2 if e not in e1[:4]][:4]:
+            m2 |= 1 << e
+        sends[0] += 8
+
+        def fused():
+            return g.remote_dma_fused([
+                RemoteDMATransfer(dst_ids=[DstId(rid=r1, pnc=p1)], dma_engine_mask=m1, remote_sem=T.sem[rx], src=ap(R(sn, 0, 64)), dst=T[ro][:]),
+                RemoteDMATransfer(dst_ids=[DstId(rid=r2, pnc=p2)], dma_engine_mask=m2, remote_sem=T.sem[rx], src=ap(R(sn, 64, 128)), dst=T[rv][:]),
+            ], local_sem=T.sem["sent"])
+        return add("G", fused, [R(sn, 0, 128)], [], 1200.0, dma="sent", lat=NET)
+
+    arr = {}
+    for t in range(VISITS):
+        for h in (0, 1):
+            if t == 0:
+                start_words(h)
+            else:
+                stage[0] = ("join", t, h)
+                q = "%d%d" % (t - 1, h)
+                join(h, R("RO" + q, 0, 64), R("RV" + q, 0, 64), [("rx" + q, 8)], [arr[h]])
+                offsets(h)
+        for h in (0, 1):
+            front(t, h)
+            middle(t, h)
+        write(t)
+        for h in (0, 1):
+            arr[h] = back(t, h)
+    dma("Q", ("yx", None), R("X", 0, 4096), 6000.0)
+    for h in (0, 1):
+        stage[0] = ("join", VISITS, h)
+        q = "%d%d" % (VISITS - 1, h)
+        join(h, R("SN" + q, 0, 64), R("RV" + q, 0, 64), [("rx" + q, 8)], [arr[h]])
+        ts(hf(h, SNM), hi(h, NMI), 1, None, A.add)
+        tt(hf(h, FN), pA(h, 1), hf(h, SNM), A.mult)
+        mm(pB(h, 0), hf(h, FN), R("IDF", 0, 128))
+        ts(R("YL", 128 * h, 128 * h + 128), pB(h, 0), -1, 0, A.add, A.max)
+        ts(hb(h, EL), pB(h, 0), 0.5, None, A.is_gt)
+        mm(R("pb%d" % (4 + 2 * h), 0, 128, 1, 8), R("SGB", 0, 8), hb(h, EL))
+        act(R("YN", 128 * h, 128 * h + 128, 1, 8), R("pb%d" % (4 + 2 * h), 0, 128, 1, 8), F.Copy)
+    dma("Q", ("yl", None), R("YL", 0, 256))
+    dma("Q", ("yn", None), R("YN", 0, 256, 1, 8))
+    return ops, sends[0]
+
+
+def schedule(ops):
+    n = len(ops)
+    succ = [[] for _ in range(n)]
+    npred = [0] * n
+
+    def lag(j, i, hard):
+        a, b = ops[j], ops[i]
+        if not hard and j not in b["after"]:
+            return None
+        if a["lat"] is not None:
+            return a["cost"] + a["lat"]
+        return a["cost"] + (OWN if a["eng"] == b["eng"] else HOP)
+    for i in range(n):
+        for j, hard in ops[i]["deps"].items():
+            succ[j].append((i, lag(j, i, hard)))
+            npred[i] += 1
+    prio = [0.0] * n
+    for i in range(n - 1, -1, -1):
+        best = ops[i]["cost"]
+        for (k, lg) in succ[i]:
+            best = max(best, prio[k] + (lg if lg is not None else 0.0))
+        prio[i] = best
+    for i in range(n):
+        s = ops[i]["stage"]
+        prio[i] += PLAN["bias"].get((s[0], s[2]), 0.0)
+    ready = {e: [] for e in "VSTGQ"}
+    at = [0.0] * n
+    for i in range(n):
+        if npred[i] == 0:
+            ready[ops[i]["eng"]].append(i)
+    free = {e: 0.0 for e in ready}
+    order = []
+    start = [0.0] * n
+    while len(order) < n:
+        best = None
+        for e in ready:
+            if not ready[e]:
+                continue
+            t0 = min(max(free[e], at[i]) for i in ready[e])
+            if best is None or t0 < best[0]:
+                best = (t0, e)
+        t0, e = best
+        i = max((k for k in ready[e] if max(free[e], at[k]) <= t0 + 1e-9), key=lambda k: (prio[k], -k))
+        ready[e].remove(i)
+        start[i] = t0
+        order.append(i)
+        free[e] = t0 + ops[i]["cost"]
+        for (k, lg) in succ[i]:
+            at[k] = max(at[k], t0 + (lg if lg is not None else 0.0))
+            npred[k] -= 1
+            if npred[k] == 0:
+                ready[ops[k]["eng"]].append(k)
+    return order, start, free
+
+
+def rank_program(g, core, T, topo):
+    if T.rank_of(core) is None:
+        return
+    ops, nsent = build(g, T, topo, core)
+    order, start, free = schedule(ops)
+    queue = {"V": g.vector, "S": g.scalar, "T": g.tensor, "G": g, "Q": g.sync}
+    need = set()
+    for i in order:
+        for j, hard in ops[i]["deps"].items():
+            if hard and not ops[j]["dma"]:
+                need.add(j)
+    count = {e: 0 for e in queue}
+    mark = {}
+    know = {e: {} for e in queue}
+    snap = {}
+    for i in order:
+        o = ops[i]
+        e = o["eng"]
+        want = {}
+        for j, hard in o["deps"].items():
+            if not hard or ops[j]["dma"] == "sent":
+                continue
+            s, v = mark[j]
+            if know[e].get(s, 0) < v:
+                want.setdefault(s, []).append((v, j))
+        todo = sorted(((max(l)[0], s, max(l)[1]) for s, l in want.items()), key=lambda x: -start[x[2]])
+        for v, s, j in todo:
+            if know[e].get(s, 0) >= v:
+                continue
+            queue[e].wait_ge(T.sem[s], v)
+            know[e][s] = v
+            for s2, v2 in snap[j].items():
+                if know[e].get(s2, 0) < v2:
+                    know[e][s2] = v2
+        for (s, v) in o["waits"]:
+            queue[e].wait_ge(T.sem[s], v)
+        ins = o["fn"]()
+        snap[i] = dict(know[e])
+        if o["dma"] and o["dma"] != "sent":
+            ins.then_inc(T.sem[o["dma"]], 16)
+            mark[i] = (o["dma"], 16)
+        elif i in need:
+            count[e] += 1
+            ins.then_inc(T.sem["e" + e], 1)
+            mark[i] = ("e" + e, count[e])
+    for e in ENGS:
+        if count[e]:
+            g.wait_ge(T.sem["e" + e], count[e])
+    g.wait_ge(T.sem["sent"], nsent)
+    for o in ops:
+        if o["dma"] and o["dma"] != "sent":
+            g.wait_ge(T.sem[o["dma"]], 16)

@@ -4,50 +4,57 @@ from concourse.mybir import dt, AluOpType, AxisListType, ActivationFunctionType
 A = AluOpType
 F = ActivationFunctionType
 VISITS = 4
+DEAD, JUNK = 4096, 4352
+BF, F32, I32, U16 = "bfloat16", "float32", "int32", "uint16"
 SCRATCH = {
-    "X": ("sbuf", [128, 8192], "bfloat16"),
-    "ZZ": ("sbuf", [128, 4096], "bfloat16"), "XD": ("sbuf", [128, 4096], "bfloat16"),
-    "QE": ("sbuf", [128, 256], "bfloat16"), "QU": ("sbuf", [128, 256], "bfloat16"), "M0": ("sbuf", [128, 256], "bfloat16"),
-    "WL": ("sbuf", [128, 256], "int32"), "WN": ("sbuf", [8, 256], "int32"), "WT": ("sbuf", [128, 1], "int32"), "TH": ("sbuf", [8, 1], "int32"),
-    "WLF": ("sbuf", [128, 256], "float32"), "WNB": ("sbuf", [8, 256], "bfloat16"), "THB": ("sbuf", [8, 8], "bfloat16"),
-    "CI": ("sbuf", [128, 144], "int32"), "CG": ("sbuf", [128, 144], "int32"), "KI": ("sbuf", [128, 128], "int32"), "CS": ("sbuf", [128, 16], "int32"),
-    "PI": ("sbuf", [128, 4], "int32"), "PQ": ("sbuf", [128, 4], "int32"), "PR_": ("sbuf", [128, 4], "int32"),
-    "KF": ("sbuf", [128, 16], "float32"),
-    "IDB": ("sbuf", [128, 128], "bfloat16"), "NIB": ("sbuf", [128, 128], "bfloat16"), "IDF": ("sbuf", [128, 128], "float32"),
-    "BO": ("sbuf", [128, 128], "bfloat16"), "ZO": ("sbuf", [128, 144], "bfloat16"), "ZW": ("sbuf", [128, 144], "bfloat16"),
-    "SF": ("sbuf", [128, 8], "bfloat16"), "SGF": ("sbuf", [128, 16], "float32"), "SGB": ("sbuf", [128, 8], "bfloat16"), "SGT": ("sbuf", [8, 128], "bfloat16"),
-    "ON": ("sbuf", [128, 128], "bfloat16"), "BIG": ("sbuf", [128, 32], "bfloat16"), "C4K": ("sbuf", [128, 16], "bfloat16"), "ZN": ("sbuf", [128, 144], "bfloat16"), "RS": ("sbuf", [128, 128], "bfloat16"),
-    "BS": ("sbuf", [128, 16], "bfloat16"),
-    "FE": ("sbuf", [128, 16], "uint16"), "TG": ("sbuf", [128, 16], "uint16"),
-    "ZF": ("sbuf", [128, 256], "bfloat16"), "SU": ("sbuf", [128, 256], "int32"), "SV": ("sbuf", [128, 256], "int32"),
-    "AI": ("sbuf", [128, 8], "int32"), "AF": ("sbuf", [128, 8], "float32"),
-    "YL": ("sbuf", [128, 256], "float32"), "YN": ("sbuf", [8, 256], "float32"),
+    "X": ("sbuf", [128, JUNK + 4096], BF),
+    "ZZ": ("sbuf", [128, 4096], BF), "XD": ("sbuf", [128, 4096], BF), "M0": ("sbuf", [128, 256], BF),
+    "WL": ("sbuf", [128, 256], I32), "WN": ("sbuf", [8, 256], I32), "WT": ("sbuf", [128, 1], I32), "TH": ("sbuf", [8, 1], I32),
+    "WNB": ("sbuf", [8, 256], BF), "THM": ("sbuf", [8, 128], BF), "SD": ("sbuf", [128, 32], BF),
+    "CI": ("sbuf", [128, 144], I32), "CG": ("sbuf", [128, 144], I32), "KI": ("sbuf", [128, 128], I32), "CD": ("sbuf", [128, 128], I32), "CS": ("sbuf", [128, 32], I32),
+    "PI": ("sbuf", [128, 8], I32), "KF": ("sbuf", [128, 32], F32),
+    "EQ": ("sbuf", [128, 24], F32), "T2": ("sbuf", [128, 144], BF),
+    "IDF": ("sbuf", [128, 128], F32), "DUP": ("sbuf", [128, 128], F32), "SGF": ("sbuf", [128, 16], F32), "SGD": ("sbuf", [128, 32], F32), "O16": ("sbuf", [128, 128], F32),
+    "BK": ("sbuf", [128, 1024], BF), "SGB": ("sbuf", [128, 8], BF), "SG32": ("sbuf", [128, 8], BF), "WG": ("sbuf", [128, 8], BF), "SGT": ("sbuf", [8, 128], BF),
+    "BS": ("sbuf", [128, 16], BF), "FE": ("sbuf", [128, 16], U16), "TG": ("sbuf", [128, 16], U16), "UA": ("sbuf", [128, 48], I32),
+    "ZF": ("sbuf", [128, 256], BF), "SU": ("sbuf", [128, 256], BF), "SV": ("sbuf", [128, 256], I32),
+    "AI": ("sbuf", [128, 8], I32), "AF": ("sbuf", [128, 8], F32), "AC": ("sbuf", [128, 8], F32),
+    "YL": ("sbuf", [128, 256], F32), "YN": ("sbuf", [8, 256], F32),
 }
+MATS = ("IDB", "I17", "I50", "BO", "SAME", "PAT", "WX", "N16", "ON", "C3", "C512") + tuple(n + e for n in ("NBO", "SH", "SH32", "TRI", "TRD") for e in "EO")
+SCRATCH["CM"] = ("sbuf", [128, 128 * len(MATS)], BF)
+for _n in ("ZO", "ZW", "ZK", "ZN"):
+    SCRATCH[_n] = ("sbuf", [128, 144], BF)
 for _h in (0, 1):
-    SCRATCH["V%d" % _h] = ("sbuf", [128, 2064], "bfloat16")
-    for _n in ("AD", "MK", "AE", "MO"):
-        SCRATCH["%s%d" % (_n, _h)] = ("sbuf", [128, 2048], "bfloat16")
-    SCRATCH["PD%d" % _h] = ("sbuf", [128, 2048], "float32")
-    SCRATCH["OF%d" % _h] = ("sbuf", [128, 128], "uint16")
-    SCRATCH["HU%d" % _h] = ("sbuf", [128, 128], "uint16")
-    SCRATCH["CT%d" % _h] = ("sbuf", [128, 144], "bfloat16")
-    SCRATCH["HB%d" % _h] = ("sbuf", [128, 128 * 16], "bfloat16")
-    SCRATCH["HF%d" % _h] = ("sbuf", [128, 128 * 6], "float32")
-    SCRATCH["HI%d" % _h] = ("sbuf", [128, 128 * 12], "int32")
+    SCRATCH["KW%d" % _h] = ("sbuf", [128, 136], BF)
+    SCRATCH["K2%d" % _h] = ("sbuf", [128, 256], BF)
+    SCRATCH["V%d" % _h] = ("sbuf", [128, 2064], BF)
+    for _n in ("MN", "MK", "AE", "XH"):
+        SCRATCH["%s%d" % (_n, _h)] = ("sbuf", [128, 2048], BF)
+    SCRATCH["MO%d" % _h] = ("sbuf", [128, 128 * 12], BF)
+    SCRATCH["PD%d" % _h] = ("sbuf", [128, 128 * 12], F32)
+    SCRATCH["OF%d" % _h] = ("sbuf", [128, 128], U16)
+    SCRATCH["HU%d" % _h] = ("sbuf", [128, 128], U16)
+    SCRATCH["HB%d" % _h] = ("sbuf", [128, 128 * 8], BF)
+    SCRATCH["HF%d" % _h] = ("sbuf", [128, 128 * 8], F32)
+    SCRATCH["HI%d" % _h] = ("sbuf", [128, 128 * 8], I32)
 for _t in range(VISITS):
     for _h in (0, 1):
-        SCRATCH["SN%d%d" % (_t, _h)] = ("sbuf", [128, 128], "float32")
-        SCRATCH["SM%d%d" % (_t, _h)] = ("sbuf", [128, 128], "bfloat16")
-        SCRATCH["RO%d%d" % (_t, _h)] = ("sbuf", [128, 64], "float32")
-        SCRATCH["RV%d%d" % (_t, _h)] = ("sbuf", [128, 64], "float32")
-        SCRATCH["RM%d%d" % (_t, _h)] = ("sbuf", [128, 128], "bfloat16")
+        SCRATCH["SN%d%d" % (_t, _h)] = ("sbuf", [128, 128], F32)
+        SCRATCH["SM%d%d" % (_t, _h)] = ("sbuf", [128, 128], BF)
+        SCRATCH["RO%d%d" % (_t, _h)] = ("sbuf", [128, 64], F32)
+        SCRATCH["RV%d%d" % (_t, _h)] = ("sbuf", [128, 64], F32)
+        SCRATCH["RM%d%d" % (_t, _h)] = ("sbuf", [128, 128], BF)
 for _b in range(8):
-    SCRATCH["pb%d" % _b] = ("psum", [128, 512], "float32")
+    SCRATCH["pb%d" % _b] = ("psum", [128, 512], F32)
 ENGS = "VSTG"
 SEMAPHORES = ["e" + e for e in ENGS] + ["sent"] + ["rx%d%d" % (t, h) for t in range(VISITS) for h in (0, 1)] \
     + ["rm%d%d" % (t, h) for t in range(VISITS) for h in (0, 1)] + ["dm%d" % i for i in range(12)]
 
-CYC, FIX, GAT, SCA, PE, HOP, OWN, NET = 1.0, 30.0, 1.6, 4.0, 0.5, 110.0, 40.0, 2800.0
+CYC, FIX, GAT, SCA, PE, HOP, OWN, NET = 0.9, 30.0, 1.56, 3.8, 0.45, 100.0, 40.0, 2800.0
+PLAN = {"gv": ("SSVS", "VSSS"), "gh": ("VSSS", "VVSS"), "mk": ("PPPP", "PPPP"), "wait": 30.0, "um": "SS", "hm": "VS", "turns": 3,
+        "bias": {"back0": 2500, "front1": -5700, "names1": 1700, "places0": -1300, "front0": -3400, "places1": -2500, "back1": 3700,
+                 "write0": 4900, "middle0": -2500, "count0": 4800, "names0": 4200, "count1": -3700}}
 
 
 def R(b, c0, c1, step=1, p=128):
@@ -67,10 +74,7 @@ def _over(a, b):
 
 
 def _wide(b):
-    return 4 if SCRATCH[b][2] in ("float32", "int32") else 2
-
-
-PLAN = {"gv": {0: (), 1: (0, 1, 2, 3)}, "xs": {0: (), 1: (2, 3)}, "bias": {}}
+    return 4 if SCRATCH[b][2] in (F32, I32) else 2
 
 
 def build(g, T, topo, core):
@@ -80,6 +84,7 @@ def build(g, T, topo, core):
     ndma = [0]
     stage = [("load", 0, 0)]
     blast = {}
+    glast = {}
 
     def ap(r):
         if r is None or isinstance(r, (int, float)):
@@ -90,7 +95,7 @@ def build(g, T, topo, core):
                 return T[w][:]
             return ap(w).indirect(ap(o))
         b, c0, c1, st, p = r
-        full = SCRATCH[b][1][1]
+        full = T[b].shape[1]
         if st == 1:
             return T[b][0:p, c0:c1]
         return T[b][0:p, c0:min(c1, full):st]
@@ -100,7 +105,7 @@ def build(g, T, topo, core):
             return []
         if len(r) == 2:
             return [] if r[1] is None else [r[0], r[1]]
-        return [r]
+        return [r] if r[0] in SCRATCH else []
 
     def add(eng, fn, reads, writes, cost, grp=None, dma=False, waits=(), after=(), lat=None):
         i = len(ops)
@@ -116,7 +121,7 @@ def build(g, T, topo, core):
         for r in writes:
             for (q, j, w) in hist.get(r[0], ()):
                 if _over(q, r) and not (grp is not None and ops[j]["grp"] == grp):
-                    dep(j, w or ops[j]["eng"] != eng or ops[j]["dma"])
+                    dep(j, True)
         for b in set(r[0] for r in list(reads) + list(writes) if r[0][:2] == "pb"):
             ph = banks.setdefault(b, [None, [], []])
             if ph[0] != eng:
@@ -131,10 +136,9 @@ def build(g, T, topo, core):
                     dep(blast[b], False)
                 blast[b] = i
         if grp is not None:
-            for j in range(i - 1, -1, -1):
-                if ops[j]["grp"] == grp:
-                    dep(j, False)
-                    break
+            if grp in glast:
+                dep(glast[grp], False)
+            glast[grp] = i
         for j in after:
             dep(j, False)
         for r in writes:
@@ -148,13 +152,12 @@ def build(g, T, topo, core):
         return i
 
     def vcost(out, ins, two=False):
-        n = _n(out)
+        n = max(_n(q) if len(q) == 5 else _n(out) for q in ins[:1] or [out])
         w = max(_wide(r[0]) for q in [out] + list(ins) for r in regs(q)[:1])
         ps = any(r[0][:2] == "pb" for q in ins for r in regs(q))
-        f = (1 if ps else 2) if two else (0.5 if w == 2 and not ps and out[0][:2] != "pb" else 1)
-        for q in ins:
-            if not isinstance(q, (int, float)) and q is not None and len(q) == 2:
-                f = max(f if two is False else 1, GAT)
+        f = (1 if ps else 2) if two else (0.5 if w == 2 else 1)
+        if ins and len(ins[0]) == 2:
+            f = GAT
         return FIX + CYC * max(64, n * f)
 
     def tt(out, a, b, op, **kw):
@@ -178,13 +181,25 @@ def build(g, T, topo, core):
     def ms(out, val):
         return add("V", lambda: g.vector.memset(ap(out), val), [], regs(out), vcost(out, []))
 
-    def act(out, a, func, bias=0.0, scale=1.0):
+    def act(out, a, func, bias=0.0, scale=1.0, acc=None):
         n = _n(out) * (GAT if len(a) == 2 else 1)
-        return add("S", lambda: g.scalar.activation(ap(out), ap(a), func, bias=ap(bias), scale=scale), regs(a) + regs(bias), regs(out), FIX + 20 + CYC * max(64, n))
+        if func == F.Copy and not isinstance(bias, float):
+            func = F.Identity
+        if acc is None:
+            fn = lambda: g.scalar.activation(ap(out), ap(a), func, bias=ap(bias), scale=scale)
+        else:
+            fn = lambda: g.scalar.activation(ap(out), ap(a), func, bias=ap(bias), scale=scale, accum_out=ap(acc))
+        return add("S", fn, regs(a) + regs(bias), regs(out) + regs(acc), FIX + 15 + CYC * max(64, n))
 
     def mm(out, lhsT, rhs, start=True, stop=True, grp=None, **kw):
-        f = 4 if SCRATCH[lhsT[0]][2] == "float32" else 1
-        return add("T", lambda: g.tensor.matmul(ap(out), ap(lhsT), ap(rhs), start, stop), regs(lhsT) + regs(rhs), regs(out), 8 + PE * f * max(64, _n(rhs)), grp=grp, **kw)
+        f = 4 if SCRATCH[lhsT[0]][2] == F32 else 1
+        return add("T", lambda: g.tensor.matmul(ap(out), ap(lhsT), ap(rhs), start, stop), regs(lhsT) + regs(rhs), regs(out), 5 + PE * f * max(64, _n(rhs)), grp=grp, **kw)
+
+    def msum(out, terms, **kw):
+        gr = ("sum", len(ops))
+        for j, x in enumerate(terms):
+            o, l, r = x if len(x) == 3 else (out,) + tuple(x)
+            mm(o, l, r, j == 0, j == len(terms) - 1, gr, **(kw if j == len(terms) - 1 else {}))
 
     def dma(q, out, a, cost=2500.0):
         i = ndma[0]
@@ -192,53 +207,111 @@ def build(g, T, topo, core):
         eng = g.sync if q == "Q" else g.scalar
         return add(q, lambda: eng.dma_start(ap(out), ap(a)), regs(a), regs(out), 100.0, dma="dm%d" % i, lat=cost)
 
-    def io(name, c0=None, c1=None):
-        return (name, None)
+    def M(n):
+        return R("CM", 128 * MATS.index(n), 128 * MATS.index(n) + 128) if n in MATS else R(n, 0, 128)
 
-    dma("Q", R("WL", 0, 256), ("wl", None))
+    def win(n, k):
+        return R(n, 15 - k, 143 - k)
+
     dma("Q", R("X", 0, 4096), ("xv", None), 6000.0)
-    dma("S", R("TH", 0, 1, 1, 8), ("th", None))
+    dma("S", R("WL", 0, 256), ("wl", None))
     dma("S", R("WN", 0, 256, 1, 8), ("wn", None))
-    dma("S", R("WT", 0, 1), ("wt", None))
+    dma("Q", R("TH", 0, 1, 1, 8), ("th", None))
+    dma("Q", R("WT", 0, 1), ("wt", None))
     add("G", lambda: g.iota(ap(R("CI", 0, 144)), [[1, 144]], 0, 0), [], [R("CI", 0, 144)], 400.0)
     add("G", lambda: g.iota(ap(R("PI", 0, 1)), [[1, 1]], 0, 1), [], [R("PI", 0, 1)], 150.0)
-    PI = R("PI", 0, 1)
-    PF, PG, T15, KC_, L16, WC, TB, PL = [R("KF", c, c + 1) for c in range(8)]
-    C128 = R("CI", 0, 128)
+    PI, PGI, PKI, P8I = [R("PI", c, c + 1) for c in range(4)]
+    PF, PG, T15, KP, L16, WC, P8, KO, CB, CBD, Q1, Q2, P7 = [R("KF", c, c + 1) for c in range(13)]
+    OVC = [R("KF", 20 + j, 21 + j) for j in range(4)]
+    C128, C144 = R("CI", 0, 128), R("CI", 0, 144)
     for h in (0, 1):
         ms(R("V%d" % h, 0, 16), 0.0)
-        ms(R("CT%d" % h, 128, 144), 0.0)
-    ms(R("BIG", 0, 32), 512.0)
-    ms(R("C4K", 0, 16), 4096.0)
-    ms(R("ON", 0, 128), 1.0)
+        ms(R("KW%d" % h, 0, 8), 0.0)
+    ms(M("ON"), 1.0)
+    ms(M("N16"), -16.0)
+    ms(M("C3"), 3.0)
+    ms(M("C512"), 512.0)
+    ms(M("O16"), 0.25)
     cp(PF, PI)
-    ts(R("PQ", 0, 1), PI, 4, None, A.logical_shift_right)
-    ts(R("PR_", 0, 1), PI, 15, None, A.bitwise_and)
-    cp(PG, R("PQ", 0, 1))
-    ts(T15, R("PQ", 0, 1), 16, 15, A.mult, A.add)
-    cp(KC_, R("PR_", 0, 1))
-    ts(L16, R("PR_", 0, 1), 16, None, A.mult)
-    ts(R("CG", 0, 144), R("CI", 0, 144), 4, None, A.logical_shift_right)
+    ts(PGI, PI, 4, None, A.logical_shift_right)
+    ts(PKI, PI, 15, None, A.bitwise_and)
+    ts(P8I, PI, 3, None, A.logical_shift_right)
+    cp(PG, PGI)
+    cp(KP, PKI)
+    cp(P8, P8I)
+    ts(T15, PGI, 16, 15, A.mult, A.add)
+    ts(L16, PKI, 16, None, A.mult)
+    ts(KO, PKI, 16384, -15 * 16384, A.mult, A.add)
+    ts(CB, PKI, 0.5, 50.5, A.mult, A.add)
+    ts(R("EQ", 0, 16), R("CI", 0, 16), KP, None, A.is_equal)
+    ts(R("X", DEAD, DEAD + 16), R("EQ", 0, 16), R("EQ", 0, 1), 255, A.mult, A.mult)
+    ts(R("CG", 0, 144), C144, 4, None, A.logical_shift_right)
+    ts(M("KI"), C128, 15, None, A.bitwise_and)
     ts(R("SGT", 0, 128, 1, 8), R("CG", 0, 128, 1, 8), R("KF", 0, 1, 1, 8), None, A.is_equal)
-    ts(R("IDB", 0, 128), C128, PF, None, A.is_equal)
-    ts(R("NIB", 0, 128), C128, PF, -1, A.is_equal, A.mult)
-    ts(R("IDF", 0, 128), C128, PF, None, A.is_equal)
-    ts(R("BO", 0, 128), R("CG", 0, 128), PG, None, A.is_equal)
-    ts(R("ZO", 0, 144), R("CI", 0, 144), T15, None, A.is_equal)
-    ts(R("ZN", 0, 144), R("CI", 0, 144), T15, -4096, A.is_equal, A.mult)
-    ts(R("SF", 0, 8), R("CI", 0, 8), 16, PF, A.mult, A.is_equal)
-    ts(R("CS", 0, 16), R("CI", 0, 16), 7, None, A.bitwise_and)
-    ts(R("SGF", 0, 16), R("CS", 0, 16), PG, None, A.is_equal)
+    ts(M("IDF"), C128, PF, None, A.is_equal)
+    ts(M("IDB"), C128, PF, None, A.is_equal)
+    ts(M("BO"), R("CG", 0, 128), PG, None, A.is_equal)
+    ts(R("ZO", 0, 144), C144, T15, None, A.is_equal)
     ts(R("SGB", 0, 8), R("CI", 0, 8), PG, None, A.is_equal)
-    ts(R("KI", 0, 128), C128, 15, None, A.bitwise_and)
-    ts(R("RS", 0, 128), R("KI", 0, 128), 0, None, A.is_gt)
-    ts(R("BS", 0, 16), R("CI", 0, 16), 256, L16, A.mult, A.add)
-    cp(R("THB", 0, 1, 1, 8), R("TH", 0, 1, 1, 8))
+    ts(R("SD", 0, 8), R("SGB", 0, 8), -1, None, A.mult)
+    ts(R("SD", 8, 16), R("SGB", 0, 8), -1, None, A.mult)
+    ts(R("SD", 16, 24), R("SGB", 0, 8), R("EQ", 0, 1), None, A.mult)
+    ts(R("SD", 24, 32), R("SGB", 0, 8), 2, None, A.mult)
+    K7 = R("HI0", 0, 128)
+    ts(K7, C128, 7, None, A.bitwise_and)
+    cp(R("KF", 17, 18, 1, 8), R("TH", 0, 1, 1, 8))
     cp(R("WNB", 0, 256, 1, 8), R("WN", 0, 256, 1, 8))
     cp(WC, R("WT", 0, 1))
-    ts(R("ZW", 0, 144), R("CI", 0, 144), T15, WC, A.is_equal, A.mult)
-    mm(R("pb3", 0, 1), R("SGT", 0, 128, 1, 8), R("THB", 0, 1, 1, 8))
-    ts(TB, R("pb3", 0, 1), 0.5, None, A.add)
+    ts(R("THM", 0, 120, 1, 8), R("HI0", 0, 120, 1, 8), R("KF", 0, 1, 1, 8), R("KF", 17, 18, 1, 8), A.is_equal, A.mult)
+    ts(R("THM", 120, 128, 1, 8), R("HI0", 120, 128, 1, 8), R("KF", 0, 1, 1, 8), -100, A.is_equal, A.mult)
+    ts(R("PI", 4, 5), PI, 7, None, A.bitwise_and)
+    cp(P7, R("PI", 4, 5))
+    ts(M("SAME"), R("CG", 0, 128), P7, None, A.is_equal)
+    ts(R("EQ", 16, 24), R("CI", 0, 8), P8, None, A.is_equal)
+    for j in range(8):
+        ts(R("BK", 128 * j, 128 * j + 128), M("SAME"), R("EQ", 16 + j, 17 + j), None, A.mult)
+    ts(M("I17"), M("IDB"), -131072, None, A.mult)
+    ts(M("I50"), M("IDB"), 50, None, A.mult)
+    ts(R("T2", 0, 128), M("KI"), 0, 0.25, A.is_gt, A.mult)
+    ts(M("PAT"), R("T2", 0, 128), -62 / 128, None, A.add)
+    ts(R("HI0", 128, 256), R("CG", 0, 128), 16, 8, A.mult, A.add)
+    tt(M("CD"), K7, R("HI0", 128, 256), A.add)
+    ts(M("DUP"), M("CD"), PF, None, A.is_equal)
+    ts(R("HI0", 256, 384), K7, 8, None, A.add)
+    ts(Q1, PI, 64, None, A.is_lt)
+    for e in (0, 1):
+        same, x = R("HB0", 128 * e, 128 * e + 128), "EO"[e]
+        qp, qm = R("KF", 24 + 2 * e, 25 + 2 * e), R("KF", 25 + 2 * e, 26 + 2 * e)
+        ts(qp, P8I, 8 * e, None, A.add)
+        ts(qm, P8I, 8 * e - 1, None, A.add)
+        ts(same, M("SAME"), 1 if e else Q1, None, A.mult)
+        ts(M("NBO" + x), same, -0.5, None, A.mult)
+        ts(R("HB1", 0, 128), M("KI"), qp, None, A.is_equal)
+        tt(M("SH" + x), R("HB1", 0, 128), same, A.mult)
+        ts(M("SH32" + x), M("SH" + x), 32, None, A.mult)
+        for n, kk in (("TRI", M("KI")), ("TRD", R("HI0", 256, 384))):
+            ts(R("HB1", 128, 256), kk, qm, -0.5, A.is_ge, A.mult)
+            ts(R("HB1", 256, 384), kk, qm, -50, A.is_equal, A.mult)
+            tt(R("HB1", 384, 512), R("HB1", 128, 256), R("HB1", 256, 384), A.add)
+            tt(M(n + x), R("HB1", 384, 512), same, A.mult)
+    ts(CBD, R("PI", 4, 5), 0.5, 54.5, A.mult, A.add)
+    ts(Q2, CBD, -108.5, None, A.add)
+    ts(R("PI", 5, 6), P8I, 1, None, A.bitwise_and)
+    for j in range(4):
+        ts(OVC[j], R("PI", 5, 6), 4, 159 + j, A.mult, A.add)
+    ts(R("SG32", 0, 8), R("SGB", 0, 8), 32, None, A.mult)
+    ts(R("WG", 0, 8), R("SGB", 0, 8), WC, 2.0 ** -12, A.mult, A.mult)
+    ts(M("WX"), M("BO"), WC, 2.0 ** -12, A.mult, A.mult)
+    ts(R("ZW", 0, 144), R("ZO", 0, 144), WC, None, A.mult)
+    ts(R("ZK", 0, 144), R("ZO", 0, 144), KP, None, A.mult)
+    ts(R("ZN", 0, 144), R("ZO", 0, 144), -JUNK, None, A.mult)
+    ts(R("CS", 0, 16), R("CI", 0, 16), 7, None, A.bitwise_and)
+    ts(R("SGF", 0, 16), R("CS", 0, 16), PG, None, A.is_equal)
+    ts(R("CS", 0, 32), R("CI", 0, 32), 15, None, A.bitwise_and)
+    ts(R("SGD", 0, 32), R("CS", 0, 32), P8, None, A.is_equal)
+    ts(R("BS", 0, 16), R("CI", 0, 16), 256, L16, A.mult, A.add)
+    KOFF = R("pb3", 0, 128)
+    ts(KOFF, M("KI"), -16384, 15 * 16384, A.mult, A.add)
 
     def H(kind, h, s, c0=0, c1=128, step=1):
         return R("%s%d" % (kind, h), 128 * s + c0, 128 * s + c1, step)
@@ -251,9 +324,9 @@ def build(g, T, topo, core):
 
     def hi(h, s, *a):
         return H("HI", h, s, *a)
-    NL_, LV, EN, CU, CC, S1, G2, CD, CL, EL, E9, T1, OV, GL, UK = range(15)
-    NM, SNM, AA, PP, KC, FN = range(6)
-    JI, NMI, AG, AG2, P1, P1M, UI, U, Y, HH, Q2, Q3 = range(12)
+    KN, GG, CL, S9, OV, RU, RQ, LV = range(8)
+    NM, KC, YY, RY, AG, PW, PL, FN = range(8)
+    JI, NMI, A1, A2, B1, B2 = range(6)
 
     def pA(h, r):
         return R("pb%d" % (4 + 2 * h), 128 * r, 128 * r + 128)
@@ -262,207 +335,199 @@ def build(g, T, topo, core):
         return R("pb%d" % (5 + 2 * h), 128 * r, 128 * r + 128)
     rank = T.rank_of(core)
     sends = [0]
+    lane = [0]
 
     def addr(d):
-        dst = T.cores[(rank + d) % 4]
+        dst = T.cores[(rank + d) % len(T.cores)]
         rid, pid, _s = topo.addr(dst)
         return dst, rid, pid
 
+    def bits(engines):
+        return sum(1 << e for e in engines)
+
     def start_words(h):
-        w = R("WL", 128 * h, 128 * h + 128)
-        cp(R("OF%d" % h, 0, 128), w)
-        cp(R("WLF", 128 * h, 128 * h + 128), w)
-        mm(pA(h, 0), R("WLF", 128 * h, 128 * h + 128), R("IDF", 0, 128))
-        act(hf(h, NM), pA(h, 0), F.Copy)
-        mm(pB(h, 0), R("WNB", 128 * h, 128 * h + 128, 1, 8), R("SGT", 0, 128, 1, 8))
-        tt(pA(h, 1), pB(h, 0), R("KI", 0, 128), A.is_gt)
-        ts(hb(h, NL_), pA(h, 1), -1, 1, A.mult, A.add)
+        mm(pA(h, 0), R("SGT", 0, 128, 1, 8), R("WNB", 128 * h, 128 * h + 128, 1, 8))
+        ts(pA(h, 1), pA(h, 0), KP, 8192, A.is_le, A.mult)
+        tt(hf(h, FN), pA(h, 1), R("WL", 128 * h, 128 * h + 128), A.add)
+        ts(R("OF%d" % h, 0, 128), hf(h, FN), DEAD, None, A.min)
+        mm(pB(h, 0), hf(h, FN), M("IDF"))
+        act(hf(h, AG), pB(h, 0), F.Copy)
+        tt(hf(h, NM), KOFF, hf(h, AG), A.add)
 
     def join(h, own, ov, waits, after):
         tt(hi(h, JI, 0, 64), own, ov, A.add, waits=waits, after=after)
-        ts(hi(h, NMI, 0, 128, 2), hi(h, JI, 0, 64), 12, 4095, A.logical_shift_right, A.bitwise_and)
-        ts(hi(h, NMI, 1, 128, 2), hi(h, JI, 0, 64), 4095, None, A.bitwise_and)
-        cp(hf(h, NM), hi(h, NMI))
-        ts(hb(h, NL_, 0, 128, 2), hi(h, JI, 0, 64), 0, None, A.is_lt)
-        ts(hb(h, NL_, 1, 128, 2), hi(h, JI, 0, 64), 0, None, A.is_lt)
-        act(pA(h, 1), hb(h, NL_), F.Copy, 1.0, -1.0)
+        ts(hi(h, NMI, 0, 128, 2), hi(h, JI, 0, 64), 12, 8191, A.logical_shift_right, A.bitwise_and)
+        ts(hi(h, NMI, 1, 128, 2), hi(h, JI, 0, 64), (1 << 24) + 4095, None, A.bitwise_and)
 
     def offsets(h):
-        mm(pB(h, 0), hf(h, NM), R("IDF", 0, 128))
-        cp(R("OF%d" % h, 0, 128), pB(h, 0))
+        tt(hf(h, NM), KOFF, hi(h, NMI), A.add)
+        mm(pB(h, 0), hf(h, NM), M("IDF"))
+        ts(R("OF%d" % h, 0, 128), pB(h, 0), KO, DEAD, A.add, A.min)
 
     def mask(h, s):
         return R("M0", 128 * h, 128 * h + 128) if s == 0 else R("MO%d" % h, 128 * s, 128 * s + 128)
+    XW = R("X", 0, DEAD + 16)
+
+    def marks(n, h):
+        return [(M(n + "EO"[e])[:4] + (72,), R("K2%d" % h, e, 256, 2, 72)) for e in (0, 1)]
 
     def front(t, h):
         stage[0] = ("front", t, h)
-        v, ad, mk = "V%d" % h, "AD%d" % h, "MK%d" % h
+        v, mn, mk = "V%d" % h, "MN%d" % h, "MK%d" % h
         for c in range(4):
-            o, i = R(v, 16 + 512 * c, 528 + 512 * c), (R("X", 0, 4096), R("OF%d" % h, 32 * c, 32 * c + 32))
-            if c in PLAN["gv"][h]:
-                cp(o, i)
+            o, i = R(v, 16 + 512 * c, 528 + 512 * c), (XW, R("OF%d" % h, 32 * c, 32 * c + 32))
+            if PLAN["gv"][h][c] == "V":
+                ts(o, i, 16, None, A.add)
             else:
-                act(o, i, F.Copy)
+                act(o, i, F.Copy, 16.0)
+            scan(R(mn, 512 * c, 512 * c + 512), R(v, 15 + 512 * c, 527 + 512 * c), o, A.max, A.min)
+        bank, kw, k2 = "pb%d" % (4 + 2 * h), "KW%d" % h, "K2%d" % h
+        msum(pA(h, 2), [(R("CM", M("ON")[1], M("ON")[2], 1, 8), R("THM", 0, 128, 1, 8))]
+             + [(R(bank, 256 + 8 * max(k - 1, 0), 264 + 8 * k), R(v, 16 + k, 2064, 16), R("SD", 0, 8) if k == 0 else R("SD", 8, 24) if k == 15 else R("SD", 0, 16)) for k in range(16)]
+             + [(R(bank, 248 + 8 * k, 256 + 8 * k), R(mn, k, 2048, 16), R("SD", 24, 32)) for k in range(1, 16)])
+        act(R(kw, 8, 136), pA(h, 2), F.Sign, 0.5)
+        for e in (0, 1):
+            mm(R(bank, e, 256, 2, 72), R(kw, 64 * e, 64 * e + 72), M("IDB"))
+        act(R(k2, 0, 256, 1, 72), R(bank, 0, 256, 1, 72), F.Copy)
         for c in range(4):
-            b = R("pb%d" % c, 0, 512)
-            gr = ("df", t, h, c)
-            mm(b, R("IDB", 0, 128), R(v, 16 + 512 * c, 528 + 512 * c), True, False, gr)
-            mm(b, R("NIB", 0, 128), R(v, 15 + 512 * c, 527 + 512 * c), False, False, gr)
-            mm(R("pb%d" % c, 0, 512, 16), R("IDB", 0, 128), R("BIG", 0, 32), False, True, gr)
-            act(R(ad, 512 * c, 512 * c + 512), b, F.Abs)
-            mm(b, R("BO", 0, 128), R(ad, 512 * c, 512 * c + 512))
-            act(R(mk, 512 * c, 512 * c + 512), b, F.Sign, TB, -1.0)
-            scan(R("ZZ", 2048 * h + 512 * c, 2048 * h + 512 * c + 512), R(mk, 512 * c, 512 * c + 512), R(v, 16 + 512 * c, 528 + 512 * c), A.mult, A.max)
-        for k in range(16):
-            mm(R("pb%d" % (4 + 2 * h), k, 128, 16), R(mk, k, 2048, 16), R("SF", 0, 8))
-        ct = R("CT%d" % h, 0, 128)
-        tt(ct, pA(h, 0), hb(h, NL_), A.is_gt)
-        tt(hb(h, EN), pA(h, 1), R("CT%d" % h, 1, 129), A.subtract)
-        scan(pA(h, 0), R("RS", 0, 128), hb(h, EN), A.mult, A.add)
-        scan(hb(h, CC), ct, R("ON", 0, 128), A.mult, A.add)
-        tt(hb(h, CD), pA(h, 0), hb(h, EN), A.mult)
-        mm(pA(h, 1), hb(h, CC), R("IDB", 0, 128))
-        mm(pA(h, 2), hb(h, CD), R("IDB", 0, 128))
-        act(hf(h, KC), pA(h, 1), F.Copy, 0.0, 19552.0)
-        act(hb(h, GL), pA(h, 1), F.Copy, 1.0, 2.0)
-        act(hb(h, CL), pA(h, 2), F.Copy)
-        act(hb(h, EL), hb(h, CL), F.Sign)
-        mm(pA(h, 0), R("BO", 0, 128), hb(h, EL))
+            b = "pb%d" % (lane[0] % 2)
+            lane[0] += 1
+            for j in range(8):
+                mm(R(b, j, 512, 8), R("BK", 128 * j, 128 * j + 128, 1, 72), R(k2, 64 * c, 64 * c + 64, 1, 72))
+            d0 = R(b, 0, 512)
+            if PLAN["mk"][h][c] == "S":
+                act(R(mk, 512 * c, 512 * c + 512), d0, F.Copy)
+                d0 = R(mk, 512 * c, 512 * c + 512)
+            scan(R("ZZ", 2048 * h + 512 * c, 2048 * h + 512 * c + 512), d0, R(v, 16 + 512 * c, 528 + 512 * c), A.mult, A.max)
+        stage[0] = ("count", t, h)
+        msum(pA(h, 2), marks("NBO", h))
+        msum(pA(h, 1), marks("TRI", h))
+        msum(pA(h, 3), marks("TRD", h))
         sm = R("SM%d%d" % (t, h), 0, 128)
-        act(sm, pA(h, 0), F.Copy)
+        act(sm, pA(h, 2), F.Copy, 8.0, acc=R("AC", h, h + 1) if t < VISITS - 1 else None)
+        act(hb(h, CL), pA(h, 1), F.Copy, CB)
+        act(hb(h, S9), pA(h, 3), F.Sign, Q2)
         dst, rid, pid = addr(-1)
-        es = topo.engines(core, dst)
-        m = 0
-        for e in es[:8]:
-            m |= 1 << e
+        m = bits(topo.engines(core, dst)[:8])
         rm = "RM%d%d" % (t, h)
         snd = add("G", lambda: g.remote_dma(out_ap=T[rm][:], in_ap=ap(sm), remote_sem=T.sem["rm%d%d" % (t, h)], local_sem=T.sem["sent"], pid=pid, routing_id=rid, dma_engine_mask=m),
                   [sm], [], 1000.0, dma="sent", lat=NET)
         sends[0] += 8
         for s in range(8):
-            ts(mask(h, s), hb(h, CL), s + 1, None, A.is_equal)
-        ts(hb(h, E9), hb(h, CL), 9, 100, A.is_lt, A.mult)
-        gr = ("ov", t, h)
-        mm(pA(h, 1), R("IDB", 0, 128), hb(h, CL), True, False, gr)
-        mm(pA(h, 1), R("NIB", 0, 128), hb(h, E9), False, False, gr)
-        mm(pA(h, 1), R("IDB", 0, 128), R(rm, 0, 128), False, True, gr, waits=[("rm%d%d" % (t, h), 8)], after=[snd])
-        act(hb(h, OV), pA(h, 1), F.Copy)
-        for s in range(8):
-            ts(R("MO%d" % h, 1024 + 128 * s, 1152 + 128 * s), hb(h, OV), s + 9, None, A.is_equal)
+            ts(mask(h, s), hb(h, CL), 101 + s, None, A.is_equal)
+        stage[0] = ("names", t, h)
+        msum(pB(h, 1), [x[::-1] for x in marks("SH32", h)] + [(M("ON"), M("PAT"))])
+        msum(pB(h, 2), [x[::-1] for x in marks("SH", h)])
+        scan(hb(h, GG), pB(h, 1), M("C3"), A.add, A.max)
+        hold = R("pb3", 128 + 128 * h, 256 + 128 * h)
+        scan(hold, pB(h, 2), hf(h, NM), A.mult, A.max)
+        act(hf(h, KC), hb(h, GG), F.Copy, -360240.0 - 65534.0, 9776.0)
+        if t == 0:
+            tt(hi(h, A1), hold, hb(h, GG), A.mult)
+        else:
+            tt(hf(h, AG), hold, hb(h, GG), A.mult)
+            ts(hi(h, A1), hf(h, AG), R("AF", t, t + 1), None, A.add)
+        ts(hi(h, A2), hi(h, A1), 0x3FFC, None, A.bitwise_and)
+        ts(hold, hi(h, A2), 1024, 1, A.mult, A.add)
+        return snd
+
+    def places(t, h, snd):
+        stage[0] = ("places", t, h)
+        rm = "RM%d%d" % (t, h)
+        msum(pA(h, 0), marks("TRD", h) + [(M("I50"), hb(h, S9)), (M("IDB"), R(rm, 0, 128))], waits=[("rm%d%d" % (t, h), 8)], after=[snd])
+        act(hb(h, OV), pA(h, 0), F.Copy, CBD)
+        for j in range(4):
+            ts(mask(h, 8 + j), hb(h, OV), OVC[j], None, A.is_equal)
 
     def middle(t, h):
         stage[0] = ("middle", t, h)
-        gr = ("u", t, h)
-        for k in range(16):
-            mm(pB(h, 0), R("ZW", 15 - k, 143 - k), R("ZZ", 2048 * h + k, 2048 * h + 2048, 16), k == 0, k == 15, gr)
-        cp(hi(h, UI), pB(h, 0))
-        ts(hi(h, U), hi(h, UI), 4095, None, A.bitwise_and)
-        ts(pB(h, 1), hi(h, U), 1184, None, A.add)
-        tt(pB(h, 2), pB(h, 1), hi(h, U), A.mult)
-        tt(hi(h, Y), pB(h, 2), hf(h, KC), A.add)
-        ts(hi(h, HH), hi(h, Y), 5, 4095, A.logical_shift_right, A.bitwise_and)
-        cp(R("HU%d" % h, 0, 128), hi(h, HH))
+        u = pA(h, 1)
+        msum(u, [(M("N16"), M("WX"))] + [(R(u[0], u[1] + k, u[2], 16), R("ZZ", 2048 * h + k, 2048 * h + 2048, 16), R("WG", 0, 8)) for k in range(16)])
+        if PLAN["um"][h] == "S":
+            act(hb(h, RU), u, F.Copy, 191.5 + 2.0 ** -13)
+        else:
+            ts(hb(h, RU), u, 191.5 + 2.0 ** -13, None, A.add)
+        tt(hf(h, RY), u, hb(h, RU), A.subtract)
+        act(pA(h, 3), hf(h, RY), F.Square, 192.0 * 4096 + 592, 4096.0)
+        tt(hf(h, YY), pA(h, 3), hf(h, KC), A.add)
+        if PLAN["hm"][h] == "S":
+            act(hf(h, RY), hf(h, YY), F.Copy, 12582912.0, 2.0 ** -17)
+            act(hb(h, RQ), hf(h, RY), F.Copy, -12582912.0)
+        else:
+            ts(hf(h, RY), hf(h, YY), 2.0 ** -17, 12582912.0, A.mult, A.add)
+            ts(hb(h, RQ), hf(h, RY), -12582912.0, None, A.add)
+        msum(pB(h, 0), [(hf(h, YY), M("IDF")), (hb(h, RQ), M("I17"))])
+        ts(R("HU%d" % h, 0, 128), pB(h, 0), 2.0 ** -5, (65534 - 15.5) / 32, A.mult, A.add)
         for c in range(4):
             a, b = 2048 * h + 512 * c, 2048 * h + 512 * c + 512
-            x = (R("X", 0, 4096), R("HU%d" % h, 32 * c, 32 * c + 32))
-            ae = R("AE%d" % h, 512 * c, 512 * c + 512)
-            if c in PLAN["xs"][h]:
-                act(R("XD", a, b), x, F.Copy)
-                pb, gr = R("pb%d" % c, 0, 512), ("xd", t, h, c)
-                mm(pb, R("IDB", 0, 128), R("XD", a, b), True, False, gr)
-                mm(pb, R("NIB", 0, 128), R("ZZ", a, b), False, True, gr)
-                act(ae, pb, F.Abs)
+            x = (XW, R("HU%d" % h, 32 * c, 32 * c + 32))
+            if PLAN["gh"][h][c] == "S":
+                xh = R("XH%d" % h, 512 * c, 512 * c + 512)
+                act(xh, x, F.Copy)
+                scan(R("XD", a, b), xh, R("ZZ", a, b), A.max, A.subtract)
             else:
                 tt(R("XD", a, b), x, R("ZZ", a, b), A.subtract)
-                act(ae, R("XD", a, b), F.Abs)
-        stage[0] = ("first", t, h)
-        ts(hi(h, UI), hi(h, U), 15, None, A.bitwise_and)
-        tt(R("QU", 128 * h, 128 * h + 128), hi(h, UI), mask(h, 0), A.mult)
-        ts(R("QE", 128 * h, 128 * h + 128), mask(h, 0), KC_, None, A.mult)
-        stage[0] = ("names", t, h)
-        ct = R("CT%d" % h, 0, 128)
-        act(pB(h, 2), ct, F.Copy, 1.0, -1.0)
-        tt(hf(h, SNM), pB(h, 2), hf(h, NM), A.mult)
-        scan(pB(h, 3), ct, hf(h, SNM), A.mult, A.add)
-        act(hb(h, G2), hb(h, CC), F.Copy, 1.0, 2.0)
-        tt(hi(h, AG), pB(h, 3), hb(h, G2), A.mult)
-        if t == 0:
-            ts(hi(h, P1M), hi(h, AG), 2, 4095, A.logical_shift_right, A.bitwise_and)
-        else:
-            ts(hi(h, AG2), hi(h, AG), 2, None, A.logical_shift_right)
-            ts(hi(h, P1), hi(h, AG2), R("AF", t, t + 1), None, A.add)
-            ts(hi(h, P1M), hi(h, P1), 4095, None, A.bitwise_and)
-        ts(hf(h, PP), hi(h, P1M), 4096, 1, A.mult, A.add)
-        mm(pA(h, 3), hf(h, PP), R("IDF", 0, 128))
+            act(R("AE%d" % h, 512 * c, 512 * c + 512), R("XD", a, b), F.Abs, 16.0)
+
+    def first(t):
+        stage[0] = ("first", t, 0)
+        fe, tg, uf, ac = [R("pb%d" % (j // 2), 16 * j, 16 + 16 * j) for j in range(4)]
+        msum(fe, [(win("ZK", k), R("M0", k, 256, 16)) for k in range(16)] + [(M("IDB"), R("BS", 0, 16))])
+        msum(tg, [(win("ZN", k), R("M0", k, 256, 16)) for k in range(16)] + [(M("IDB"), R("BS", 0, 16))])
+        cp(R("FE", 0, 16), fe)
+        act(R("ZF", 0, 256), (R("ZZ", 0, 4096), R("FE", 0, 16)), F.Copy, -32.0, 2.0)
+        msum(uf, [(win("ZW", k), R("ZF", k, 256, 16)) for k in range(16)])
+        cp(R("UA", 0, 16), uf)
+        ts(R("UA", 16, 32), R("UA", 0, 16), 1, 15, A.logical_shift_right, A.bitwise_and)
+        tt(R("UA", 32, 48), tg, R("UA", 16, 32), A.add)
+        ts(R("TG", 0, 16), R("UA", 32, 48), JUNK, None, A.add)
+        if t < VISITS - 1:
+            a1 = R(ac[0], ac[1], ac[1] + 1)
+            msum(a1, [(M("O16"), R("AC", h, h + 1)) for h in (0, 1)])
+            cp(R("AI", 0, 1), a1)
+            ts(R("AI", 1, 2), R("AI", 0, 1), 1020, None, A.bitwise_and)
+            cp(R("AF", t + 1, t + 2), R("AI", 1, 2))
 
     def write(t):
         stage[0] = ("write", t, 0)
-        fe, tg = R("pb3", 0, 16), R("pb2", 0, 16)
-        g1, g2 = ("fe", t), ("tg", t)
-        for k in range(16):
-            mm(fe, R("ZO", 15 - k, 143 - k), R("QE", k, 256, 16), k == 0, False, g1)
-        mm(fe, R("IDB", 0, 128), R("BS", 0, 16), False, True, g1)
-        for k in range(16):
-            mm(tg, R("ZO", 15 - k, 143 - k), R("QU", k, 256, 16), k == 0, False, g2)
-            mm(tg, R("ZN", 15 - k, 143 - k), R("M0", k, 256, 16), False, False, g2)
-        mm(tg, R("IDB", 0, 128), R("BS", 0, 16), False, False, g2)
-        mm(tg, R("IDB", 0, 128), R("C4K", 0, 16), False, True, g2)
-        cp(R("FE", 0, 16), fe)
-        cp(R("TG", 0, 16), tg)
-        seg = [1.0 if c % 4 in PLAN["xs"][c // 4] else 2.0 for c in range(8)]
-        c0 = 0
-        for c in range(1, 9):
-            if c == 8 or seg[c] != seg[c0]:
-                act(R("ZF", 32 * c0, 32 * c), (R("ZZ", 0, 4096), R("FE", 2 * c0, 2 * c)), F.Copy, 0.0, seg[c0])
-                c0 = c
         tt(R("SU", 0, 256), (R("XD", 0, 4096), R("FE", 0, 16)), R("ZF", 0, 256), A.add)
-        ts(R("SV", 0, 256), R("SU", 0, 256), 1, None, A.arith_shift_right)
-        cp((R("X", 0, 8192), R("TG", 0, 16)), R("SV", 0, 256))
-        if t < VISITS - 1:
-            for h in (0, 1):
-                mm(R("pb1", 0, 128), R("ON", 0, 128), hb(h, EN), h == 0, h == 1, ("a", t))
-            add("V", lambda: g.vector.tensor_reduce(ap(R("AF", 4 + t, 5 + t)), ap(R("pb1", 0, 128)), axis=AxisListType.X, op=A.add), [R("pb1", 0, 128)], [R("AF", 4 + t, 5 + t)], FIX + 128)
-            cp(R("AI", 0, 1), R("AF", 4 + t, 5 + t))
-            ts(R("AI", 1, 2), R("AI", 0, 1), 255, None, A.bitwise_and)
-            cp(R("AF", t + 1, t + 2), R("AI", 1, 2))
+        ts(R("SV", 0, 256), R("SU", 0, 256), 0.5, 7.75, A.mult, A.add)
+        cp((R("X", 0, JUNK + 4096), R("TG", 0, 16)), R("SV", 0, 256))
 
     def back(t, h):
         stage[0] = ("back", t, h)
-        gr = ("d", t, h)
-        for k in range(16):
-            mm(pB(h, 3), R("ZO", 15 - k, 143 - k), R("AE%d" % h, k, 2048, 16), k == 0, k == 15, gr)
-        tt(pB(h, 1), pB(h, 3), hb(h, GL), A.mult)
-        tt(hi(h, Q2), pB(h, 1), hi(h, HH), A.add)
-        ts(hi(h, Q3), hi(h, Q2), 4095, None, A.bitwise_and)
-        tt(pB(h, 2), pA(h, 3), hi(h, Q3), A.add)
+        d = pB(h, 1)
+        msum(d, [(M("ON"), M("C512"))] + [(R(d[0], d[1] + k, d[2], 16), R("AE%d" % h, k, 2048, 16), R("SG32", 0, 8)) for k in range(16)])
+        tt(d, d, hb(h, GG), A.mult)
+        tt(hi(h, B1), d, hf(h, YY), A.add)
+        ts(hi(h, B2), hi(h, B1), 5, 4095, A.arith_shift_right, A.bitwise_and)
+        tt(hf(h, PW), R("pb3", 128 + 128 * h, 256 + 128 * h), hi(h, B2), A.add)
+        mm(pB(h, 2), hf(h, PW), M("IDF"))
+        act(hf(h, PL), pB(h, 2), F.Copy)
+        dup = R("pb2", 128 * h, 128 * h + 128)
+        mm(dup, M("DUP"), hf(h, PL))
         last = t == VISITS - 1
-        sg = R("SGF", 0, 8) if last else R("SGF", 7, 15)
-        bank = "pb%d" % (4 + 2 * h)
-        for s in (list(range(8, 16)) + list(range(8)) if last else range(16)):
+        o = pA(h, 2)
+        for s in (list(range(8, 12)) + list(range(8)) if last else range(12)):
             pr = R("PD%d" % h, 128 * s, 128 * s + 128)
-            tt(pr, pB(h, 2), mask(h, s), A.mult)
-            o = 64 * (s // 8)
-            mm(R(bank, o + s % 8, o + 64, 8), pr, sg)
+            tt(pr, pB(h, 2) if s < 8 else dup, mask(h, s), A.mult)
+            if s < 8:
+                mm(R(o[0], o[1] + s, o[1] + 64, 8), pr, R("SGF", 0, 8) if last else R("SGF", 7, 15))
+            else:
+                mm(R(o[0], o[1] + 56 + s, o[1] + 128, 4), pr, R("SGD", 0, 16) if last else R("SGD", 14, 30))
         sn = "SN%d%d" % (t, h)
-        act(R(sn, 0, 64), R(bank, 0, 64), F.Copy, -1.0)
-        act(R(sn, 64, 128), R(bank, 64, 128), F.Copy)
+        act(R(sn, 0, 64), R(o[0], o[1], o[1] + 64), F.Copy, -1.0)
+        act(R(sn, 64, 128), R(o[0], o[1] + 64, o[1] + 128), F.Copy)
         ro, rv, rx = "RO%d%d" % (t, h), "RV%d%d" % (t, h), "rx%d%d" % (t, h)
         d1, r1, p1 = addr(1)
         d2, r2, p2 = addr(2)
         e1, e2 = topo.engines(core, d1), topo.engines(core, d2)
+        sends[0] += 8
         if last:
-            m = 0
-            for e in e1[:8]:
-                m |= 1 << e
-            sends[0] += 8
+            m = bits(e1[:8])
             return add("G", lambda: g.remote_dma(out_ap=T[rv][:], in_ap=ap(R(sn, 64, 128)), remote_sem=T.sem[rx], local_sem=T.sem["sent"], pid=p1, routing_id=r1, dma_engine_mask=m),
                        [R(sn, 64, 128)], [], 1000.0, dma="sent", lat=NET)
-        m1 = m2 = 0
-        for e in e1[:4]:
-            m1 |= 1 << e
-        for e in [e for e in e2 if e not in e1[:4]][:4]:
-            m2 |= 1 << e
-        sends[0] += 8
+        m1, m2 = bits(e1[:4]), bits([e for e in e2 if e not in e1[:4]][:4])
 
         def fused():
             return g.remote_dma_fused([
@@ -472,65 +537,51 @@ def build(g, T, topo, core):
         return add("G", fused, [R(sn, 0, 128)], [], 1200.0, dma="sent", lat=NET)
 
     arr = {}
+
+    def arrive(t, h):
+        if t == 0:
+            start_words(h)
+        else:
+            stage[0] = ("join", t, h)
+            q = "%d%d" % (t - 1, h)
+            join(h, R("RO" + q, 0, 64), R("RV" + q, 0, 64), [("rx" + q, 8)], [arr[h]])
+            offsets(h)
     for t in range(VISITS):
-        for h in (0, 1):
-            if t == 0:
-                start_words(h)
-            else:
-                stage[0] = ("join", t, h)
-                q = "%d%d" % (t - 1, h)
-                join(h, R("RO" + q, 0, 64), R("RV" + q, 0, 64), [("rx" + q, 8)], [arr[h]])
-                offsets(h)
-        for h in (0, 1):
-            front(t, h)
-            middle(t, h)
+        arrive(t, 0)
+        s0 = front(t, 0)
+        middle(t, 0)
+        places(t, 0, s0)
+        arrive(t, 1)
+        s1 = front(t, 1)
+        arr[0] = back(t, 0)
+        first(t)
+        middle(t, 1)
         write(t)
-        for h in (0, 1):
-            arr[h] = back(t, h)
-    dma("Q", ("yx", None), R("X", 0, 4096), 6000.0)
+        places(t, 1, s1)
+        arr[1] = back(t, 1)
+    add("Q", lambda: g.sync.dma_start(T.yx[:], ap(R("X", 0, 4096))), [R("X", 0, 4096)], [], 100.0, dma="dm10", lat=6000.0)
     for h in (0, 1):
         stage[0] = ("join", VISITS, h)
         q = "%d%d" % (VISITS - 1, h)
         join(h, R("SN" + q, 0, 64), R("RV" + q, 0, 64), [("rx" + q, 8)], [arr[h]])
-        ts(hf(h, SNM), hi(h, NMI), 1, None, A.add)
-        tt(hf(h, FN), pA(h, 1), hf(h, SNM), A.mult)
-        mm(pB(h, 0), hf(h, FN), R("IDF", 0, 128))
-        ts(R("YL", 128 * h, 128 * h + 128), pB(h, 0), -1, 0, A.add, A.max)
-        ts(hb(h, EL), pB(h, 0), 0.5, None, A.is_gt)
-        mm(R("pb%d" % (4 + 2 * h), 0, 128, 1, 8), R("SGB", 0, 8), hb(h, EL))
+        cp(hf(h, NM), hi(h, NMI))
+        mm(pB(h, 0), hf(h, NM), M("IDF"))
+        ts(hb(h, LV), pB(h, 0), DEAD, None, A.is_lt)
+        tt(R("YL", 128 * h, 128 * h + 128), pB(h, 0), hb(h, LV), A.mult)
+        mm(R("pb%d" % (4 + 2 * h), 0, 128, 1, 8), R("SGB", 0, 8), hb(h, LV))
         act(R("YN", 128 * h, 128 * h + 128, 1, 8), R("pb%d" % (4 + 2 * h), 0, 128, 1, 8), F.Copy)
     dma("Q", ("yl", None), R("YL", 0, 256))
-    dma("Q", ("yn", None), R("YN", 0, 256, 1, 8))
+    dma("S", ("yn", None), R("YN", 0, 256, 1, 8))
     return ops, sends[0]
 
 
-def schedule(ops):
+def _pass(ops, links, prio, at):
     n = len(ops)
-    succ = [[] for _ in range(n)]
     npred = [0] * n
-
-    def lag(j, i, hard):
-        a, b = ops[j], ops[i]
-        if not hard and j not in b["after"]:
-            return None
-        if a["lat"] is not None:
-            return a["cost"] + a["lat"]
-        return a["cost"] + (OWN if a["eng"] == b["eng"] else HOP)
     for i in range(n):
-        for j, hard in ops[i]["deps"].items():
-            succ[j].append((i, lag(j, i, hard)))
-            npred[i] += 1
-    prio = [0.0] * n
-    for i in range(n - 1, -1, -1):
-        best = ops[i]["cost"]
-        for (k, lg) in succ[i]:
-            best = max(best, prio[k] + (lg if lg is not None else 0.0))
-        prio[i] = best
-    for i in range(n):
-        s = ops[i]["stage"]
-        prio[i] += PLAN["bias"].get((s[0], s[2]), 0.0)
+        for (k, lg) in links[i]:
+            npred[k] += 1
     ready = {e: [] for e in "VSTGQ"}
-    at = [0.0] * n
     for i in range(n):
         if npred[i] == 0:
             ready[ops[i]["eng"]].append(i)
@@ -538,25 +589,50 @@ def schedule(ops):
     order = []
     start = [0.0] * n
     while len(order) < n:
-        best = None
-        for e in ready:
-            if not ready[e]:
-                continue
-            t0 = min(max(free[e], at[i]) for i in ready[e])
-            if best is None or t0 < best[0]:
-                best = (t0, e)
-        t0, e = best
-        i = max((k for k in ready[e] if max(free[e], at[k]) <= t0 + 1e-9), key=lambda k: (prio[k], -k))
+        t0, e = min((max(free[e], min(at[i] for i in ready[e])), e) for e in ready if ready[e])
+        i = max(ready[e], key=lambda k: (prio[k] - PLAN["wait"] * max(0.0, at[k] - t0), -k))
+        t0 = max(t0, at[i])
         ready[e].remove(i)
         start[i] = t0
         order.append(i)
         free[e] = t0 + ops[i]["cost"]
-        for (k, lg) in succ[i]:
-            at[k] = max(at[k], t0 + (lg if lg is not None else 0.0))
+        for (k, lg) in links[i]:
+            at[k] = max(at[k], t0 + lg)
             npred[k] -= 1
             if npred[k] == 0:
                 ready[ops[k]["eng"]].append(k)
-    return order, start, free
+    return order, start, max(start[i] + ops[i]["cost"] + (ops[i]["lat"] or 0.0) for i in range(n))
+
+
+def schedule(ops):
+    n = len(ops)
+    succ = [[] for _ in range(n)]
+    pred = [[] for _ in range(n)]
+    for i in range(n):
+        b = ops[i]
+        for j, hard in b["deps"].items():
+            a = ops[j]
+            if not hard and j not in b["after"]:
+                lg = a["cost"] if a["eng"] == b["eng"] else 0.0
+            elif a["lat"] is not None:
+                lg = a["cost"] + a["lat"]
+            else:
+                lg = a["cost"] + (OWN if a["eng"] == b["eng"] else HOP)
+            succ[j].append((i, lg))
+            pred[i].append((j, lg - a["cost"] + b["cost"]))
+    prio = [0.0] * n
+    for i in range(n - 1, -1, -1):
+        prio[i] = max([ops[i]["cost"] + (ops[i]["lat"] or 0.0)] + [prio[k] + lg for (k, lg) in succ[i]])
+    for i in range(n):
+        s = ops[i]["stage"]
+        prio[i] += PLAN["bias"].get("%s%d" % (s[0], s[2]), 0.0)
+    best = now = _pass(ops, succ, prio, [0.0] * n)
+    for _ in range(PLAN["turns"]):
+        back = _pass(ops, pred, [now[1][i] + ops[i]["cost"] + (ops[i]["lat"] or 0.0) for i in range(n)], [o["lat"] or 0.0 for o in ops])
+        now = _pass(ops, succ, [back[1][i] + ops[i]["cost"] for i in range(n)], [0.0] * n)
+        if now[2] < best[2]:
+            best = now
+    return best
 
 
 def rank_program(g, core, T, topo):
@@ -566,10 +642,13 @@ def rank_program(g, core, T, topo):
     order, start, free = schedule(ops)
     queue = {"V": g.vector, "S": g.scalar, "T": g.tensor, "G": g, "Q": g.sync}
     need = set()
+    place = {i: p for p, i in enumerate(order)}
     for i in order:
+        late = {}
         for j, hard in ops[i]["deps"].items():
-            if hard and not ops[j]["dma"]:
-                need.add(j)
+            if hard and not ops[j]["dma"] and place[j] > place.get(late.get(ops[j]["eng"]), -1):
+                late[ops[j]["eng"]] = j
+        need.update(late.values())
     count = {e: 0 for e in queue}
     mark = {}
     know = {e: {} for e in queue}
@@ -579,7 +658,7 @@ def rank_program(g, core, T, topo):
         e = o["eng"]
         want = {}
         for j, hard in o["deps"].items():
-            if not hard or ops[j]["dma"] == "sent":
+            if not hard or j not in mark:
                 continue
             s, v = mark[j]
             if know[e].get(s, 0) < v:

@@ -7,31 +7,33 @@ VISITS = 4
 DEAD, JUNK = 4096, 4352
 BF, F32, I32, U16 = "bfloat16", "float32", "int32", "uint16"
 SCRATCH = {
-    "X": ("sbuf", [128, JUNK + 4096], BF),
-    "ZZ": ("sbuf", [128, 4096], BF), "XD": ("sbuf", [128, 4096], BF), "M0": ("sbuf", [128, 256], BF),
+    "X0": ("sbuf", [128, JUNK + 4096], BF), "X1": ("sbuf", [128, JUNK + 4096], BF),
+    "ZZ": ("sbuf", [128, 4096], BF), "XD": ("sbuf", [128, 4096], BF), "MO": ("sbuf", [128, 128 * 24], BF),
     "WL": ("sbuf", [128, 256], I32), "WN": ("sbuf", [8, 256], I32), "WT": ("sbuf", [128, 1], I32), "TH": ("sbuf", [8, 1], I32),
-    "WNB": ("sbuf", [8, 256], BF), "THM": ("sbuf", [8, 128], BF), "SD": ("sbuf", [128, 32], BF),
-    "CI": ("sbuf", [128, 144], I32), "CG": ("sbuf", [128, 144], I32), "KI": ("sbuf", [128, 128], I32), "CD": ("sbuf", [128, 128], I32), "CS": ("sbuf", [128, 32], I32),
-    "PI": ("sbuf", [128, 8], I32), "KF": ("sbuf", [128, 32], F32),
+    "WNB": ("sbuf", [8, 256], BF), "THM": ("sbuf", [8, 128], BF),
+    "CI": ("sbuf", [128, 144], I32), "CG": ("sbuf", [128, 128], I32), "KI": ("sbuf", [128, 128], I32), "ONF": ("sbuf", [128, 128], F32),
+    "PI": ("sbuf", [128, 8], I32), "KF": ("sbuf", [128, 40], F32),
     "EQ": ("sbuf", [128, 24], F32), "T2": ("sbuf", [128, 144], BF),
     "IDF": ("sbuf", [128, 128], F32), "DUP": ("sbuf", [128, 128], F32), "SGF": ("sbuf", [128, 16], F32), "SGD": ("sbuf", [128, 32], F32), "O16": ("sbuf", [128, 128], F32),
-    "BK": ("sbuf", [128, 1024], BF), "SGB": ("sbuf", [128, 8], BF), "SG32": ("sbuf", [128, 8], BF), "WG": ("sbuf", [128, 8], BF), "SGT": ("sbuf", [8, 128], BF),
-    "BS": ("sbuf", [128, 16], BF), "FE": ("sbuf", [128, 16], U16), "TG": ("sbuf", [128, 16], U16), "UA": ("sbuf", [128, 48], I32),
-    "ZF": ("sbuf", [128, 256], BF), "SU": ("sbuf", [128, 256], BF), "SV": ("sbuf", [128, 256], I32),
+    "BK": ("sbuf", [128, 1024], BF), "SGB": ("sbuf", [128, 8], BF), "SGT": ("sbuf", [8, 128], BF),
+    "BS": ("sbuf", [128, 16], BF), "FE": ("sbuf", [128, 16], U16), "HF": ("sbuf", [128, 16], U16), "TG": ("sbuf", [128, 32], U16),
+    "UA": ("sbuf", [128, 96], I32), "UF": ("sbuf", [128, 96], F32),
+    "ZF": ("sbuf", [128, 256], BF), "SU": ("sbuf", [128, 256], BF), "SV": ("sbuf", [128, 512], I32),
     "AI": ("sbuf", [128, 8], I32), "AF": ("sbuf", [128, 8], F32), "AC": ("sbuf", [128, 8], F32),
     "YL": ("sbuf", [128, 256], F32), "YN": ("sbuf", [8, 256], F32),
 }
-MATS = ("IDB", "I17", "I50", "BO", "SAME", "PAT", "WX", "N16", "ON", "C3", "C512") + tuple(n + e for n in ("NBO", "SH", "SH32", "TRI", "TRD") for e in "EO")
+MATS = ("IDB", "WX", "N16", "IH", "NIB", "MON", "I17", "I50", "BO", "SAME", "PAT", "ON", "C3", "C512") + tuple(n + e for n in ("NBO", "SH", "SH32", "TRI", "TRD") for e in "EO")
 SCRATCH["CM"] = ("sbuf", [128, 128 * len(MATS)], BF)
-for _n in ("ZO", "ZW", "ZK", "ZN"):
+SCRATCH["WV"] = ("sbuf", [128, 4 * 144], BF)
+for _n in ("ZO", "ZW", "ZK", "ZN", "ZU", "Z32"):
     SCRATCH[_n] = ("sbuf", [128, 144], BF)
 for _h in (0, 1):
-    SCRATCH["KW%d" % _h] = ("sbuf", [128, 136], BF)
     SCRATCH["K2%d" % _h] = ("sbuf", [128, 256], BF)
+    SCRATCH["KW%d" % _h] = ("sbuf", [128, 136], BF)
     SCRATCH["V%d" % _h] = ("sbuf", [128, 2064], BF)
     for _n in ("MN", "MK", "AE", "XH"):
         SCRATCH["%s%d" % (_n, _h)] = ("sbuf", [128, 2048], BF)
-    SCRATCH["MO%d" % _h] = ("sbuf", [128, 128 * 12], BF)
+    SCRATCH["CW%d" % _h] = ("sbuf", [128, 128 * 8], BF)
     SCRATCH["PD%d" % _h] = ("sbuf", [128, 128 * 12], F32)
     SCRATCH["OF%d" % _h] = ("sbuf", [128, 128], U16)
     SCRATCH["HU%d" % _h] = ("sbuf", [128, 128], U16)
@@ -51,10 +53,29 @@ ENGS = "VSTG"
 SEMAPHORES = ["e" + e for e in ENGS] + ["sent"] + ["rx%d%d" % (t, h) for t in range(VISITS) for h in (0, 1)] \
     + ["rm%d%d" % (t, h) for t in range(VISITS) for h in (0, 1)] + ["dm%d" % i for i in range(12)]
 
-CYC, FIX, GAT, SCA, PE, HOP, OWN, NET = 0.9, 30.0, 1.56, 3.8, 0.45, 100.0, 40.0, 2800.0
-PLAN = {"gv": ("SSVS", "VSSS"), "gh": ("VSSS", "VVSS"), "mk": ("PPPP", "PPPP"), "wait": 30.0, "um": "SS", "hm": "VS", "turns": 3,
-        "bias": {"back0": 2500, "front1": -5700, "names1": 1700, "places0": -1300, "front0": -3400, "places1": -2500, "back1": 3700,
-                 "write0": 4900, "middle0": -2500, "count0": 4800, "names0": 4200, "count1": -3700}}
+CYC, FIX, SFIX, TFIX, GAT, SCA, PE, HOP, OWN, NET = 0.83, 12.0, 45.0, 6.0, 1.6, 3.8, 0.42, 200.0, 200.0, 3000.0
+PLAN = {"gv": ("VSSS", "VSSS"), "gh": ("VSVT", "VSVV"), "mk": ("PPSP", "PPPP"), "um": "VS", "hm": "SS", "se": "QH", "mw": ("NN", "NN"), "aw": ("WN", "NN"),
+        "vw": ("WW", "WW"), "hw": ("WW", "WW"), "kq": "QQ", "uq": "QQ", "kn": "V", "s9": "V", "cl": "VV", "kc": "VV", "gl": "VV", "ov": "VV", "pl": "TT", "sc": "VV",
+        "fd": "W", "fu": "W", "k2": "SS", "aff": 0, "nm": "11", "no": "11", "np": "22", "wait": 30.0, "tables": 1, "early": 0, "sn": 1, "turns": 1}
+RANK = ({'kn00': 51, 'mn01': 17, 'zf1': 11, 'mn10': -43, 'z30': 34, 'gh11': -25, 'places1': 21, 'h10': 22, 'mask11': -1, 'df31': 28, 'count1': -31, 'ab20': -21, 'mask01': -40, 'count0': 17, 'gh10': -18, 'mn30': -80, 'gh31': -21, 'join1': 22, 'z00': 1, 'ab31': -45, 'mn20': 17, 'df00': 44, 'z20': 45, 'd00': -18, 'mn21': -51, 'gh00': 79, 'h00': -22, 'mask10': 81, 'z11': -40, 'mn00': -17, 'z10': 12, 'run1': -17, 'back0': 5, 'df11': -14, 'gh21': 15, 'send1': -38, 'join0': 19, 'u10': -6, 'kn11': -4, 'ab00': 78, 'p11': 11, 'u00': 9, 'back1': 1, 'ab10': 33, 'd01': 31, 'df30': -10, 'df10': 19, 'ab11': 11, 'kn10': 13, 'gh30': 13, 'gv20': 13, 'gv01': -24, 'df21': -49, 'u11': 1, 'mn11': -20, 'wr21': -34, 'df01': 1, 'gv30': -28, 'ab21': 15, 'fe1': 3, 'runs1': 31, 'gv11': 56, 'z21': 13, 'ab30': 11, 'gv00': -7, 'ab01': 20, 'h11': -22, 'run0': -27, 'wr1': -49, 'gv10': 37, 'places0': 3, 'gh01': 3, 'df20': -14, 'z31': 1, 'kn01': 1, 'gv21': 1, 'send0': -26, 'z01': -2, 'h01': -6},
+        {'count1': -4, 'gh21': -14, 'join0': -12, 'mn10': -6, 'mn11': -5, 'gv30': -21, 'gh01': -39, 'places1': -3, 'count0': -5, 'ab00': 23, 'gv11': -7, 'h10': 7, 'mask11': 2, 'd00': -5, 'kn00': 4, 'gv20': 1, 'df20': 5, 'z20': -5, 'send1': -10, 'z11': 9, 'h11': 27, 'mn00': 8, 'gh31': 1, 'kn01': 7, 'df30': 34, 'gv10': -34, 'kn10': -6, 'mn01': -5, 'z31': 26, 'u10': 6, 'ab11': -14, 'z00': 2, 'df01': -3, 'ab01': 2, 'mask00': -29, 'gh30': 1, 'df00': -7, 'mn21': -9, 'send0': 7, 'z01': 19, 'z30': -4, 'mask10': -3, 'ab10': -14, 'fe1': -5, 'gh00': 5, 'zf1': -8, 'u00': -11, 'run0': -13, 'p11': 8, 'mn30': -8, 'u11': -9, 'gh10': -5, 'z21': 13, 'gh11': -15, 'back1': 3, 'mn20': -5, 'ab20': -10, 'wr21': -4, 'ab30': 4, 'gv00': -5, 'df11': -6, 'd01': -21, 'z10': -9, 'gv01': -14, 'd10': -7, 'run1': -5, 'gv31': 3, 'places0': 16, 'mask01': 8, 'kn11': 8, 'mn31': 8, 'df31': -3, 'p10': -17, 'ab21': 5, 'u01': 10, 'ab31': 15, 'runs1': -4, 'df21': -5, 'gh20': 3, 'join1': -8})
+
+
+PLAN.update({'aff': 16, 'kn': 'S', 's9': 'S', 'gv': ('VSSV', 'VSSS'), 'gh': ('VVST', 'SVVS'), 'mk': ('PPPP', 'PPPS'), 'um': 'VV', 'hm': 'II', 'se': 'QH', 'mw': ('NN', 'NW'), 'aw': ('NW', 'WW'), 'nm': '12', 'no': '12', 'np': '22', 'vw': ('WW', 'WW'), 'hw': ('WW', 'WW'), 'kq': 'QQ', 'uq': 'QQ', 'cl': 'SV', 'kc': 'SS', 'gl': 'VS', 'ov': 'SS', 'pl': 'TV', 'sc': 'SS'})
+RANK = {'df31': -59, 'ab31': 37, 'gv00': 16, 'z00': 6, 'gv11': -46, 'ab11': 26, 'zf1': 33, 'back0': 6, 'mask00': 57, 'd00': -37, 'gh00': 12, 'runs1': 31, 'count1': 10, 'u01': -15, 'gh11': -9, 'back1': -18, 'df01': 53, 'mn20': -13, 'wr1': -9, 'mn21': 30, 'mn00': -32, 'join0': -22, 'mask10': -34, 'mn11': 23, 'z30': 18, 'places1': -15, 'kn11': -15, 'df30': 14, 'kn01': 29, 'gh01': -3, 'places0': -13, 'p11': 47, 'z21': -31, 'gh10': 20, 'z31': 6, 'send0': -60, 'p10': -2, 'kn00': 29, 'df10': -38, 'd11': 26, 'gh20': -18, 'gv01': -5, 'mn31': 9, 'h11': -18, 'mn10': 33, 'gh21': 15, 'ab10': 23, 'u11': -2, 'ab30': 2, 'mn30': -6, 'mask01': -4, 'load1': -33, 'z20': 30, 'df21': -22, 'df20': -5, 'join1': -12, 'mask11': 3, 'z01': 4},{'d00': 5, 'mn31': 2, 'back0': -16, 'join1': 8, 'z20': -7, 'ab10': -18, 'mn01': -4, 'u00': -1, 'gv11': -4, 'gv01': -23, 'u01': 1, 'df10': 2, 'wr21': -3, 'kn01': 12, 'mn30': 13, 'ab31': -2, 'z01': 6, 'gv00': -2, 'gv21': 16, 'mn11': -12, 'u11': -3, 'gh10': -7, 'mn20': -6, 'join0': -7, 'gv10': -2, 'count0': -5, 'df21': 3, 'gh21': 2, 'mask01': 4, 'mn21': 1, 'z00': 8, 'df01': -3, 'df30': 7, 'wr1': 2, 'p11': -12, 'gh01': 2, 'gh00': -1, 'd11': -3, 'z30': 3, 'h01': 8, 'd10': -5, 'u10': 18, 'mn00': 6, 'gv20': 5, 'gh20': -2, 'mask10': -6, 'z21': -12, 'df20': -4, 'df11': -20, 'd01': 5, 'gh30': -1, 'z10': -10, 'ab00': 18, 'back1': -4, 'places0': -4, 'df31': 5, 'gh31': -5, 'load0': 1, 'z31': 1, 'send1': 4, 'gh11': -12, 'ab30': -5}
+
+
+PLAN.update({'aff': 1, 'gv': ('SVVS', 'SSSS'), 'gh': ('VTSV', 'VVSS'), 'mk': ('PPPP', 'SPPP'), 'um': 'VS', 'hm': 'SS', 'mw': ('NW', 'WW'), 'aw': ('NW', 'WW'), 'nm': '14', 'no': '12', 'np': '21', 'vw': ('NN', 'NW'), 'hw': ('WW', 'NN'), 'cl': 'VS', 'kc': 'VS', 'ov': 'SV', 'pl': 'VS', 'sc': 'VS', 'k2': 'VV'})
+RANK = {'mn10': -31, 'df10': -91, 'ab30': 34, 'wr1': -23, 'p11': 48, 'wr21': 73, 'gh21': -85, 'gh10': 64, 'mn20': -45, 'gv01': -53, 'kn10': 112, 'load1': -16, 'df01': -32, 'join0': 6, 'df30': 36, 'd10': -35, 'kn01': -34, 'gv00': 100, 'load0': 23, 'send0': -13, 'mn11': -44, 'fe1': -72, 'z20': -50, 'count1': -38, 'count0': 28, 'gv11': 2, 'join1': -39, 'd11': 84, 'mn31': -26, 'gv30': -41, 'run0': 3, 'df20': -44, 'mn01': -54, 'runs1': -80, 'z00': 70, 'mask00': -84, 'places1': 70, 'df31': 63, 'gh01': 15, 'ab10': 42, 'gh20': 35, 'mask11': -75, 'h01': 76, 'zf1': 27, 'z31': -9, 'send1': 39, 'df21': 89, 'u01': 44, 'df11': 31, 'kn00': -10, 'z11': -10, 'gv20': 8, 'df00': -147, 'kn11': 64, 'h00': -48, 'z10': 147, 'back0': -33, 'mn30': 130, 'run1': 13, 'gh00': 40, 'z30': 62, 'ab11': 38, 'back1': -54, 'ab00': 7, 'ab31': -14, 'gh11': 23, 'mn00': 39, 'u00': 18, 'gv21': 14, 'z21': 22, 'mask10': -3, 'z01': -9, 'places0': 14, 'gv10': 35, 'gh30': -4, 'gh31': -7, 'mask01': 10},{'run0': -6, 'z11': -10, 'wr1': -26, 'mn30': 15, 'mn01': 28, 'mask11': 3, 'ab00': -1, 'p10': 29, 'mask00': -5, 'd10': 29, 'join1': -7, 'kn01': 2, 'load1': -11, 'df10': -11, 'z00': 6, 'wr21': -31, 'gh21': 14, 'z10': 6, 'back0': 29, 'df21': 23, 'df00': 4, 'h01': 20, 'gv30': 1, 'ab10': 20, 'gh10': 18, 'gv00': 11, 'z30': 8, 'gv11': -20, 'kn11': 24, 'mask10': 1, 'd11': 35, 'mn20': 9, 'df30': 11, 'df20': 3, 'mn10': -3, 'gh01': 21, 'ab11': -26, 'gv21': 18, 'places0': 1, 'ab31': -33, 'df01': 32, 'load0': 10, 'kn00': 41, 'kn10': 6, 'send0': 35, 'mask01': -39, 'ab30': -5, 'run1': -7, 'z20': 6, 'gh20': -15, 'send1': 46, 'fe1': -32, 'gv20': -7, 'z01': 6, 'count0': -2, 'places1': -13, 'mn00': 16, 'df31': 32, 'df11': 15, 'count1': -18, 'u01': 2, 'z31': 8, 'runs1': -44, 'gh00': -11, 'back1': 17, 'gv01': -16, 'join0': -11, 'h00': 4, 'z21': -17, 'gh11': 30, 'p11': 3, 'gh30': -31, 'gv10': -16, 'zf1': 17, 'gh31': -11, 'u00': 5, 'mn11': 12, 'mn31': -11}
+
+
+PLAN.update({'fd': 'L', 'fu': 'L', 'gv': ('VSSS', 'VSVS'), 'gh': ('VSVS', 'VSVS'), 'mk': ('PPPP', 'PPPP'), 'um': 'VV', 'hm': 'II', 'mw': ('NN', 'NN'), 'aw': ('WN', 'NN'), 'nm': '21', 'no': '11', 'np': '11', 'vw': ('NN', 'NN'), 'hw': ('WN', 'WN'), 'cl': 'SS', 'kc': 'SV', 'ov': 'SS', 'pl': 'ST', 'sc': 'SS', 'k2': 'VS', 'se': 'HH', 'uq': 'QQ', 'gl': 'SS', 'kq': 'HQ'})
+RANK = {'mn21': 42, 'mask11': 1, 'ab11': 16, 'join0': 42, 'gv30': -43, 'count1': 17, 'mn00': 6, 'gh31': 14, 'mn30': 3, 'df10': 14, 'ab10': 23, 'mn20': 27, 'u11': 3, 'gh11': 11, 'mask00': 2, 'run1': 7, 'run0': 6, 'df31': 13, 'mask01': 20, 'h01': -4, 'join1': 5, 'z31': 8, 'z11': 17, 'z21': -23, 'places1': 23, 'z30': 36, 'gh00': 5, 'ab21': -20, 'd11': 21, 'gh01': 12, 'count0': 29, 'p10': 4, 'z10': 22, 'send0': -19, 'u01': -17, 'load0': -37, 'fe1': -31, 'df11': 39, 'df21': -5, 'gv11': -25, 'mask10': -6, 'df00': -8, 'gh30': 29, 'z00': 13, 'gv01': 30, 'd01': 13, 'runs1': 10, 'gh20': -6, 'h00': 1, 'kn01': 4, 'zf1': -8, 'kn10': 43, 'wr1': 44, 'gh10': -3, 'gv00': -22, 'h10': 31, 'df20': -2, 'ab31': 9, 'kn00': -3, 'z20': 1, 'ab00': -14, 'send1': -3, 'gv21': 18, 'h11': -3, 'mn31': -21, 'wr21': 35, 'gh21': 47, 'ab01': -7, 'df01': 38, 'gv20': 5, 'gv31': 10, 'mn10': -20, 'd00': 5, 'mn11': -15},{'kn00': 22, 'ab10': 9, 'mask01': -10, 'p11': 2, 'df21': 5, 'kn11': -10, 'count0': 6, 'df30': -14, 'join1': 14, 'mn21': -1, 'kn01': -10, 'wr21': -14, 'df31': 4, 'df10': -5, 'mn00': -14, 'u00': 4, 'gv11': -18, 'places0': -25, 'kn10': 2, 'run0': -2, 'gv20': 5, 'ab31': -3, 'ab20': -1, 'h10': -2, 'gv30': -9, 'count1': -3, 'load1': -1, 'df00': -4, 'gh30': -1, 'df01': 2, 'z00': -6, 'z11': 6, 'gv01': 10, 'z01': -6, 'ab00': 6, 'gh31': -3, 'zf1': -11, 'mn01': 2, 'ab11': 6, 'u11': -2, 'gv21': 1, 'mask00': 6, 'send0': -23, 'gh10': 3, 'wr1': -16, 'runs1': 13, 'gh11': 4, 'ab21': -2, 'ab01': -14, 'u01': 1, 'd10': 2, 'z20': 3, 'gh21': 2, 'mn10': -3, 'fe1': 13, 'h01': 10, 'mn31': -9, 'gv00': -4, 'h11': 4, 'join0': 7, 'mn11': -4, 'df20': -7, 'mask11': -21, 'mn20': 4, 'places1': -11, 'd01': 7, 'h00': 2, 'z30': 1, 'gh01': 8, 'send1': 17, 'p10': -1, 'mask10': 1, 'load0': 4}
+
+
+TFIX = 12.0
+PLAN.update({'fd': 'W', 'fu': 'W', 'early': 1, 'gv': ('VSVS', 'VSSS'), 'gh': ('VTVS', 'VSVS'), 'mk': ('PPPP', 'PPPP'), 'um': 'VV', 'hm': 'JJ', 'mw': ('NW', 'WN'), 'aw': ('NN', 'NN'), 'nm': '12', 'no': '24', 'np': '11', 'vw': ('NN', 'WN'), 'hw': ('WN', 'WN'), 'cl': 'SS', 'kc': 'VS', 'ov': 'SS', 'pl': 'VS', 'sc': 'SV', 'k2': 'SV'})
+RANK = {'send0': -71, 'df20': -22, 'runs1': -47, 'gv01': -5, 'h01': -60, 'h00': 16, 'df30': -38, 'ab30': -9, 'mask11': 26, 'wr21': 70, 'mn20': -21, 'ab01': -34, 'mn21': -73, 'mn01': 62, 'y01': -19, 'ab00': -19, 'gh20': 104, 'mask00': -9, 'send1': -8, 'join0': -24, 'z21': 13, 'gh11': 57, 'gh30': -2, 'df10': -17, 'p10': 7, 'kn11': 19, 'join1': -9, 'z10': 2, 'gh10': 14, 'd11': -16, 'p11': -65, 'u01': 12, 'fe1': -7, 'load1': 76, 'zf1': -20, 'mn30': -52, 'mn11': -17, 'gh31': 2, 'kn01': -7, 'z11': 55, 'u00': -28, 'ab31': 29, 'gh00': 10, 'df01': 9, 'z30': 44, 'mask10': -13, 'mn00': -37, 'df31': 13, 'df11': 42, 'places0': 6, 'gv21': -70, 'df00': 12, 'count1': 10, 'd10': -27, 'gv20': -5, 'gv11': -20, 'count0': -5, 'z31': 34, 'mn31': 12, 'mn10': 12, 'ab11': 2, 'gv30': -13, 'gv10': -57, 'kn10': -9, 'back1': 20, 'mask01': -14, 'z01': 54, 'gh01': -23, 'gh21': 10, 'places1': -36, 'ab20': 1, 'z00': 16, 'kn00': -37, 'gv00': 28, 'ab10': 11, 'df21': -22, 'run0': -1, 'load0': 14, 'y00': 25, 'z20': -12, 'back0': -16, 'ab21': 23, 'wr1': -29, 'run1': -5},{'kn11': -8, 'ab31': 15, 'kn00': -16, 'df10': 7, 'gh10': 10, 'mask01': 1, 'mn11': -14, 'h01': 5, 'gh20': 2, 'ab30': -10, 'z11': 24, 'df01': 36, 'gv00': 9, 'mn10': 17, 'gv30': -7, 'gv11': 15, 'gv01': 1, 'load1': 28, 'y01': 1, 'gh01': 29, 'p10': -1, 'gv10': -11, 'ab21': -29, 'p11': -11, 'z20': -7, 'ab01': -17, 'ab00': 26, 'mn20': -3, 'join0': 4, 'places1': -3, 'join1': 17, 'df30': 16, 'ab20': -1, 'mn01': 10, 'wr21': 21, 'send0': 5, 'df31': 16, 'count0': -17, 'gv31': -10, 'z10': -7, 'gh21': 15, 'gh11': -9, 'gh30': 3, 'df20': -5, 'mn30': -2, 'u00': 17, 'gv21': 11, 'gh31': -13, 'z21': -9, 'wr1': -20, 'df21': 18, 'gh00': -13, 'mn00': 20, 'ab10': -3, 'count1': -11, 'z31': -7, 'mask11': 2, 'runs1': 12, 'load0': 12, 'send1': -6, 'back0': -10, 'back1': 1, 'ab11': 1, 'df00': 2, 'places0': 2, 'h00': -3, 'y00': -10, 'mask00': -4, 'z00': 9, 'z30': -3, 'd11': -9, 'df11': 4, 'gv20': 6, 'mn31': -17, 'kn01': -12, 'zf1': 1, 'run1': 3, 'mask10': 2, 'z01': -7, 'mn21': 1, 'run0': -7, 'd10': 2}
 
 
 def R(b, c0, c1, step=1, p=128):
@@ -181,19 +202,24 @@ def build(g, T, topo, core):
     def ms(out, val):
         return add("V", lambda: g.vector.memset(ap(out), val), [], regs(out), vcost(out, []))
 
-    def act(out, a, func, bias=0.0, scale=1.0, acc=None):
+    def act(out, a, func, bias=0.0, scale=1.0, acc=None, **kw):
         n = _n(out) * (GAT if len(a) == 2 else 1)
         if func == F.Copy and not isinstance(bias, float):
             func = F.Identity
         if acc is None:
-            fn = lambda: g.scalar.activation(ap(out), ap(a), func, bias=ap(bias), scale=scale)
+            fn = lambda: g.scalar.activation(ap(out), ap(a), func, bias=ap(bias), scale=ap(scale))
         else:
-            fn = lambda: g.scalar.activation(ap(out), ap(a), func, bias=ap(bias), scale=scale, accum_out=ap(acc))
-        return add("S", fn, regs(a) + regs(bias), regs(out) + regs(acc), FIX + 15 + CYC * max(64, n))
+            fn = lambda: g.scalar.activation(ap(out), ap(a), func, bias=ap(bias), scale=ap(scale), accum_out=ap(acc))
+        return add("S", fn, regs(a) + regs(bias) + regs(scale), regs(out) + regs(acc), SFIX + CYC * max(64, n), **kw)
+
+    def lin(eng, out, a, scale, bias):
+        if eng == "S":
+            return act(out, a, F.Copy, bias, scale)
+        return ts(out, a, scale, bias, A.mult, A.add)
 
     def mm(out, lhsT, rhs, start=True, stop=True, grp=None, **kw):
         f = 4 if SCRATCH[lhsT[0]][2] == F32 else 1
-        return add("T", lambda: g.tensor.matmul(ap(out), ap(lhsT), ap(rhs), start, stop), regs(lhsT) + regs(rhs), regs(out), 5 + PE * f * max(64, _n(rhs)), grp=grp, **kw)
+        return add("T", lambda: g.tensor.matmul(ap(out), ap(lhsT), ap(rhs), start, stop), regs(lhsT) + regs(rhs), regs(out), TFIX + PE * f * max(64, _n(rhs)), grp=grp, **kw)
 
     def msum(out, terms, **kw):
         gr = ("sum", len(ops))
@@ -213,105 +239,126 @@ def build(g, T, topo, core):
     def win(n, k):
         return R(n, 15 - k, 143 - k)
 
-    dma("Q", R("X", 0, 4096), ("xv", None), 6000.0)
-    dma("S", R("WL", 0, 256), ("wl", None))
-    dma("S", R("WN", 0, 256, 1, 8), ("wn", None))
-    dma("Q", R("TH", 0, 1, 1, 8), ("th", None))
-    dma("Q", R("WT", 0, 1), ("wt", None))
-    add("G", lambda: g.iota(ap(R("CI", 0, 144)), [[1, 144]], 0, 0), [], [R("CI", 0, 144)], 400.0)
-    add("G", lambda: g.iota(ap(R("PI", 0, 1)), [[1, 1]], 0, 1), [], [R("PI", 0, 1)], 150.0)
-    PI, PGI, PKI, P8I = [R("PI", c, c + 1) for c in range(4)]
-    PF, PG, T15, KP, L16, WC, P8, KO, CB, CBD, Q1, Q2, P7 = [R("KF", c, c + 1) for c in range(13)]
+    small = [dma("Q", R("WT", 0, 1), ("wt", None), 4000.0), dma("S", R("WN", 0, 256, 1, 8), ("wn", None), 4000.0),
+             dma("S", R("TH", 0, 1, 1, 8), ("th", None), 4000.0), dma("Q", R("WL", 0, 256), ("wl", None), 4000.0)]
+    dma("Q", R("X0", 0, 4096), ("xv", None), 8000.0)
+    ops[-1]["deps"].update({j: False for j in small})
+    NX = PLAN["tables"]
+    if NX == 2:
+        add("Q", lambda: g.sync.dma_start(ap(R("X1", 0, 4096)), T.xv[:]), [R("X0", 0, 16)], [R("X1", 0, 4096)], 100.0, dma="dm11", lat=8000.0)
+    def iota(out, pattern, base=0, mult=0):
+        add("G", lambda: g.iota(ap(out), pattern, base, mult), [], [out], 150.0 + 2 * CYC * _n(out))
+
+    def pick(out, a, pattern, op, fill, base):
+        add("G", lambda: g.affine_select(ap(out), ap(a), pattern, op, fill, base, -1), [a], [out], 170.0 + 2 * CYC * _n(out))
+
+    def aff(out, a, scale, bias=0.0):
+        lin("S" if _n(out) > PLAN["aff"] else "V", out, a, float(scale) if isinstance(scale, int) else scale, float(bias) if isinstance(bias, int) else bias)
+    PI, PGI, PKI, P8I, P7I, PCI = [R("PI", c, c + 1) for c in range(6)]
+    PF, PG, KP, P8, P7, PC, T15, L16, WC, KO, CB, CBD, Q1, Q2, Q3, Q4, TB, RUB, SQB, WU = [R("KF", c, c + 1) for c in range(20)]
     OVC = [R("KF", 20 + j, 21 + j) for j in range(4)]
-    C128, C144 = R("CI", 0, 128), R("CI", 0, 144)
+    C144, K7 = R("CI", 0, 144), R("HI1", 768, 896)
+    iota(PI, [[1, 1]], 0, 1)
+    iota(C144, [[1, 144]])
+    iota(M("CG"), [[1, 8], [0, 16]])
+    iota(K7, [[0, 16], [1, 8]])
+    iota(M("KI"), [[0, 8], [1, 16]])
+    MARK = 2 if PLAN["kn"] == "V" else 1
+    ms(M("ONF"), 1.0)
+    ms(R("AE0", 0, 1024), float(MARK))
     for h in (0, 1):
         ms(R("V%d" % h, 0, 16), 0.0)
-        ms(R("KW%d" % h, 0, 8), 0.0)
     ms(M("ON"), 1.0)
-    ms(M("N16"), -16.0)
-    ms(M("C3"), 3.0)
-    ms(M("C512"), 512.0)
-    ms(M("O16"), 0.25)
-    cp(PF, PI)
     ts(PGI, PI, 4, None, A.logical_shift_right)
     ts(PKI, PI, 15, None, A.bitwise_and)
     ts(P8I, PI, 3, None, A.logical_shift_right)
-    cp(PG, PGI)
-    cp(KP, PKI)
-    cp(P8, P8I)
-    ts(T15, PGI, 16, 15, A.mult, A.add)
-    ts(L16, PKI, 16, None, A.mult)
-    ts(KO, PKI, 16384, -15 * 16384, A.mult, A.add)
-    ts(CB, PKI, 0.5, 50.5, A.mult, A.add)
+    ts(P7I, PI, 7, None, A.bitwise_and)
+    ts(PCI, PI, 3, 1, A.logical_shift_right, A.bitwise_and)
+    cp(R("KF", 0, 6), R("PI", 0, 6))
+    for n, f in (("C3", 3), ("C512", 512), ("O16", 0.25), ("MON", -1.0 / 128)):
+        aff(M(n), M("ON"), f)
+    aff(T15, PG, 16, 15)
+    aff(L16, KP, 16)
+    aff(KO, KP, 16384, -15 * 16384)
+    CBS, CDS = [R("KF", 32 + j, 33 + j) for j in range(4)], [R("KF", 36 + j, 37 + j) for j in range(4)]
+    for j in range(max(int(x) for x in PLAN["nm"])):
+        aff(CBS[j], KP, 0.5, 50.5 - j)
+    for j in range(max(int(x) for x in PLAN["no"])):
+        aff(CDS[j], P7, 0.5, 54.5 - j)
+    aff(Q2, P7, *((-0.5, 54) if PLAN["s9"] == "V" else (0.5, -54)))
+    for j in range(4):
+        aff(OVC[j], PC, 4, 159 + j)
     ts(R("EQ", 0, 16), R("CI", 0, 16), KP, None, A.is_equal)
-    ts(R("X", DEAD, DEAD + 16), R("EQ", 0, 16), R("EQ", 0, 1), 255, A.mult, A.mult)
-    ts(R("CG", 0, 144), C144, 4, None, A.logical_shift_right)
-    ts(M("KI"), C128, 15, None, A.bitwise_and)
+    for n in ("X0", "X1")[:NX]:
+        ts(R(n, DEAD, DEAD + 16), R("EQ", 0, 16), R("EQ", 0, 1), 255, A.mult, A.mult)
     ts(R("SGT", 0, 128, 1, 8), R("CG", 0, 128, 1, 8), R("KF", 0, 1, 1, 8), None, A.is_equal)
-    ts(M("IDF"), C128, PF, None, A.is_equal)
-    ts(M("IDB"), C128, PF, None, A.is_equal)
-    ts(M("BO"), R("CG", 0, 128), PG, None, A.is_equal)
+    pick(M("IDF"), M("ONF"), [[1, 128]], A.is_equal, 0.0, 0)
+    pick(R("BK", 0, 1024), R("AE0", 0, 1024), [[8, 8], [1, 8], [0, 16]], A.is_equal, 0.0, 0)
+    aff(M("IDB"), M("IDF"), 1)
+    ts(M("BO"), M("CG"), PG, None, A.is_equal)
     ts(R("ZO", 0, 144), C144, T15, None, A.is_equal)
     ts(R("SGB", 0, 8), R("CI", 0, 8), PG, None, A.is_equal)
-    ts(R("SD", 0, 8), R("SGB", 0, 8), -1, None, A.mult)
-    ts(R("SD", 8, 16), R("SGB", 0, 8), -1, None, A.mult)
-    ts(R("SD", 16, 24), R("SGB", 0, 8), R("EQ", 0, 1), None, A.mult)
-    ts(R("SD", 24, 32), R("SGB", 0, 8), 2, None, A.mult)
-    K7 = R("HI0", 0, 128)
-    ts(K7, C128, 7, None, A.bitwise_and)
-    cp(R("KF", 17, 18, 1, 8), R("TH", 0, 1, 1, 8))
     cp(R("WNB", 0, 256, 1, 8), R("WN", 0, 256, 1, 8))
     cp(WC, R("WT", 0, 1))
-    ts(R("THM", 0, 120, 1, 8), R("HI0", 0, 120, 1, 8), R("KF", 0, 1, 1, 8), R("KF", 17, 18, 1, 8), A.is_equal, A.mult)
-    ts(R("THM", 120, 128, 1, 8), R("HI0", 120, 128, 1, 8), R("KF", 0, 1, 1, 8), -100, A.is_equal, A.mult)
-    ts(R("PI", 4, 5), PI, 7, None, A.bitwise_and)
-    cp(P7, R("PI", 4, 5))
-    ts(M("SAME"), R("CG", 0, 128), P7, None, A.is_equal)
-    ts(R("EQ", 16, 24), R("CI", 0, 8), P8, None, A.is_equal)
-    for j in range(8):
-        ts(R("BK", 128 * j, 128 * j + 128), M("SAME"), R("EQ", 16 + j, 17 + j), None, A.mult)
-    ts(M("I17"), M("IDB"), -131072, None, A.mult)
-    ts(M("I50"), M("IDB"), 50, None, A.mult)
+    aff(WU, WC, 2.0 ** -12)
+    ts(Q4, PI, 8, -0.5, A.is_ge, A.mult)
+    if PLAN["fd"] == "W":
+        for c, f in ((0, -1), (8, -1), (16, R("EQ", 0, 1)), (24, 2)):
+            aff(R("WV", c, c + 8), R("SGB", 0, 8), f)
+        cp(Q3[:4] + (8,), R("TH", 0, 1, 1, 8))
+        ts(R("THM", 0, 120, 1, 8), R(K7[0], K7[1], K7[1] + 120, 1, 8), R("KF", 0, 1, 1, 8), Q3[:4] + (8,), A.is_equal, A.mult)
+        ts(R("THM", 120, 128, 1, 8), R(K7[0], K7[1], K7[1] + 8, 1, 8), R("KF", 0, 1, 1, 8), -100, A.is_equal, A.mult)
+        for h in (0, 1):
+            ms(R("KW%d" % h, 0, 8), 0.0)
+    else:
+        ms(R("WV", 0, 4 * 144), 0.0)
+        for c, f in ((64, -1), (72, -1), (144 + 64, 2), (288, -16), (288 + 8, -1), (432 + 56, -1), (432 + 64, R("EQ", 0, 1))):
+            aff(R("WV", c, c + 8), R("SGB", 0, 8), f)
+        cp(R("T2", 128, 129, 1, 8), R("TH", 0, 1, 1, 8))
+        ts(R("THM", 0, 128, 1, 8), K7[:4] + (8,), R("KF", 0, 1, 1, 8), None, A.is_equal)
+        mm(R("pb0", 0, 1), R("THM", 0, 128, 1, 8), R("T2", 128, 129, 1, 8))
+        ts(Q1, PI, 64, None, A.is_lt)
+        aff(Q3, R("pb0", 0, 1), 1, 100)
+        aff(TB, Q3, Q1, -99.5)
+        if PLAN["kn"] == "V":
+            aff(TB, TB, -1)
+    if PLAN["fu"] == "W":
+        aff(R("WV", 32, 40), R("SGB", 0, 8), WU)
+        aff(R("WV", 40, 48), R("SGB", 0, 8), 32)
+        aff(M("WX"), M("BO"), WU)
+        aff(M("N16"), M("ON"), -16)
+        RUB, SQB = 191.5 + 2.0 ** -13, 192.0 * 4096 + 592
+    else:
+        aff(R("T2", 130, 131), WC, 1)
+        mm(R("pb0", 1, 2), M("BO"), R("T2", 130, 131))
+        aff(RUB, R("pb0", 1, 2), -2.0 ** -8, 191.5 + 2.0 ** -13)
+        aff(SQB, R("pb0", 1, 2), -16, 192 * 4096 + 592)
+        for n, f in (("Z32", 32), ("ZU", WU)):
+            aff(R(n, 0, 144), R("ZO", 0, 144), f)
+    ts(M("SAME"), M("CG"), P7, MARK, A.is_equal, A.mult)
+    aff(M("I17"), M("IDF"), -131072)
+    aff(M("I50"), M("IDF"), 100 if PLAN["s9"] == "V" else 50)
+    aff(M("NIB"), M("IDF"), -1)
+    aff(M("IH"), M("IDF"), 0.5)
     ts(R("T2", 0, 128), M("KI"), 0, 0.25, A.is_gt, A.mult)
-    ts(M("PAT"), R("T2", 0, 128), -62 / 128, None, A.add)
-    ts(R("HI0", 128, 256), R("CG", 0, 128), 16, 8, A.mult, A.add)
-    tt(M("CD"), K7, R("HI0", 128, 256), A.add)
-    ts(M("DUP"), M("CD"), PF, None, A.is_equal)
-    ts(R("HI0", 256, 384), K7, 8, None, A.add)
-    ts(Q1, PI, 64, None, A.is_lt)
+    aff(M("PAT"), R("T2", 0, 128), 1, -62 / 128)
     for e in (0, 1):
-        same, x = R("HB0", 128 * e, 128 * e + 128), "EO"[e]
-        qp, qm = R("KF", 24 + 2 * e, 25 + 2 * e), R("KF", 25 + 2 * e, 26 + 2 * e)
-        ts(qp, P8I, 8 * e, None, A.add)
-        ts(qm, P8I, 8 * e - 1, None, A.add)
-        ts(same, M("SAME"), 1 if e else Q1, None, A.mult)
-        ts(M("NBO" + x), same, -0.5, None, A.mult)
-        ts(R("HB1", 0, 128), M("KI"), qp, None, A.is_equal)
-        tt(M("SH" + x), R("HB1", 0, 128), same, A.mult)
-        ts(M("SH32" + x), M("SH" + x), 32, None, A.mult)
-        for n, kk in (("TRI", M("KI")), ("TRD", R("HI0", 256, 384))):
-            ts(R("HB1", 128, 256), kk, qm, -0.5, A.is_ge, A.mult)
-            ts(R("HB1", 256, 384), kk, qm, -50, A.is_equal, A.mult)
-            tt(R("HB1", 384, 512), R("HB1", 128, 256), R("HB1", 256, 384), A.add)
-            tt(M(n + x), R("HB1", 384, 512), same, A.mult)
-    ts(CBD, R("PI", 4, 5), 0.5, 54.5, A.mult, A.add)
-    ts(Q2, CBD, -108.5, None, A.add)
-    ts(R("PI", 5, 6), P8I, 1, None, A.bitwise_and)
-    for j in range(4):
-        ts(OVC[j], R("PI", 5, 6), 4, 159 + j, A.mult, A.add)
-    ts(R("SG32", 0, 8), R("SGB", 0, 8), 32, None, A.mult)
-    ts(R("WG", 0, 8), R("SGB", 0, 8), WC, 2.0 ** -12, A.mult, A.mult)
-    ts(M("WX"), M("BO"), WC, 2.0 ** -12, A.mult, A.mult)
-    ts(R("ZW", 0, 144), R("ZO", 0, 144), WC, None, A.mult)
-    ts(R("ZK", 0, 144), R("ZO", 0, 144), KP, None, A.mult)
-    ts(R("ZN", 0, 144), R("ZO", 0, 144), -JUNK, None, A.mult)
-    ts(R("CS", 0, 16), R("CI", 0, 16), 7, None, A.bitwise_and)
-    ts(R("SGF", 0, 16), R("CS", 0, 16), PG, None, A.is_equal)
-    ts(R("CS", 0, 32), R("CI", 0, 32), 15, None, A.bitwise_and)
-    ts(R("SGD", 0, 32), R("CS", 0, 32), P8, None, A.is_equal)
+        x = "EO"[e]
+        aff(M("NBO" + x), M("SAME"), -0.5 if e else Q4)
+        pick(M("SH" + x), R("AE0", 0, 128), [[1, 8], [8, 16]], A.is_equal, 0.0, -64 * e)
+        aff(M("SH32" + x), M("SH" + x), 32)
+        for n, pattern, base in (("TRI", [[1, 8], [8, 16]], 8 - 64 * e), ("TRD", [[1, 8], [0, 2], [8, 8]], 72 - 64 * e)):
+            pick(M(n + x), M("NBO" + x), pattern, A.is_ge, 0.0, base)
+            pick(M(n + x), M(n + x), pattern, A.not_equal, -50.5 * MARK, base)
+    pick(M("DUP"), M("ONF"), [[16, 8], [0, 2], [1, 8]], A.is_equal, 0.0, 8)
+    aff(CB, KP, 1, 32)
+    for n, f in (("ZW", WC), ("ZK", CB)):
+        aff(R(n, 0, 144), R("ZO", 0, 144), f)
+    ts(R("SGF", 0, 16), R(K7[0], K7[1], K7[1] + 16), PG, None, A.is_equal)
+    ts(R("SGD", 0, 32), R("KI", 0, 32), P8, None, A.is_equal)
     ts(R("BS", 0, 16), R("CI", 0, 16), 256, L16, A.mult, A.add)
-    KOFF = R("pb3", 0, 128)
-    ts(KOFF, M("KI"), -16384, 15 * 16384, A.mult, A.add)
+    for h in (0, 1):
+        ts(R("pb%d" % (2 + h), 0, 128), M("KI"), -16384, 15 * 16384, A.mult, A.add)
 
     def H(kind, h, s, c0=0, c1=128, step=1):
         return R("%s%d" % (kind, h), 128 * s + c0, 128 * s + c1, step)
@@ -324,7 +371,7 @@ def build(g, T, topo, core):
 
     def hi(h, s, *a):
         return H("HI", h, s, *a)
-    KN, GG, CL, S9, OV, RU, RQ, LV = range(8)
+    GL, GG, CL, S9, OV, RU, RQ, LV = range(8)
     NM, KC, YY, RY, AG, PW, PL, FN = range(8)
     JI, NMI, A1, A2, B1, B2 = range(6)
 
@@ -333,6 +380,9 @@ def build(g, T, topo, core):
 
     def pB(h, r):
         return R("pb%d" % (5 + 2 * h), 128 * r, 128 * r + 128)
+
+    def pC(h, r):
+        return R("pb%d" % (2 + h), 128 * r, 128 * r + 128)
     rank = T.rank_of(core)
     sends = [0]
     lane = [0]
@@ -352,7 +402,7 @@ def build(g, T, topo, core):
         ts(R("OF%d" % h, 0, 128), hf(h, FN), DEAD, None, A.min)
         mm(pB(h, 0), hf(h, FN), M("IDF"))
         act(hf(h, AG), pB(h, 0), F.Copy)
-        tt(hf(h, NM), KOFF, hf(h, AG), A.add)
+        tt(hf(h, NM), pC(h, 0), hf(h, AG), A.add)
 
     def join(h, own, ov, waits, after):
         tt(hi(h, JI, 0, 64), own, ov, A.add, waits=waits, after=after)
@@ -360,38 +410,78 @@ def build(g, T, topo, core):
         ts(hi(h, NMI, 1, 128, 2), hi(h, JI, 0, 64), (1 << 24) + 4095, None, A.bitwise_and)
 
     def offsets(h):
-        tt(hf(h, NM), KOFF, hi(h, NMI), A.add)
-        mm(pB(h, 0), hf(h, NM), M("IDF"))
-        ts(R("OF%d" % h, 0, 128), pB(h, 0), KO, DEAD, A.add, A.min)
+        tt(hf(h, NM), pC(h, 0), hi(h, NMI), A.add)
+        mm(pC(h, 2), hf(h, NM), M("IDF"))
+        ts(R("OF%d" % h, 0, 128), pC(h, 2), KO, DEAD, A.add, A.min)
 
-    def mask(h, s):
-        return R("M0", 128 * h, 128 * h + 128) if s == 0 else R("MO%d" % h, 128 * s, 128 * s + 128)
-    XW = R("X", 0, DEAD + 16)
+    def tile(h, s):
+        return 16 + 4 * h + s - 8 if s >= 8 else 8 + s if h else 7 - s
+
+    def mask(h, s, n=1):
+        a = min(tile(h, s), tile(h, s + n - 1))
+        return R("MO", 128 * a, 128 * (a + n))
+
+    def table(t):
+        return R("X%d" % (t % NX), 0, DEAD + 16)
 
     def marks(n, h):
-        return [(M(n + "EO"[e])[:4] + (72,), R("K2%d" % h, e, 256, 2, 72)) for e in (0, 1)]
+        return [(M(n + "EO"[e])[:4] + (64 + 8 * e,), R("K2%d" % h, e, 256, 2, 64 + 8 * e)) for e in (0, 1)]
 
     def front(t, h):
-        stage[0] = ("front", t, h)
         v, mn, mk = "V%d" % h, "MN%d" % h, "MK%d" % h
         for c in range(4):
-            o, i = R(v, 16 + 512 * c, 528 + 512 * c), (XW, R("OF%d" % h, 32 * c, 32 * c + 32))
+            stage[0] = ("gv%d" % c, t, h)
+            o, i = R(v, 16 + 512 * c, 528 + 512 * c), (table(t), R("OF%d" % h, 32 * c, 32 * c + 32))
             if PLAN["gv"][h][c] == "V":
                 ts(o, i, 16, None, A.add)
-            else:
+            elif PLAN["vw"][h][c // 2] == "N" or "V" in PLAN["gv"][h][c - c % 2:c - c % 2 + 2]:
                 act(o, i, F.Copy, 16.0)
-            scan(R(mn, 512 * c, 512 * c + 512), R(v, 15 + 512 * c, 527 + 512 * c), o, A.max, A.min)
-        bank, kw, k2 = "pb%d" % (4 + 2 * h), "KW%d" % h, "K2%d" % h
-        msum(pA(h, 2), [(R("CM", M("ON")[1], M("ON")[2], 1, 8), R("THM", 0, 128, 1, 8))]
-             + [(R(bank, 256 + 8 * max(k - 1, 0), 264 + 8 * k), R(v, 16 + k, 2064, 16), R("SD", 0, 8) if k == 0 else R("SD", 8, 24) if k == 15 else R("SD", 0, 16)) for k in range(16)]
-             + [(R(bank, 248 + 8 * k, 256 + 8 * k), R(mn, k, 2048, 16), R("SD", 24, 32)) for k in range(1, 16)])
-        act(R(kw, 8, 136), pA(h, 2), F.Sign, 0.5)
-        for e in (0, 1):
-            mm(R(bank, e, 256, 2, 72), R(kw, 64 * e, 64 * e + 72), M("IDB"))
-        act(R(k2, 0, 256, 1, 72), R(bank, 0, 256, 1, 72), F.Copy)
+            elif c % 2 == 0:
+                act(R(v, 16 + 512 * c, 1040 + 512 * c), (table(t), R("OF%d" % h, 32 * c, 32 * c + 64)), F.Copy, 16.0)
+            stage[0] = ("mn%d" % c, t, h)
+            if PLAN["mw"][h][c // 2] == "N":
+                scan(R(mn, 512 * c, 512 * c + 512), R(v, 15 + 512 * c, 527 + 512 * c), o, A.max, A.min)
+            elif c % 2:
+                scan(R(mn, 512 * c - 512, 512 * c + 512), R(v, 512 * c - 497, 527 + 512 * c), R(v, 512 * c - 496, 528 + 512 * c), A.max, A.min)
+        k2 = "K2%d" % h
+        if PLAN["fd"] == "W":
+            stage[0] = ("kn0", t, h)
+            bank, kw = "pb%d" % (4 + 2 * h), "KW%d" % h
+            msum(pA(h, 2), [(M("ON")[:4] + (8,), R("THM", 0, 128, 1, 8))]
+                 + [(R(bank, 256 + 8 * max(k - 1, 0), 264 + 8 * k), R(v, 16 + k, 2064, 16), R("WV", 0, 8) if k == 0 else R("WV", 8, 24) if k == 15 else R("WV", 0, 16)) for k in range(16)]
+                 + [(R(bank, 248 + 8 * k, 256 + 8 * k), R(mn, k, 2048, 16), R("WV", 24, 32)) for k in range(1, 16)])
+            if PLAN["kn"] == "S":
+                act(R(kw, 8, 136), pA(h, 2), F.Sign, 0.5)
+            else:
+                ts(R(kw, 8, 136), pA(h, 2), -0.5, 0.5, A.is_gt, A.subtract)
+            stage[0] = ("kn1", t, h)
+            for e in (0, 1):
+                mm(R(bank, e, 256, 2, 72), R(kw, 64 * e, 64 * e + 72), M("IDB"))
+            lin(PLAN["k2"][h], R(k2, 0, 256, 1, 72), R(bank, 0, 256, 1, 72), 1.0, 0.0)
         for c in range(4):
+            whole = PLAN["kq"][h] == "H"
+            for q in () if PLAN["fd"] == "W" else ((0, 1) if c == 0 else ()) if whole else ((c // 2,) if c % 2 == 0 else ()):
+                stage[0] = ("kn%d" % q, t, h)
+                bank, o = ("pb%d" % (4 + 2 * h), 128 * q) if whole else ("pb%d" % (4 + 2 * h + q), 0)
+                for e in (0, 1):
+                    def blk(n, j):
+                        return R("WV", 144 * n + 64 - 8 * j, 144 * n + 136 - 8 * j)
+                    msum(R(bank, o + e, o + 128, 2, 72),
+                         [(blk(2, 8) if k == 0 else blk(3, 8) if k == 15 else blk(0, k - 8 * e), R(v, 16 + 1024 * q + k, 1040 + 1024 * q, 16)) for k in range(7 * e, 8 + 8 * e)]
+                         + [(blk(1, k - 8 * e), R(mn, 1024 * q + k, 1024 * q + 1024, 16)) for k in range(1 + 7 * e, 8 + 8 * e)])
+                if whole and q == 0:
+                    continue
+                o, i = (R(k2, 0, 256, 1, 72), R(bank, 0, 256, 1, 72)) if whole else (R(k2, 128 * q, 128 * q + 128, 1, 72), R(bank, 0, 128, 1, 72))
+                if PLAN["kn"] == "S":
+                    act(o, i, F.Sign, TB[:4] + (72,))
+                else:
+                    ts(o, i, TB[:4] + (72,), 0.5, A.is_gt, A.subtract)
+            stage[0] = ("z%d" % c, t, h)
             b = "pb%d" % (lane[0] % 2)
-            lane[0] += 1
+            if c == 2 and PLAN["fd"] == "W":
+                b = "pb%d" % (4 + 2 * h)
+            else:
+                lane[0] += 1
             for j in range(8):
                 mm(R(b, j, 512, 8), R("BK", 128 * j, 128 * j + 128, 1, 72), R(k2, 64 * c, 64 * c + 64, 1, 72))
             d0 = R(b, 0, 512)
@@ -400,124 +490,271 @@ def build(g, T, topo, core):
                 d0 = R(mk, 512 * c, 512 * c + 512)
             scan(R("ZZ", 2048 * h + 512 * c, 2048 * h + 512 * c + 512), d0, R(v, 16 + 512 * c, 528 + 512 * c), A.mult, A.max)
         stage[0] = ("count", t, h)
-        msum(pA(h, 2), marks("NBO", h))
-        msum(pA(h, 1), marks("TRI", h))
-        msum(pA(h, 3), marks("TRD", h))
+        msum(pB(h, 3), marks("NBO", h))
+        msum(pB(h, 2), marks("TRI", h))
+        msum(pB(h, 0), marks("TRD", h))
         sm = R("SM%d%d" % (t, h), 0, 128)
-        act(sm, pA(h, 2), F.Copy, 8.0, acc=R("AC", h, h + 1) if t < VISITS - 1 else None)
-        act(hb(h, CL), pA(h, 1), F.Copy, CB)
-        act(hb(h, S9), pA(h, 3), F.Sign, Q2)
+        act(sm, pB(h, 3), F.Copy, 8.0, acc=R("AC", h, h + 1) if t < VISITS - 1 else None)
+        nm = int(PLAN["nm"][h])
+        for j in range(nm):
+            c = j if h else nm - 1 - j
+            lin(PLAN["cl"][h], R("CW%d" % h, 128 * c, 128 * c + 128), pB(h, 2), 1.0, CBS[j])
+        if PLAN["s9"] == "S":
+            act(hb(h, S9), pB(h, 0), F.Sign, Q2)
+        else:
+            ts(hb(h, S9), pB(h, 0), Q2, 0.5, A.is_gt, A.subtract)
         dst, rid, pid = addr(-1)
         m = bits(topo.engines(core, dst)[:8])
         rm = "RM%d%d" % (t, h)
         snd = add("G", lambda: g.remote_dma(out_ap=T[rm][:], in_ap=ap(sm), remote_sem=T.sem["rm%d%d" % (t, h)], local_sem=T.sem["sent"], pid=pid, routing_id=rid, dma_engine_mask=m),
                   [sm], [], 1000.0, dma="sent", lat=NET)
         sends[0] += 8
-        for s in range(8):
-            ts(mask(h, s), hb(h, CL), 101 + s, None, A.is_equal)
-        stage[0] = ("names", t, h)
-        msum(pB(h, 1), [x[::-1] for x in marks("SH32", h)] + [(M("ON"), M("PAT"))])
-        msum(pB(h, 2), [x[::-1] for x in marks("SH", h)])
-        scan(hb(h, GG), pB(h, 1), M("C3"), A.add, A.max)
-        hold = R("pb3", 128 + 128 * h, 256 + 128 * h)
-        scan(hold, pB(h, 2), hf(h, NM), A.mult, A.max)
-        act(hf(h, KC), hb(h, GG), F.Copy, -360240.0 - 65534.0, 9776.0)
+        for s in range(0, 8, nm):
+            stage[0] = ("mask%d" % min(s, 1), t, h)
+            ts(mask(h, s, nm), R("CW%d" % h, 0, 128 * nm), 101 + s, None, A.is_equal)
+        stage[0] = ("run", t, h)
+        msum(pC(h, 2), [x[::-1] for x in marks("SH32", h)] + [(M("ON"), M("PAT"))])
+        msum(pC(h, 3), [x[::-1] for x in marks("SH", h)])
+        scan(hb(h, GG), pC(h, 2), M("C3"), A.add, A.max)
+        hold = pC(h, 1)
+        scan(hold, pC(h, 3), hf(h, NM), A.mult, A.max)
+        if PLAN["fu"] == "W":
+            lin(PLAN["kc"][h], hf(h, KC), hb(h, GG), 9776.0, -360240.0 - 65534.0)
+        else:
+            mm(pC(h, 2), hb(h, GG), M("IDB"))
+            lin(PLAN["kc"][h], hf(h, KC), pC(h, 2), 9776.0, -360240.0 - 65534.0)
+            lin(PLAN["gl"][h], hb(h, GL), pC(h, 2), 1.0, 0.0)
+        stage[0] = ("p1", t, h)
         if t == 0:
             tt(hi(h, A1), hold, hb(h, GG), A.mult)
         else:
             tt(hf(h, AG), hold, hb(h, GG), A.mult)
             ts(hi(h, A1), hf(h, AG), R("AF", t, t + 1), None, A.add)
         ts(hi(h, A2), hi(h, A1), 0x3FFC, None, A.bitwise_and)
-        ts(hold, hi(h, A2), 1024, 1, A.mult, A.add)
+        if PLAN["fu"] == "W":
+            ts(hold, hi(h, A2), 1024, 1, A.mult, A.add)
+        else:
+            ts(hf(h, PW), hi(h, A2), 1024, 1, A.mult, A.add)
+            mm(pC(h, 3), hf(h, PW), M("IDF"))
         return snd
 
     def places(t, h, snd):
         stage[0] = ("places", t, h)
         rm = "RM%d%d" % (t, h)
-        msum(pA(h, 0), marks("TRD", h) + [(M("I50"), hb(h, S9)), (M("IDB"), R(rm, 0, 128))], waits=[("rm%d%d" % (t, h), 8)], after=[snd])
-        act(hb(h, OV), pA(h, 0), F.Copy, CBD)
-        for j in range(4):
-            ts(mask(h, 8 + j), hb(h, OV), OVC[j], None, A.is_equal)
+        msum(pB(h, 2), marks("TRD", h) + [(M("I50"), hb(h, S9)), (M("IDB"), R(rm, 0, 128))], waits=[("rm%d%d" % (t, h), 8)], after=[snd])
+        no = int(PLAN["no"][h])
+        for j in range(no):
+            lin(PLAN["ov"][h], R("CW%d" % h, 512 + 128 * j, 640 + 128 * j), pB(h, 2), 1.0, CDS[j])
+        for j in range(0, 4, no):
+            ts(mask(h, 8 + j, no), R("CW%d" % h, 512, 512 + 128 * no), OVC[j], None, A.is_equal)
 
-    def middle(t, h):
-        stage[0] = ("middle", t, h)
-        u = pA(h, 1)
-        msum(u, [(M("N16"), M("WX"))] + [(R(u[0], u[1] + k, u[2], 16), R("ZZ", 2048 * h + k, 2048 * h + 2048, 16), R("WG", 0, 8)) for k in range(16)])
+    def middle(t, h, q):
+        stage[0] = ("u%d" % q, t, h)
+        if PLAN["fu"] == "W":
+            if q == 0:
+                names_h(t, h, q, (0, 128), pA(h, 1), pA(h, 0), pB(h, 1))
+        elif PLAN["uq"][h] == "Q":
+            names_h(t, h, q, (64 * q, 64 * q + 64), *[R("pb%d" % (4 + 2 * h + q), c, c + 64) for c in (128, 192, 256)])
+        elif q == 0:
+            names_h(t, h, q, (0, 128), pB(h, 1), pB(h, 0), pB(h, 2))
+        distances(t, h, q)
+
+    def names_h(t, h, q, w, u, sq, y):
+        z0 = 2048 * h + 16 * w[0]
+        word = PLAN["fu"] == "W"
+        if word:
+            msum(u, [(M("N16"), M("WX"))] + [(R(u[0], u[1] + k, u[2], 16), R("ZZ", z0 + k, z0 + 2048, 16), R("WV", 32, 40)) for k in range(16)])
+        else:
+            msum(u, [(win("ZU", k), R("ZZ", z0 + k, z0 + 16 * (w[1] - w[0]), 16)) for k in range(16)])
         if PLAN["um"][h] == "S":
-            act(hb(h, RU), u, F.Copy, 191.5 + 2.0 ** -13)
+            act(hb(h, RU, *w), u, F.Copy, RUB)
         else:
-            ts(hb(h, RU), u, 191.5 + 2.0 ** -13, None, A.add)
-        tt(hf(h, RY), u, hb(h, RU), A.subtract)
-        act(pA(h, 3), hf(h, RY), F.Square, 192.0 * 4096 + 592, 4096.0)
-        tt(hf(h, YY), pA(h, 3), hf(h, KC), A.add)
-        if PLAN["hm"][h] == "S":
-            act(hf(h, RY), hf(h, YY), F.Copy, 12582912.0, 2.0 ** -17)
-            act(hb(h, RQ), hf(h, RY), F.Copy, -12582912.0)
+            ts(hb(h, RU, *w), u, RUB, None, A.add)
+        tt(hf(h, RY, *w), u, hb(h, RU, *w), A.subtract)
+        if PLAN["hm"][h] == "J":
+            act(hf(h, FN, *w), hf(h, RY, *w), F.Square, SQB, 4096.0)
+            stage[0] = ("h%d" % q, t, h)
+            msum(y, [x[::-1] if word else x for x in ((M("IDF"), hf(h, KC, *w)), (M("IDF"), hf(h, FN, *w)))])
+            ts(hi(h, B1, *w), y, 65534, None, A.add)
+            ts(hi(h, B2, *w), hi(h, B1, *w), 5, 4095, A.logical_shift_right, A.bitwise_and)
+            cp(R("HU%d" % h, *w), hi(h, B2, *w))
+            stage[0] = ("y%d" % q, t, h)
+            tt(hf(h, YY, *w), hf(h, FN, *w), hf(h, KC, *w), A.add)
+            return
+        act(sq, hf(h, RY, *w), F.Square, SQB, 4096.0)
+        stage[0] = ("h%d" % q, t, h)
+        tt(hf(h, YY, *w), sq, hf(h, KC, *w), A.add)
+        hu = R("HU%d" % h, *w)
+        if PLAN["hm"][h] == "I":
+            if word:
+                mm(y, hf(h, YY), M("IDF"))
+            ts(hi(h, B1, *w), y if word else hf(h, YY, *w), 65534, None, A.add)
+            ts(hi(h, B2, *w), hi(h, B1, *w), 5, 4095, A.logical_shift_right, A.bitwise_and)
+            cp(hu, hi(h, B2, *w))
         else:
-            ts(hf(h, RY), hf(h, YY), 2.0 ** -17, 12582912.0, A.mult, A.add)
-            ts(hb(h, RQ), hf(h, RY), -12582912.0, None, A.add)
-        msum(pB(h, 0), [(hf(h, YY), M("IDF")), (hb(h, RQ), M("I17"))])
-        ts(R("HU%d" % h, 0, 128), pB(h, 0), 2.0 ** -5, (65534 - 15.5) / 32, A.mult, A.add)
-        for c in range(4):
+            if PLAN["hm"][h] == "S":
+                act(hf(h, RY, *w), hf(h, YY, *w), F.Copy, 12582912.0, 2.0 ** -17)
+                act(hb(h, RQ, *w), hf(h, RY, *w), F.Copy, -12582912.0)
+            else:
+                ts(hf(h, RY, *w), hf(h, YY, *w), 2.0 ** -17, 12582912.0, A.mult, A.add)
+                ts(hb(h, RQ, *w), hf(h, RY, *w), -12582912.0, None, A.add)
+            msum(y, [x[::-1] if word else x for x in ((M("IDF"), hf(h, YY, *w)), (M("I17"), hb(h, RQ, *w)))])
+            ts(hu, y, 2.0 ** -5, (65534 - 15.5) / 32, A.mult, A.add)
+
+    def distances(t, h, q):
+        for c in (2 * q, 2 * q + 1):
             a, b = 2048 * h + 512 * c, 2048 * h + 512 * c + 512
-            x = (XW, R("HU%d" % h, 32 * c, 32 * c + 32))
-            if PLAN["gh"][h][c] == "S":
+            x = (table(t), R("HU%d" % h, 32 * c, 32 * c + 32))
+            stage[0] = ("gh%d" % c, t, h)
+            if PLAN["hw"][h][q] == "W" and PLAN["gh"][h][2 * q:2 * q + 2] == "SS":
+                if c % 2 == 0:
+                    xh = R("XH%d" % h, 512 * c, 512 * c + 1024)
+                    act(xh, (table(t), R("HU%d" % h, 32 * c, 32 * c + 64)), F.Copy)
+                    stage[0] = ("df%d" % c, t, h)
+                    scan(R("XD", a, b + 512), xh, R("ZZ", a, b + 512), A.max, A.subtract)
+            elif PLAN["gh"][h][c] == "S":
                 xh = R("XH%d" % h, 512 * c, 512 * c + 512)
                 act(xh, x, F.Copy)
+                stage[0] = ("df%d" % c, t, h)
                 scan(R("XD", a, b), xh, R("ZZ", a, b), A.max, A.subtract)
+            elif PLAN["gh"][h][c] == "T":
+                act(R("XD", a, b), x, F.Copy)
+                pb = R("pb%d" % (lane[0] % 2), 0, 512)
+                lane[0] += 1
+                stage[0] = ("ab%d" % c, t, h)
+                msum(pb, [(M("NIB"), R("ZZ", a, b)), (M("IDB"), R("XD", a, b))])
+                act(R("AE%d" % h, 512 * c, 512 * c + 512), pb, F.Abs, 16.0)
+                continue
             else:
                 tt(R("XD", a, b), x, R("ZZ", a, b), A.subtract)
-            act(R("AE%d" % h, 512 * c, 512 * c + 512), R("XD", a, b), F.Abs, 16.0)
+            stage[0] = ("ab%d" % c, t, h)
+            if PLAN["aw"][h][q] == "N" or "T" in PLAN["gh"][h][2 * q:2 * q + 2]:
+                act(R("AE%d" % h, 512 * c, 512 * c + 512), R("XD", a, b), F.Abs, 16.0)
+            elif c % 2:
+                act(R("AE%d" % h, 512 * c - 512, 512 * c + 512), R("XD", a - 512, b), F.Abs, 16.0)
 
     def first(t):
-        stage[0] = ("first", t, 0)
+        stage[0] = ("fe", t, 1)
         fe, tg, uf, ac = [R("pb%d" % (j // 2), 16 * j, 16 + 16 * j) for j in range(4)]
-        msum(fe, [(win("ZK", k), R("M0", k, 256, 16)) for k in range(16)] + [(M("IDB"), R("BS", 0, 16))])
-        msum(tg, [(win("ZN", k), R("M0", k, 256, 16)) for k in range(16)] + [(M("IDB"), R("BS", 0, 16))])
-        cp(R("FE", 0, 16), fe)
-        act(R("ZF", 0, 256), (R("ZZ", 0, 4096), R("FE", 0, 16)), F.Copy, -32.0, 2.0)
+        msum(fe, [(win("ZK", k), R("MO", 896 + k, 1152, 16)) for k in range(16)])
+        ui, u, u15, at, y, hh = [R("UA", 16 * j, 16 * j + 16) for j in range(6)]
+        e0, kc, u1, sq, none, tg = [R("UF", 16 * j, 16 * j + 16) for j in range(6)]
+        tt(e0, fe, R("BS", 0, 16), A.add)
+        ts(none, fe, 1, JUNK, A.is_lt, A.mult)
+        if PLAN["early"]:
+            ts(kc, fe, 19552, -31 * 19552, A.mult, A.add)
+        ts(R("FE", 0, 16), e0, -32, None, A.add)
+        tt(tg, none, R("BS", 0, 16), A.add)
+        stage[0] = ("zf", t, 1)
+        act(R("ZF", 0, 256), (R("ZZ", 0, 4096), R("FE", 0, 16)), F.Copy, -16.0)
         msum(uf, [(win("ZW", k), R("ZF", k, 256, 16)) for k in range(16)])
-        cp(R("UA", 0, 16), uf)
-        ts(R("UA", 16, 32), R("UA", 0, 16), 1, 15, A.logical_shift_right, A.bitwise_and)
-        tt(R("UA", 32, 48), tg, R("UA", 16, 32), A.add)
-        ts(R("TG", 0, 16), R("UA", 32, 48), JUNK, None, A.add)
+        cp(ui, uf)
+        if PLAN["early"]:
+            ts(u, ui, 4095, None, A.bitwise_and)
+            ts(u1, u, 1184, None, A.add)
+            tt(sq, u1, u, A.mult)
+            tt(y, sq, kc, A.add)
+            ts(hh, y, 5, 4095, A.logical_shift_right, A.bitwise_and)
+            cp(R("HF", 0, 16), hh)
+        ts(u15, ui, 15, None, A.bitwise_and)
+        tt(at, tg, u15, A.add)
+        cp(R("TG", 16 * (t % 2), 16 * (t % 2) + 16), at)
         if t < VISITS - 1:
+            stage[0] = ("runs", t, 1)
             a1 = R(ac[0], ac[1], ac[1] + 1)
             msum(a1, [(M("O16"), R("AC", h, h + 1)) for h in (0, 1)])
             cp(R("AI", 0, 1), a1)
             ts(R("AI", 1, 2), R("AI", 0, 1), 1020, None, A.bitwise_and)
             cp(R("AF", t + 1, t + 2), R("AI", 1, 2))
+        if PLAN["early"]:
+            mean(t)
 
-    def write(t):
-        stage[0] = ("write", t, 0)
-        tt(R("SU", 0, 256), (R("XD", 0, 4096), R("FE", 0, 16)), R("ZF", 0, 256), A.add)
-        ts(R("SV", 0, 256), R("SU", 0, 256), 0.5, 7.75, A.mult, A.add)
-        cp((R("X", 0, JUNK + 4096), R("TG", 0, 16)), R("SV", 0, 256))
+    def mean(t):
+        stage[0] = ("wr", t, 1)
+        if PLAN["early"]:
+            mm(R("pb1", 256, 512), M("IH"), R("ZF", 0, 256))
+            act(R("SU", 0, 256), (table(t), R("HF", 0, 16)), F.Copy, -0.25, 0.5)
+        else:
+            kind = [x == "T" for x in "".join(PLAN["gh"])]
+            cut = [c for c in range(9) if c in (0, 8) or kind[c] != kind[c - 1]]
+            for c0, c1 in zip(cut, cut[1:]):
+                mm(R("pb1", 256 + 32 * c0, 256 + 32 * c1), M("IH" if kind[c0] else "IDB"), R("ZF", 32 * c0, 32 * c1))
+                act(R("SU", 32 * c0, 32 * c1), (R("XD", 0, 4096), R("FE", 2 * c0, 2 * c1)), F.Copy, -0.25 if kind[c0] else 7.75, 0.5)
+        tt(R("SV", 256 * (t % 2), 256 * (t % 2) + 256), R("pb1", 256, 512), R("SU", 0, 256), A.add)
+        if NX == 2:
+            write(t, t + 1)
+
+    def write(t, to):
+        cp((R("X%d" % (to % NX), 0, JUNK + 4096), R("TG", 16 * (t % 2), 16 * (t % 2) + 16)), R("SV", 256 * (t % 2), 256 * (t % 2) + 256))
+
+    def second(t, h, q):
+        stage[0] = ("d%d" % q, t, h)
+        if PLAN["fu"] == "W":
+            if q:
+                d = pA(h, 2)
+                msum(d, [(M("ON"), M("C512"))] + [(R(d[0], d[1] + k, d[2], 16), R("AE%d" % h, k, 2048, 16), R("WV", 40, 48)) for k in range(16)])
+                tt(d, d, hb(h, GG), A.mult)
+                tt(hi(h, B1), d, hf(h, YY), A.add)
+                ts(hi(h, B2), hi(h, B1), 5, 4095, A.arith_shift_right, A.bitwise_and)
+                tt(hf(h, PW), pC(h, 1), hi(h, B2), A.add)
+            return
+        w = (64 * q, 64 * q + 64)
+        d = R("pb%d" % (4 + 2 * h + q), 320, 384)
+        if PLAN["se"][h] == "H":
+            d = R("pb%d" % (4 + 2 * h), 256 + 64 * q, 320 + 64 * q)
+        msum(d, [(M("ON"), M("C512")[:2] + (M("C512")[1] + 64, 1, 128))] + [(win("Z32", k), R("AE%d" % h, 1024 * q + k, 1024 * q + 1024, 16)) for k in range(16)])
+        if PLAN["se"][h] == "H":
+            if q == 0:
+                return
+            d, w = pA(h, 2), (0, 128)
+        tt(d, d, hb(h, GL, *w), A.mult)
+        tt(hi(h, B1, *w), d, hf(h, YY, *w), A.add)
+        ts(hi(h, B2, *w), hi(h, B1, *w), 5, 4095, A.arith_shift_right, A.bitwise_and)
+        tt(hf(h, PL, *w) if PLAN["pl"][h] == "T" else R("pb%d" % (2 + h), 128 + w[0], 128 + w[1]), R("pb%d" % (2 + h), 384 + w[0], 384 + w[1]), hi(h, B2, *w), A.add)
 
     def back(t, h):
         stage[0] = ("back", t, h)
-        d = pB(h, 1)
-        msum(d, [(M("ON"), M("C512"))] + [(R(d[0], d[1] + k, d[2], 16), R("AE%d" % h, k, 2048, 16), R("SG32", 0, 8)) for k in range(16)])
-        tt(d, d, hb(h, GG), A.mult)
-        tt(hi(h, B1), d, hf(h, YY), A.add)
-        ts(hi(h, B2), hi(h, B1), 5, 4095, A.arith_shift_right, A.bitwise_and)
-        tt(hf(h, PW), R("pb3", 128 + 128 * h, 256 + 128 * h), hi(h, B2), A.add)
-        mm(pB(h, 2), hf(h, PW), M("IDF"))
-        act(hf(h, PL), pB(h, 2), F.Copy)
-        dup = R("pb2", 128 * h, 128 * h + 128)
-        mm(dup, M("DUP"), hf(h, PL))
+        np_ = int(PLAN["np"][h])
+        if PLAN["fu"] == "W":
+            twice = PLAN["pl"][h] == "T"
+            if twice:
+                mm(pA(h, 3), hf(h, PW), M("IDF"))
+            for j in range(np_):
+                mm(pC(h, 1 + j), hf(h, PW), M("IDF"))
+            lin(PLAN["pl"][h].replace("T", "S"), hf(h, PL), pA(h, 3) if twice else pC(h, 1), 1.0, 0.0)
+        elif PLAN["pl"][h] == "T":
+            for j in range(np_):
+                mm(pC(h, 1 + j), M("IDF"), hf(h, PL))
+        else:
+            lin(PLAN["pl"][h], hf(h, PL), pC(h, 1), 1.0, 0.0)
+            if np_ == 2:
+                lin(PLAN["pl"][h], pC(h, 2), pC(h, 1), 1.0, 0.0)
+        for j in range(np_):
+            mm(pA(h, j), M("DUP"), hf(h, PL))
         last = t == VISITS - 1
-        o = pA(h, 2)
+        o = pB(h, 3)
+        one = PLAN["sn"] == 1 and not last
+        gr = ("slots", t, h) if one else None
+        if one:
+            mm(R(o[0], o[1], o[1] + 64), M("ON"), R("CM", M("MON")[1], M("MON")[1] + 64), True, False, gr)
         for s in (list(range(8, 12)) + list(range(8)) if last else range(12)):
-            pr = R("PD%d" % h, 128 * s, 128 * s + 128)
-            tt(pr, pB(h, 2) if s < 8 else dup, mask(h, s), A.mult)
+            c = s if h or s >= 8 else 7 - s
+            pr = R("PD%d" % h, 128 * c, 128 * c + 128)
+            if s % np_ == 0:
+                c0 = c - c % np_
+                src = R("pb%d" % (2 + h), 128, 128 + 128 * np_) if s < 8 else R("pb%d" % (4 + 2 * h), 0, 128 * np_)
+                tt(R("PD%d" % h, 128 * c0, 128 * (c0 + np_)), src, mask(h, s, np_), A.mult)
             if s < 8:
-                mm(R(o[0], o[1] + s, o[1] + 64, 8), pr, R("SGF", 0, 8) if last else R("SGF", 7, 15))
+                mm(R(o[0], o[1] + s, o[1] + 64, 8), pr, R("SGF", 0, 8) if last else R("SGF", 7, 15), not one, not one, gr)
             else:
-                mm(R(o[0], o[1] + 56 + s, o[1] + 128, 4), pr, R("SGD", 0, 16) if last else R("SGD", 14, 30))
+                mm(R(o[0], o[1] + 56 + s, o[1] + 128, 4), pr, R("SGD", 0, 16) if last else R("SGD", 14, 30), not one, not one or s == 11, gr)
         sn = "SN%d%d" % (t, h)
-        act(R(sn, 0, 64), R(o[0], o[1], o[1] + 64), F.Copy, -1.0)
-        act(R(sn, 64, 128), R(o[0], o[1] + 64, o[1] + 128), F.Copy)
+        stage[0] = ("send", t, h)
+        if one:
+            lin(PLAN["sc"][h], R(sn, 0, 128), o, 1.0, 0.0)
+        else:
+            lin(PLAN["sc"][h], R(sn, 0, 64), R(o[0], o[1], o[1] + 64), 1.0, -1.0)
+            lin(PLAN["sc"][h], R(sn, 64, 128), R(o[0], o[1] + 64, o[1] + 128), 1.0, 0.0)
         ro, rv, rx = "RO%d%d" % (t, h), "RV%d%d" % (t, h), "rx%d%d" % (t, h)
         d1, r1, p1 = addr(1)
         d2, r2, p2 = addr(2)
@@ -540,6 +777,7 @@ def build(g, T, topo, core):
 
     def arrive(t, h):
         if t == 0:
+            stage[0] = ("load", 0, h)
             start_words(h)
         else:
             stage[0] = ("join", t, h)
@@ -549,17 +787,28 @@ def build(g, T, topo, core):
     for t in range(VISITS):
         arrive(t, 0)
         s0 = front(t, 0)
-        middle(t, 0)
-        places(t, 0, s0)
+        for q in (0, 1):
+            middle(t, 0, q)
         arrive(t, 1)
         s1 = front(t, 1)
+        for q in (0, 1):
+            second(t, 0, q)
+        places(t, 0, s0)
         arr[0] = back(t, 0)
         first(t)
-        middle(t, 1)
-        write(t)
+        for q in (0, 1):
+            middle(t, 1, q)
+        if not PLAN["early"]:
+            mean(t)
+        if t < VISITS - 1 or NX == 1:
+            stage[0] = ("wr2", t, 1)
+            write(t, t)
+        for q in (0, 1):
+            second(t, 1, q)
         places(t, 1, s1)
         arr[1] = back(t, 1)
-    add("Q", lambda: g.sync.dma_start(T.yx[:], ap(R("X", 0, 4096))), [R("X", 0, 4096)], [], 100.0, dma="dm10", lat=6000.0)
+    stage[0] = ("wr", VISITS - 1, 1)
+    add("Q", lambda: g.sync.dma_start(T.yx[:], ap(R("X%d" % (VISITS % NX), 0, 4096))), [R("X%d" % (VISITS % NX), 0, 4096)], [], 100.0, dma="dm10", lat=8000.0)
     for h in (0, 1):
         stage[0] = ("join", VISITS, h)
         q = "%d%d" % (VISITS - 1, h)
@@ -625,11 +874,12 @@ def schedule(ops):
         prio[i] = max([ops[i]["cost"] + (ops[i]["lat"] or 0.0)] + [prio[k] + lg for (k, lg) in succ[i]])
     for i in range(n):
         s = ops[i]["stage"]
-        prio[i] += PLAN["bias"].get("%s%d" % (s[0], s[2]), 0.0)
+        prio[i] += 1e6 if s[0] == "load" and ops[i]["eng"] != "S" else 100.0 * RANK[0].get("%s%d" % (s[0], s[2]), 0)
+    more = [1e6 if o["stage"][0] == "load" and o["eng"] != "S" else 100.0 * RANK[1].get("%s%d" % (o["stage"][0], o["stage"][2]), 0) for o in ops]
     best = now = _pass(ops, succ, prio, [0.0] * n)
     for _ in range(PLAN["turns"]):
         back = _pass(ops, pred, [now[1][i] + ops[i]["cost"] + (ops[i]["lat"] or 0.0) for i in range(n)], [o["lat"] or 0.0 for o in ops])
-        now = _pass(ops, succ, [back[1][i] + ops[i]["cost"] for i in range(n)], [0.0] * n)
+        now = _pass(ops, succ, [back[1][i] + ops[i]["cost"] + more[i] for i in range(n)], [0.0] * n)
         if now[2] < best[2]:
             best = now
     return best

from concourse.bass import DstId, RemoteDMATransfer
from concourse.mybir import dt, AluOpType, AxisListType, ActivationFunctionType

A = AluOpType
F = ActivationFunctionType
VISITS = 4
DEAD, JUNK = 4096, 4352
BF, F32, I32, U16 = "bfloat16", "float32", "int32", "uint16"
SCRATCH = {
    "X0": ("sbuf", [128, JUNK + 4096], BF), "X1": ("sbuf", [128, JUNK + 4096], BF),
    "ZZ": ("sbuf", [128, 4096], BF), "XD": ("sbuf", [128, 4096], BF), "MO": ("sbuf", [128, 128 * 24], BF),
    "WL": ("sbuf", [128, 256], I32), "WN": ("sbuf", [8, 256], I32), "WT": ("sbuf", [128, 1], I32), "TH": ("sbuf", [8, 1], I32),
    "WNB": ("sbuf", [8, 256], BF), "THM": ("sbuf", [8, 128], BF),
    "CI": ("sbuf", [128, 144], I32), "CG": ("sbuf", [128, 128], I32), "KI": ("sbuf", [128, 128], I32), "ONF": ("sbuf", [128, 128], F32),
    "PI": ("sbuf", [128, 8], I32), "KF": ("sbuf", [128, 40], F32),
    "EQ": ("sbuf", [128, 24], F32), "T2": ("sbuf", [128, 144], BF),
    "IDF": ("sbuf", [128, 128], F32), "DUP": ("sbuf", [128, 128], F32), "SGF": ("sbuf", [128, 16], F32), "SGD": ("sbuf", [128, 32], F32), "O16": ("sbuf", [128, 128], F32),
    "BK": ("sbuf", [128, 1024], BF), "SGB": ("sbuf", [128, 8], BF), "SGT": ("sbuf", [8, 128], BF),
    "BS": ("sbuf", [128, 16], BF), "FE": ("sbuf", [128, 16], U16), "HF": ("sbuf", [128, 16], U16), "TG": ("sbuf", [128, 32], U16),
    "UA": ("sbuf", [128, 96], I32), "UF": ("sbuf", [128, 96], F32),
    "ZF": ("sbuf", [128, 256], BF), "SU": ("sbuf", [128, 256], BF), "SV": ("sbuf", [128, 512], I32),
    "AI": ("sbuf", [128, 8], I32), "AF": ("sbuf", [128, 8], F32), "AC": ("sbuf", [128, 8], F32),
    "YL": ("sbuf", [128, 256], F32), "YN": ("sbuf", [8, 256], F32),
}
MATS = ("IDB", "WX", "N16", "IH", "NIB", "MON", "I17", "I50", "BO", "SAME", "PAT", "ON", "C3", "C512") + tuple(n + e for n in ("NBO", "SH", "SH32", "TRI", "TRD") for e in "EO")
SCRATCH["CM"] = ("sbuf", [128, 128 * len(MATS)], BF)
SCRATCH["WV"] = ("sbuf", [128, 4 * 144], BF)
for _n in ("ZO", "ZW", "ZK", "ZN", "ZU", "Z32"):
    SCRATCH[_n] = ("sbuf", [128, 144], BF)
for _h in (0, 1):
    SCRATCH["K2%d" % _h] = ("sbuf", [128, 256], BF)
    SCRATCH["KW%d" % _h] = ("sbuf", [128, 136], BF)
    SCRATCH["V%d" % _h] = ("sbuf", [128, 2064], BF)
    for _n in ("MN", "MK", "AE", "XH"):
        SCRATCH["%s%d" % (_n, _h)] = ("sbuf", [128, 2048], BF)
    SCRATCH["CW%d" % _h] = ("sbuf", [128, 128 * 8], BF)
    SCRATCH["PD%d" % _h] = ("sbuf", [128, 128 * 12], F32)
    SCRATCH["OF%d" % _h] = ("sbuf", [128, 128], U16)
    SCRATCH["HU%d" % _h] = ("sbuf", [128, 128], U16)
    SCRATCH["HB%d" % _h] = ("sbuf", [128, 128 * 8], BF)
    SCRATCH["HF%d" % _h] = ("sbuf", [128, 128 * 8], F32)
    SCRATCH["HI%d" % _h] = ("sbuf", [128, 128 * 8], I32)
for _t in range(VISITS):
    for _h in (0, 1):
        SCRATCH["SN%d%d" % (_t, _h)] = ("sbuf", [128, 128], F32)
        SCRATCH["SM%d%d" % (_t, _h)] = ("sbuf", [128, 128], BF)
        SCRATCH["RO%d%d" % (_t, _h)] = ("sbuf", [128, 64], F32)
        SCRATCH["RV%d%d" % (_t, _h)] = ("sbuf", [128, 64], F32)
        SCRATCH["RM%d%d" % (_t, _h)] = ("sbuf", [128, 128], BF)
for _b in range(8):
    SCRATCH["pb%d" % _b] = ("psum", [128, 512], F32)
ENGS = "VSTG"
SEMAPHORES = ["e" + e for e in ENGS] + ["sent"] + ["rx%d%d" % (t, h) for t in range(VISITS) for h in (0, 1)] \
    + ["rm%d%d" % (t, h) for t in range(VISITS) for h in (0, 1)] + ["dm%d" % i for i in range(12)]

CYC, FIX, SFIX, TFIX, GAT, SCA, PE, HOP, OWN, NET = 0.83, 12.0, 45.0, 6.0, 1.6, 3.8, 0.42, 200.0, 200.0, 3000.0
PLAN = {"gv": ("VSSS", "VSSS"), "gh": ("VSVT", "VSVV"), "mk": ("PPSP", "PPPP"), "um": "VS", "hm": "SS", "se": "QH", "mw": ("NN", "NN"), "aw": ("WN", "NN"),
        "vw": ("WW", "WW"), "hw": ("WW", "WW"), "kq": "QQ", "uq": "QQ", "kn": "V", "s9": "V", "cl": "VV", "kc": "VV", "gl": "VV", "ov": "VV", "pl": "TT", "sc": "VV",
        "fd": "W", "fu": "W", "k2": "SS", "aff": 0, "nm": "11", "no": "11", "np": "22", "wait": 30.0, "tables": 1, "early": 0, "sn": 1, "turns": 1}
RANK = ({'kn00': 51, 'mn01': 17, 'zf1': 11, 'mn10': -43, 'z30': 34, 'gh11': -25, 'places1': 21, 'h10': 22, 'mask11': -1, 'df31': 28, 'count1': -31, 'ab20': -21, 'mask01': -40, 'count0': 17, 'gh10': -18, 'mn30': -80, 'gh31': -21, 'join1': 22, 'z00': 1, 'ab31': -45, 'mn20': 17, 'df00': 44, 'z20': 45, 'd00': -18, 'mn21': -51, 'gh00': 79, 'h00': -22, 'mask10': 81, 'z11': -40, 'mn00': -17, 'z10': 12, 'run1': -17, 'back0': 5, 'df11': -14, 'gh21': 15, 'send1': -38, 'join0': 19, 'u10': -6, 'kn11': -4, 'ab00': 78, 'p11': 11, 'u00': 9, 'back1': 1, 'ab10': 33, 'd01': 31, 'df30': -10, 'df10': 19, 'ab11': 11, 'kn10': 13, 'gh30': 13, 'gv20': 13, 'gv01': -24, 'df21': -49, 'u11': 1, 'mn11': -20, 'wr21': -34, 'df01': 1, 'gv30': -28, 'ab21': 15, 'fe1': 3, 'runs1': 31, 'gv11': 56, 'z21': 13, 'ab30': 11, 'gv00': -7, 'ab01': 20, 'h11': -22, 'run0': -27, 'wr1': -49, 'gv10': 37, 'places0': 3, 'gh01': 3, 'df20': -14, 'z31': 1, 'kn01': 1, 'gv21': 1, 'send0': -26, 'z01': -2, 'h01': -6},
        {'count1': -4, 'gh21': -14, 'join0': -12, 'mn10': -6, 'mn11': -5, 'gv30': -21, 'gh01': -39, 'places1': -3, 'count0': -5, 'ab00': 23, 'gv11': -7, 'h10': 7, 'mask11': 2, 'd00': -5, 'kn00': 4, 'gv20': 1, 'df20': 5, 'z20': -5, 'send1': -10, 'z11': 9, 'h11': 27, 'mn00': 8, 'gh31': 1, 'kn01': 7, 'df30': 34, 'gv10': -34, 'kn10': -6, 'mn01': -5, 'z31': 26, 'u10': 6, 'ab11': -14, 'z00': 2, 'df01': -3, 'ab01': 2, 'mask00': -29, 'gh30': 1, 'df00': -7, 'mn21': -9, 'send0': 7, 'z01': 19, 'z30': -4, 'mask10': -3, 'ab10': -14, 'fe1': -5, 'gh00': 5, 'zf1': -8, 'u00': -11, 'run0': -13, 'p11': 8, 'mn30': -8, 'u11': -9, 'gh10': -5, 'z21': 13, 'gh11': -15, 'back1': 3, 'mn20': -5, 'ab20': -10, 'wr21': -4, 'ab30': 4, 'gv00': -5, 'df11': -6, 'd01': -21, 'z10': -9, 'gv01': -14, 'd10': -7, 'run1': -5, 'gv31': 3, 'places0': 16, 'mask01': 8, 'kn11': 8, 'mn31': 8, 'df31': -3, 'p10': -17, 'ab21': 5, 'u01': 10, 'ab31': 15, 'runs1': -4, 'df21': -5, 'gh20': 3, 'join1': -8})


PLAN.update({'aff': 16, 'kn': 'S', 's9': 'S', 'gv': ('VSSV', 'VSSS'), 'gh': ('VVST', 'SVVS'), 'mk': ('PPPP', 'PPPS'), 'um': 'VV', 'hm': 'II', 'se': 'QH', 'mw': ('NN', 'NW'), 'aw': ('NW', 'WW'), 'nm': '12', 'no': '12', 'np': '22', 'vw': ('WW', 'WW'), 'hw': ('WW', 'WW'), 'kq': 'QQ', 'uq': 'QQ', 'cl': 'SV', 'kc': 'SS', 'gl': 'VS', 'ov': 'SS', 'pl': 'TV', 'sc': 'SS'})
RANK = {'df31': -59, 'ab31': 37, 'gv00': 16, 'z00': 6, 'gv11': -46, 'ab11': 26, 'zf1': 33, 'back0': 6, 'mask00': 57, 'd00': -37, 'gh00': 12, 'runs1': 31, 'count1': 10, 'u01': -15, 'gh11': -9, 'back1': -18, 'df01': 53, 'mn20': -13, 'wr1': -9, 'mn21': 30, 'mn00': -32, 'join0': -22, 'mask10': -34, 'mn11': 23, 'z30': 18, 'places1': -15, 'kn11': -15, 'df30': 14, 'kn01': 29, 'gh01': -3, 'places0': -13, 'p11': 47, 'z21': -31, 'gh10': 20, 'z31': 6, 'send0': -60, 'p10': -2, 'kn00': 29, 'df10': -38, 'd11': 26, 'gh20': -18, 'gv01': -5, 'mn31': 9, 'h11': -18, 'mn10': 33, 'gh21': 15, 'ab10': 23, 'u11': -2, 'ab30': 2, 'mn30': -6, 'mask01': -4, 'load1': -33, 'z20': 30, 'df21': -22, 'df20': -5, 'join1': -12, 'mask11': 3, 'z01': 4},{'d00': 5, 'mn31': 2, 'back0': -16, 'join1': 8, 'z20': -7, 'ab10': -18, 'mn01': -4, 'u00': -1, 'gv11': -4, 'gv01': -23, 'u01': 1, 'df10': 2, 'wr21': -3, 'kn01': 12, 'mn30': 13, 'ab31': -2, 'z01': 6, 'gv00': -2, 'gv21': 16, 'mn11': -12, 'u11': -3, 'gh10': -7, 'mn20': -6, 'join0': -7, 'gv10': -2, 'count0': -5, 'df21': 3, 'gh21': 2, 'mask01': 4, 'mn21': 1, 'z00': 8, 'df01': -3, 'df30': 7, 'wr1': 2, 'p11': -12, 'gh01': 2, 'gh00': -1, 'd11': -3, 'z30': 3, 'h01': 8, 'd10': -5, 'u10': 18, 'mn00': 6, 'gv20': 5, 'gh20': -2, 'mask10': -6, 'z21': -12, 'df20': -4, 'df11': -20, 'd01': 5, 'gh30': -1, 'z10': -10, 'ab00': 18, 'back1': -4, 'places0': -4, 'df31': 5, 'gh31': -5, 'load0': 1, 'z31': 1, 'send1': 4, 'gh11': -12, 'ab30': -5}


PLAN.update({'aff': 1, 'gv': ('SVVS', 'SSSS'), 'gh': ('VTSV', 'VVSS'), 'mk': ('PPPP', 'SPPP'), 'um': 'VS', 'hm': 'SS', 'mw': ('NW', 'WW'), 'aw': ('NW', 'WW'), 'nm': '14', 'no': '12', 'np': '21', 'vw': ('NN', 'NW'), 'hw': ('WW', 'NN'), 'cl': 'VS', 'kc': 'VS', 'ov': 'SV', 'pl': 'VS', 'sc': 'VS', 'k2': 'VV'})
RANK = {'mn10': -31, 'df10': -91, 'ab30': 34, 'wr1': -23, 'p11': 48, 'wr21': 73, 'gh21': -85, 'gh10': 64, 'mn20': -45, 'gv01': -53, 'kn10': 112, 'load1': -16, 'df01': -32, 'join0': 6, 'df30': 36, 'd10': -35, 'kn01': -34, 'gv00': 100, 'load0': 23, 'send0': -13, 'mn11': -44, 'fe1': -72, 'z20': -50, 'count1': -38, 'count0': 28, 'gv11': 2, 'join1': -39, 'd11': 84, 'mn31': -26, 'gv30': -41, 'run0': 3, 'df20': -44, 'mn01': -54, 'runs1': -80, 'z00': 70, 'mask00': -84, 'places1': 70, 'df31': 63, 'gh01': 15, 'ab10': 42, 'gh20': 35, 'mask11': -75, 'h01': 76, 'zf1': 27, 'z31': -9, 'send1': 39, 'df21': 89, 'u01': 44, 'df11': 31, 'kn00': -10, 'z11': -10, 'gv20': 8, 'df00': -147, 'kn11': 64, 'h00': -48, 'z10': 147, 'back0': -33, 'mn30': 130, 'run1': 13, 'gh00': 40, 'z30': 62, 'ab11': 38, 'back1': -54, 'ab00': 7, 'ab31': -14, 'gh11': 23, 'mn00': 39, 'u00': 18, 'gv21': 14, 'z21': 22, 'mask10': -3, 'z01': -9, 'places0': 14, 'gv10': 35, 'gh30': -4, 'gh31': -7, 'mask01': 10},{'run0': -6, 'z11': -10, 'wr1': -26, 'mn30': 15, 'mn01': 28, 'mask11': 3, 'ab00': -1, 'p10': 29, 'mask00': -5, 'd10': 29, 'join1': -7, 'kn01': 2, 'load1': -11, 'df10': -11, 'z00': 6, 'wr21': -31, 'gh21': 14, 'z10': 6, 'back0': 29, 'df21': 23, 'df00': 4, 'h01': 20, 'gv30': 1, 'ab10': 20, 'gh10': 18, 'gv00': 11, 'z30': 8, 'gv11': -20, 'kn11': 24, 'mask10': 1, 'd11': 35, 'mn20': 9, 'df30': 11, 'df20': 3, 'mn10': -3, 'gh01': 21, 'ab11': -26, 'gv21': 18, 'places0': 1, 'ab31': -33, 'df01': 32, 'load0': 10, 'kn00': 41, 'kn10': 6, 'send0': 35, 'mask01': -39, 'ab30': -5, 'run1': -7, 'z20': 6, 'gh20': -15, 'send1': 46, 'fe1': -32, 'gv20': -7, 'z01': 6, 'count0': -2, 'places1': -13, 'mn00': 16, 'df31': 32, 'df11': 15, 'count1': -18, 'u01': 2, 'z31': 8, 'runs1': -44, 'gh00': -11, 'back1': 17, 'gv01': -16, 'join0': -11, 'h00': 4, 'z21': -17, 'gh11': 30, 'p11': 3, 'gh30': -31, 'gv10': -16, 'zf1': 17, 'gh31': -11, 'u00': 5, 'mn11': 12, 'mn31': -11}


PLAN.update({'fd': 'L', 'fu': 'L', 'gv': ('VSSS', 'VSVS'), 'gh': ('VSVS', 'VSVS'), 'mk': ('PPPP', 'PPPP'), 'um': 'VV', 'hm': 'II', 'mw': ('NN', 'NN'), 'aw': ('WN', 'NN'), 'nm': '21', 'no': '11', 'np': '11', 'vw': ('NN', 'NN'), 'hw': ('WN', 'WN'), 'cl': 'SS', 'kc': 'SV', 'ov': 'SS', 'pl': 'ST', 'sc': 'SS', 'k2': 'VS', 'se': 'HH', 'uq': 'QQ', 'gl': 'SS', 'kq': 'HQ'})
RANK = {'mn21': 42, 'mask11': 1, 'ab11': 16, 'join0': 42, 'gv30': -43, 'count1': 17, 'mn00': 6, 'gh31': 14, 'mn30': 3, 'df10': 14, 'ab10': 23, 'mn20': 27, 'u11': 3, 'gh11': 11, 'mask00': 2, 'run1': 7, 'run0': 6, 'df31': 13, 'mask01': 20, 'h01': -4, 'join1': 5, 'z31': 8, 'z11': 17, 'z21': -23, 'places1': 23, 'z30': 36, 'gh00': 5, 'ab21': -20, 'd11': 21, 'gh01': 12, 'count0': 29, 'p10': 4, 'z10': 22, 'send0': -19, 'u01': -17, 'load0': -37, 'fe1': -31, 'df11': 39, 'df21': -5, 'gv11': -25, 'mask10': -6, 'df00': -8, 'gh30': 29, 'z00': 13, 'gv01': 30, 'd01': 13, 'runs1': 10, 'gh20': -6, 'h00': 1, 'kn01': 4, 'zf1': -8, 'kn10': 43, 'wr1': 44, 'gh10': -3, 'gv00': -22, 'h10': 31, 'df20': -2, 'ab31': 9, 'kn00': -3, 'z20': 1, 'ab00': -14, 'send1': -3, 'gv21': 18, 'h11': -3, 'mn31': -21, 'wr21': 35, 'gh21': 47, 'ab01': -7, 'df01': 38, 'gv20': 5, 'gv31': 10, 'mn10': -20, 'd00': 5, 'mn11': -15},{'kn00': 22, 'ab10': 9, 'mask01': -10, 'p11': 2, 'df21': 5, 'kn11': -10, 'count0': 6, 'df30': -14, 'join1': 14, 'mn21': -1, 'kn01': -10, 'wr21': -14, 'df31': 4, 'df10': -5, 'mn00': -14, 'u00': 4, 'gv11': -18, 'places0': -25, 'kn10': 2, 'run0': -2, 'gv20': 5, 'ab31': -3, 'ab20': -1, 'h10': -2, 'gv30': -9, 'count1': -3, 'load1': -1, 'df00': -4, 'gh30': -1, 'df01': 2, 'z00': -6, 'z11': 6, 'gv01': 10, 'z01': -6, 'ab00': 6, 'gh31': -3, 'zf1': -11, 'mn01': 2, 'ab11': 6, 'u11': -2, 'gv21': 1, 'mask00': 6, 'send0': -23, 'gh10': 3, 'wr1': -16, 'runs1': 13, 'gh11': 4, 'ab21': -2, 'ab01': -14, 'u01': 1, 'd10': 2, 'z20': 3, 'gh21': 2, 'mn10': -3, 'fe1': 13, 'h01': 10, 'mn31': -9, 'gv00': -4, 'h11': 4, 'join0': 7, 'mn11': -4, 'df20': -7, 'mask11': -21, 'mn20': 4, 'places1': -11, 'd01': 7, 'h00': 2, 'z30': 1, 'gh01': 8, 'send1': 17, 'p10': -1, 'mask10': 1, 'load0': 4}


TFIX = 12.0
PLAN.update({'fd': 'W', 'fu': 'W', 'early': 1, 'gv': ('VSVS', 'VSSS'), 'gh': ('VTVS', 'VSVS'), 'mk': ('PPPP', 'PPPP'), 'um': 'VV', 'hm': 'JJ', 'mw': ('NW', 'WN'), 'aw': ('NN', 'NN'), 'nm': '12', 'no': '24', 'np': '11', 'vw': ('NN', 'WN'), 'hw': ('WN', 'WN'), 'cl': 'SS', 'kc': 'VS', 'ov': 'SS', 'pl': 'VS', 'sc': 'SV', 'k2': 'SV'})
RANK = {'send0': -71, 'df20': -22, 'runs1': -47, 'gv01': -5, 'h01': -60, 'h00': 16, 'df30': -38, 'ab30': -9, 'mask11': 26, 'wr21': 70, 'mn20': -21, 'ab01': -34, 'mn21': -73, 'mn01': 62, 'y01': -19, 'ab00': -19, 'gh20': 104, 'mask00': -9, 'send1': -8, 'join0': -24, 'z21': 13, 'gh11': 57, 'gh30': -2, 'df10': -17, 'p10': 7, 'kn11': 19, 'join1': -9, 'z10': 2, 'gh10': 14, 'd11': -16, 'p11': -65, 'u01': 12, 'fe1': -7, 'load1': 76, 'zf1': -20, 'mn30': -52, 'mn11': -17, 'gh31': 2, 'kn01': -7, 'z11': 55, 'u00': -28, 'ab31': 29, 'gh00': 10, 'df01': 9, 'z30': 44, 'mask10': -13, 'mn00': -37, 'df31': 13, 'df11': 42, 'places0': 6, 'gv21': -70, 'df00': 12, 'count1': 10, 'd10': -27, 'gv20': -5, 'gv11': -20, 'count0': -5, 'z31': 34, 'mn31': 12, 'mn10': 12, 'ab11': 2, 'gv30': -13, 'gv10': -57, 'kn10': -9, 'back1': 20, 'mask01': -14, 'z01': 54, 'gh01': -23, 'gh21': 10, 'places1': -36, 'ab20': 1, 'z00': 16, 'kn00': -37, 'gv00': 28, 'ab10': 11, 'df21': -22, 'run0': -1, 'load0': 14, 'y00': 25, 'z20': -12, 'back0': -16, 'ab21': 23, 'wr1': -29, 'run1': -5},{'kn11': -8, 'ab31': 15, 'kn00': -16, 'df10': 7, 'gh10': 10, 'mask01': 1, 'mn11': -14, 'h01': 5, 'gh20': 2, 'ab30': -10, 'z11': 24, 'df01': 36, 'gv00': 9, 'mn10': 17, 'gv30': -7, 'gv11': 15, 'gv01': 1, 'load1': 28, 'y01': 1, 'gh01': 29, 'p10': -1, 'gv10': -11, 'ab21': -29, 'p11': -11, 'z20': -7, 'ab01': -17, 'ab00': 26, 'mn20': -3, 'join0': 4, 'places1': -3, 'join1': 17, 'df30': 16, 'ab20': -1, 'mn01': 10, 'wr21': 21, 'send0': 5, 'df31': 16, 'count0': -17, 'gv31': -10, 'z10': -7, 'gh21': 15, 'gh11': -9, 'gh30': 3, 'df20': -5, 'mn30': -2, 'u00': 17, 'gv21': 11, 'gh31': -13, 'z21': -9, 'wr1': -20, 'df21': 18, 'gh00': -13, 'mn00': 20, 'ab10': -3, 'count1': -11, 'z31': -7, 'mask11': 2, 'runs1': 12, 'load0': 12, 'send1': -6, 'back0': -10, 'back1': 1, 'ab11': 1, 'df00': 2, 'places0': 2, 'h00': -3, 'y00': -10, 'mask00': -4, 'z00': 9, 'z30': -3, 'd11': -9, 'df11': 4, 'gv20': 6, 'mn31': -17, 'kn01': -12, 'zf1': 1, 'run1': 3, 'mask10': 2, 'z01': -7, 'mn21': 1, 'run0': -7, 'd10': 2}


def R(b, c0, c1, step=1, p=128):
    return (b, c0, c1, step, p)


def _n(r):
    return (r[2] - r[1] + r[3] - 1) // r[3]


def _over(a, b):
    if a[2] <= b[1] or b[2] <= a[1]:
        return False
    if a[3] == b[3] and a[3] > 1 and (a[1] - b[1]) % a[3]:
        return False
    return True


def _wide(b):
    return 4 if SCRATCH[b][2] in (F32, I32) else 2


def build(g, T, topo, core):
    ops = []
    hist = {}
    banks = {}
    ndma = [0]
    stage = [("load", 0, 0)]
    blast = {}
    glast = {}

    def ap(r):
        if r is None or isinstance(r, (int, float)):
            return r
        if len(r) == 2:
            w, o = r
            if o is None:
                return T[w][:]
            return ap(w).indirect(ap(o))
        b, c0, c1, st, p = r
        full = T[b].shape[1]
        if st == 1:
            return T[b][0:p, c0:c1]
        return T[b][0:p, c0:min(c1, full):st]

    def regs(r):
        if r is None or isinstance(r, (int, float)):
            return []
        if len(r) == 2:
            return [] if r[1] is None else [r[0], r[1]]
        return [r] if r[0] in SCRATCH else []

    def add(eng, fn, reads, writes, cost, grp=None, dma=False, waits=(), after=(), lat=None):
        i = len(ops)
        deps = {}

        def dep(j, hard):
            if j != i:
                deps[j] = deps.get(j, False) or hard
        for r in reads:
            for (q, j, w) in hist.get(r[0], ()):
                if w and _over(q, r) and not (grp is not None and ops[j]["grp"] == grp):
                    dep(j, True)
        for r in writes:
            for (q, j, w) in hist.get(r[0], ()):
                if _over(q, r) and not (grp is not None and ops[j]["grp"] == grp):
                    dep(j, True)
        for b in set(r[0] for r in list(reads) + list(writes) if r[0][:2] == "pb"):
            ph = banks.setdefault(b, [None, [], []])
            if ph[0] != eng:
                ph[2] = ph[1]
                ph[0], ph[1] = eng, []
            ph[1].append(i)
            for j in ph[2]:
                dep(j, True)
        if eng == "T":
            for b in set(r[0] for r in writes):
                if b in blast and ops[blast[b]]["grp"] != grp:
                    dep(blast[b], False)
                blast[b] = i
        if grp is not None:
            if grp in glast:
                dep(glast[grp], False)
            glast[grp] = i
        for j in after:
            dep(j, False)
        for r in writes:
            lst = hist.setdefault(r[0], [])
            if r[3] == 1:
                lst[:] = [e for e in lst if not (e[0][1] >= r[1] and e[0][2] <= r[2] and e[0][4] <= r[4])]
            lst.append((r, i, True))
        for r in reads:
            hist.setdefault(r[0], []).append((r, i, False))
        ops.append({"stage": stage[0], "eng": eng, "fn": fn, "deps": deps, "cost": cost, "grp": grp, "dma": dma, "waits": waits, "lat": lat, "after": after})
        return i

    def vcost(out, ins, two=False):
        n = max(_n(q) if len(q) == 5 else _n(out) for q in ins[:1] or [out])
        w = max(_wide(r[0]) for q in [out] + list(ins) for r in regs(q)[:1])
        ps = any(r[0][:2] == "pb" for q in ins for r in regs(q))
        f = (1 if ps else 2) if two else (0.5 if w == 2 else 1)
        if ins and len(ins[0]) == 2:
            f = GAT
        return FIX + CYC * max(64, n * f)

    def tt(out, a, b, op, **kw):
        return add("V", lambda: g.vector.tensor_tensor(ap(out), ap(a), ap(b), op), regs(a) + regs(b), regs(out), vcost(out, [a, b], True), **kw)

    def ts(out, a, s1, s2, op0, op1=None, **kw):
        if op1 is None:
            fn = lambda: g.vector.tensor_scalar(ap(out), ap(a), ap(s1), None, op0)
        else:
            fn = lambda: g.vector.tensor_scalar(ap(out), ap(a), ap(s1), ap(s2), op0, op1)
        return add("V", fn, regs(a) + regs(s1) + regs(s2), regs(out), vcost(out, [a]), **kw)

    def cp(out, a, **kw):
        if len(out) == 2:
            return add("V", lambda: g.vector.tensor_copy(ap(out), ap(a)), regs(a) + [out[1]], [out[0]], FIX + CYC * SCA * _n(a), **kw)
        return add("V", lambda: g.vector.tensor_copy(ap(out), ap(a)), regs(a), regs(out), vcost(out, [a]), **kw)

    def scan(out, d0, d1, op0, op1):
        return add("V", lambda: g.vector.tensor_tensor_scan(ap(out), ap(d0), ap(d1), 0.0, op0, op1), regs(d0) + regs(d1), regs(out), vcost(out, [d0, d1]))

    def ms(out, val):
        return add("V", lambda: g.vector.memset(ap(out), val), [], regs(out), vcost(out, []))

    def act(out, a, func, bias=0.0, scale=1.0, acc=None, **kw):
        n = _n(out) * (GAT if len(a) == 2 else 1)
        if func == F.Copy and not isinstance(bias, float):
            func = F.Identity
        if acc is None:
            fn = lambda: g.scalar.activation(ap(out), ap(a), func, bias=ap(bias), scale=ap(scale))
        else:
            fn = lambda: g.scalar.activation(ap(out), ap(a), func, bias=ap(bias), scale=ap(scale), accum_out=ap(acc))
        return add("S", fn, regs(a) + regs(bias) + regs(scale), regs(out) + regs(acc), SFIX + CYC * max(64, n), **kw)

    def lin(eng, out, a, scale, bias):
        if eng == "S":
            return act(out, a, F.Copy, bias, scale)
        return ts(out, a, scale, bias, A.mult, A.add)

    def mm(out, lhsT, rhs, start=True, stop=True, grp=None, **kw):
        f = 4 if SCRATCH[lhsT[0]][2] == F32 else 1
        return add("T", lambda: g.tensor.matmul(ap(out), ap(lhsT), ap(rhs), start, stop), regs(lhsT) + regs(rhs), regs(out), TFIX + PE * f * max(64, _n(rhs)), grp=grp, **kw)

    def msum(out, terms, **kw):
        gr = ("sum", len(ops))
        for j, x in enumerate(terms):
            o, l, r = x if len(x) == 3 else (out,) + tuple(x)
            mm(o, l, r, j == 0, j == len(terms) - 1, gr, **(kw if j == len(terms) - 1 else {}))

    def dma(q, out, a, cost=2500.0):
        i = ndma[0]
        ndma[0] += 1
        eng = g.sync if q == "Q" else g.scalar
        return add(q, lambda: eng.dma_start(ap(out), ap(a)), regs(a), regs(out), 100.0, dma="dm%d" % i, lat=cost)

    def M(n):
        return R("CM", 128 * MATS.index(n), 128 * MATS.index(n) + 128) if n in MATS else R(n, 0, 128)

    def win(n, k):
        return R(n, 15 - k, 143 - k)

    small = [dma("Q", R("WT", 0, 1), ("wt", None), 4000.0), dma("S", R("WN", 0, 256, 1, 8), ("wn", None), 4000.0),
             dma("S", R("TH", 0, 1, 1, 8), ("th", None), 4000.0), dma("Q", R("WL", 0, 256), ("wl", None), 4000.0)]
    dma("Q", R("X0", 0, 4096), ("xv", None), 8000.0)
    ops[-1]["deps"].update({j: False for j in small})
    NX = PLAN["tables"]
    if NX == 2:
        add("Q", lambda: g.sync.dma_start(ap(R("X1", 0, 4096)), T.xv[:]), [R("X0", 0, 16)], [R("X1", 0, 4096)], 100.0, dma="dm11", lat=8000.0)
    def iota(out, pattern, base=0, mult=0):
        add("G", lambda: g.iota(ap(out), pattern, base, mult), [], [out], 150.0 + 2 * CYC * _n(out))

    def pick(out, a, pattern, op, fill, base):
        add("G", lambda: g.affine_select(ap(out), ap(a), pattern, op, fill, base, -1), [a], [out], 170.0 + 2 * CYC * _n(out))

    def aff(out, a, scale, bias=0.0):
        lin("S" if _n(out) > PLAN["aff"] else "V", out, a, float(scale) if isinstance(scale, int) else scale, float(bias) if isinstance(bias, int) else bias)
    PI, PGI, PKI, P8I, P7I, PCI = [R("PI", c, c + 1) for c in range(6)]
    PF, PG, KP, P8, P7, PC, T15, L16, WC, KO, CB, CBD, Q1, Q2, Q3, Q4, TB, RUB, SQB, WU = [R("KF", c, c + 1) for c in range(20)]
    OVC = [R("KF", 20 + j, 21 + j) for j in range(4)]
    C144, K7 = R("CI", 0, 144), R("HI1", 768, 896)
    iota(PI, [[1, 1]], 0, 1)
    iota(C144, [[1, 144]])
    iota(M("CG"), [[1, 8], [0, 16]])
    iota(K7, [[0, 16], [1, 8]])
    iota(M("KI"), [[0, 8], [1, 16]])
    MARK = 2 if PLAN["kn"] == "V" else 1
    ms(M("ONF"), 1.0)
    ms(R("AE0", 0, 1024), float(MARK))
    for h in (0, 1):
        ms(R("V%d" % h, 0, 16), 0.0)
    ms(M("ON"), 1.0)
    ts(PGI, PI, 4, None, A.logical_shift_right)
    ts(PKI, PI, 15, None, A.bitwise_and)
    ts(P8I, PI, 3, None, A.logical_shift_right)
    ts(P7I, PI, 7, None, A.bitwise_and)
    ts(PCI, PI, 3, 1, A.logical_shift_right, A.bitwise_and)
    cp(R("KF", 0, 6), R("PI", 0, 6))
    for n, f in (("C3", 3), ("C512", 512), ("O16", 0.25), ("MON", -1.0 / 128)):
        aff(M(n), M("ON"), f)
    aff(T15, PG, 16, 15)
    aff(L16, KP, 16)
    aff(KO, KP, 16384, -15 * 16384)
    CBS, CDS = [R("KF", 32 + j, 33 + j) for j in range(4)], [R("KF", 36 + j, 37 + j) for j in range(4)]
    for j in range(max(int(x) for x in PLAN["nm"])):
        aff(CBS[j], KP, 0.5, 50.5 - j)
    for j in range(max(int(x) for x in PLAN["no"])):
        aff(CDS[j], P7, 0.5, 54.5 - j)
    aff(Q2, P7, *((-0.5, 54) if PLAN["s9"] == "V" else (0.5, -54)))
    for j in range(4):
        aff(OVC[j], PC, 4, 159 + j)
    ts(R("EQ", 0, 16), R("CI", 0, 16), KP, None, A.is_equal)
    for n in ("X0", "X1")[:NX]:
        ts(R(n, DEAD, DEAD + 16), R("EQ", 0, 16), R("EQ", 0, 1), 255, A.mult, A.mult)
    ts(R("SGT", 0, 128, 1, 8), R("CG", 0, 128, 1, 8), R("KF", 0, 1, 1, 8), None, A.is_equal)
    pick(M("IDF"), M("ONF"), [[1, 128]], A.is_equal, 0.0, 0)
    pick(R("BK", 0, 1024), R("AE0", 0, 1024), [[8, 8], [1, 8], [0, 16]], A.is_equal, 0.0, 0)
    aff(M("IDB"), M("IDF"), 1)
    ts(M("BO"), M("CG"), PG, None, A.is_equal)
    ts(R("ZO", 0, 144), C144, T15, None, A.is_equal)
    ts(R("SGB", 0, 8), R("CI", 0, 8), PG, None, A.is_equal)
    cp(R("WNB", 0, 256, 1, 8), R("WN", 0, 256, 1, 8))
    cp(WC, R("WT", 0, 1))
    aff(WU, WC, 2.0 ** -12)
    ts(Q4, PI, 8, -0.5, A.is_ge, A.mult)
    if PLAN["fd"] == "W":
        for c, f in ((0, -1), (8, -1), (16, R("EQ", 0, 1)), (24, 2)):
            aff(R("WV", c, c + 8), R("SGB", 0, 8), f)
        cp(Q3[:4] + (8,), R("TH", 0, 1, 1, 8))
        ts(R("THM", 0, 120, 1, 8), R(K7[0], K7[1], K7[1] + 120, 1, 8), R("KF", 0, 1, 1, 8), Q3[:4] + (8,), A.is_equal, A.mult)
        ts(R("THM", 120, 128, 1, 8), R(K7[0], K7[1], K7[1] + 8, 1, 8), R("KF", 0, 1, 1, 8), -100, A.is_equal, A.mult)
        for h in (0, 1):
            ms(R("KW%d" % h, 0, 8), 0.0)
    else:
        ms(R("WV", 0, 4 * 144), 0.0)
        for c, f in ((64, -1), (72, -1), (144 + 64, 2), (288, -16), (288 + 8, -1), (432 + 56, -1), (432 + 64, R("EQ", 0, 1))):
            aff(R("WV", c, c + 8), R("SGB", 0, 8), f)
        cp(R("T2", 128, 129, 1, 8), R("TH", 0, 1, 1, 8))
        ts(R("THM", 0, 128, 1, 8), K7[:4] + (8,), R("KF", 0, 1, 1, 8), None, A.is_equal)
        mm(R("pb0", 0, 1), R("THM", 0, 128, 1, 8), R("T2", 128, 129, 1, 8))
        ts(Q1, PI, 64, None, A.is_lt)
        aff(Q3, R("pb0", 0, 1), 1, 100)
        aff(TB, Q3, Q1, -99.5)
        if PLAN["kn"] == "V":
            aff(TB, TB, -1)
    if PLAN["fu"] == "W":
        aff(R("WV", 32, 40), R("SGB", 0, 8), WU)
        aff(R("WV", 40, 48), R("SGB", 0, 8), 32)
        aff(M("WX"), M("BO"), WU)
        aff(M("N16"), M("ON"), -16)
        RUB, SQB = 191.5 + 2.0 ** -13, 192.0 * 4096 + 592
    else:
        aff(R("T2", 130, 131), WC, 1)
        mm(R("pb0", 1, 2), M("BO"), R("T2", 130, 131))
        aff(RUB, R("pb0", 1, 2), -2.0 ** -8, 191.5 + 2.0 ** -13)
        aff(SQB, R("pb0", 1, 2), -16, 192 * 4096 + 592)
        for n, f in (("Z32", 32), ("ZU", WU)):
            aff(R(n, 0, 144), R("ZO", 0, 144), f)
    ts(M("SAME"), M("CG"), P7, MARK, A.is_equal, A.mult)
    aff(M("I17"), M("IDF"), -131072)
    aff(M("I50"), M("IDF"), 100 if PLAN["s9"] == "V" else 50)
    aff(M("NIB"), M("IDF"), -1)
    aff(M("IH"), M("IDF"), 0.5)
    ts(R("T2", 0, 128), M("KI"), 0, 0.25, A.is_gt, A.mult)
    aff(M("PAT"), R("T2", 0, 128), 1, -62 / 128)
    for e in (0, 1):
        x = "EO"[e]
        aff(M("NBO" + x), M("SAME"), -0.5 if e else Q4)
        pick(M("SH" + x), R("AE0", 0, 128), [[1, 8], [8, 16]], A.is_equal, 0.0, -64 * e)
        aff(M("SH32" + x), M("SH" + x), 32)
        for n, pattern, base in (("TRI", [[1, 8], [8, 16]], 8 - 64 * e), ("TRD", [[1, 8], [0, 2], [8, 8]], 72 - 64 * e)):
            pick(M(n + x), M("NBO" + x), pattern, A.is_ge, 0.0, base)
            pick(M(n + x), M(n + x), pattern, A.not_equal, -50.5 * MARK, base)
    pick(M("DUP"), M("ONF"), [[16, 8], [0, 2], [1, 8]], A.is_equal, 0.0, 8)
    aff(CB, KP, 1, 32)
    for n, f in (("ZW", WC), ("ZK", CB)):
        aff(R(n, 0, 144), R("ZO", 0, 144), f)
    ts(R("SGF", 0, 16), R(K7[0], K7[1], K7[1] + 16), PG, None, A.is_equal)
    ts(R("SGD", 0, 32), R("KI", 0, 32), P8, None, A.is_equal)
    ts(R("BS", 0, 16), R("CI", 0, 16), 256, L16, A.mult, A.add)
    for h in (0, 1):
        ts(R("pb%d" % (2 + h), 0, 128), M("KI"), -16384, 15 * 16384, A.mult, A.add)

    def H(kind, h, s, c0=0, c1=128, step=1):
        return R("%s%d" % (kind, h), 128 * s + c0, 128 * s + c1, step)

    def hb(h, s, *a):
        return H("HB", h, s, *a)

    def hf(h, s, *a):
        return H("HF", h, s, *a)

    def hi(h, s, *a):
        return H("HI", h, s, *a)
    GL, GG, CL, S9, OV, RU, RQ, LV = range(8)
    NM, KC, YY, RY, AG, PW, PL, FN = range(8)
    JI, NMI, A1, A2, B1, B2 = range(6)

    def pA(h, r):
        return R("pb%d" % (4 + 2 * h), 128 * r, 128 * r + 128)

    def pB(h, r):
        return R("pb%d" % (5 + 2 * h), 128 * r, 128 * r + 128)

    def pC(h, r):
        return R("pb%d" % (2 + h), 128 * r, 128 * r + 128)
    rank = T.rank_of(core)
    sends = [0]
    lane = [0]

    def addr(d):
        dst = T.cores[(rank + d) % len(T.cores)]
        rid, pid, _s = topo.addr(dst)
        return dst, rid, pid

    def bits(engines):
        return sum(1 << e for e in engines)

    def start_words(h):
        mm(pA(h, 0), R("SGT", 0, 128, 1, 8), R("WNB", 128 * h, 128 * h + 128, 1, 8))
        ts(pA(h, 1), pA(h, 0), KP, 8192, A.is_le, A.mult)
        tt(hf(h, FN), pA(h, 1), R("WL", 128 * h, 128 * h + 128), A.add)
        ts(R("OF%d" % h, 0, 128), hf(h, FN), DEAD, None, A.min)
        mm(pB(h, 0), hf(h, FN), M("IDF"))
        act(hf(h, AG), pB(h, 0), F.Copy)
        tt(hf(h, NM), pC(h, 0), hf(h, AG), A.add)

    def join(h, own, ov, waits, after):
        tt(hi(h, JI, 0, 64), own, ov, A.add, waits=waits, after=after)
        ts(hi(h, NMI, 0, 128, 2), hi(h, JI, 0, 64), 12, 8191, A.logical_shift_right, A.bitwise_and)
        ts(hi(h, NMI, 1, 128, 2), hi(h, JI, 0, 64), (1 << 24) + 4095, None, A.bitwise_and)

    def offsets(h):
        tt(hf(h, NM), pC(h, 0), hi(h, NMI), A.add)
        mm(pC(h, 2), hf(h, NM), M("IDF"))
        ts(R("OF%d" % h, 0, 128), pC(h, 2), KO, DEAD, A.add, A.min)

    def tile(h, s):
        return 16 + 4 * h + s - 8 if s >= 8 else 8 + s if h else 7 - s

    def mask(h, s, n=1):
        a = min(tile(h, s), tile(h, s + n - 1))
        return R("MO", 128 * a, 128 * (a + n))

    def table(t):
        return R("X%d" % (t % NX), 0, DEAD + 16)

    def marks(n, h):
        return [(M(n + "EO"[e])[:4] + (64 + 8 * e,), R("K2%d" % h, e, 256, 2, 64 + 8 * e)) for e in (0, 1)]

    def front(t, h):
        v, mn, mk = "V%d" % h, "MN%d" % h, "MK%d" % h
        for c in range(4):
            stage[0] = ("gv%d" % c, t, h)
            o, i = R(v, 16 + 512 * c, 528 + 512 * c), (table(t), R("OF%d" % h, 32 * c, 32 * c + 32))
            if PLAN["gv"][h][c] == "V":
                ts(o, i, 16, None, A.add)
            elif PLAN["vw"][h][c // 2] == "N" or "V" in PLAN["gv"][h][c - c % 2:c - c % 2 + 2]:
                act(o, i, F.Copy, 16.0)
            elif c % 2 == 0:
                act(R(v, 16 + 512 * c, 1040 + 512 * c), (table(t), R("OF%d" % h, 32 * c, 32 * c + 64)), F.Copy, 16.0)
            stage[0] = ("mn%d" % c, t, h)
            if PLAN["mw"][h][c // 2] == "N":
                scan(R(mn, 512 * c, 512 * c + 512), R(v, 15 + 512 * c, 527 + 512 * c), o, A.max, A.min)
            elif c % 2:
                scan(R(mn, 512 * c - 512, 512 * c + 512), R(v, 512 * c - 497, 527 + 512 * c), R(v, 512 * c - 496, 528 + 512 * c), A.max, A.min)
        k2 = "K2%d" % h
        if PLAN["fd"] == "W":
            stage[0] = ("kn0", t, h)
            bank, kw = "pb%d" % (4 + 2 * h), "KW%d" % h
            msum(pA(h, 2), [(M("ON")[:4] + (8,), R("THM", 0, 128, 1, 8))]
                 + [(R(bank, 256 + 8 * max(k - 1, 0), 264 + 8 * k), R(v, 16 + k, 2064, 16), R("WV", 0, 8) if k == 0 else R("WV", 8, 24) if k == 15 else R("WV", 0, 16)) for k in range(16)]
                 + [(R(bank, 248 + 8 * k, 256 + 8 * k), R(mn, k, 2048, 16), R("WV", 24, 32)) for k in range(1, 16)])
            if PLAN["kn"] == "S":
                act(R(kw, 8, 136), pA(h, 2), F.Sign, 0.5)
            else:
                ts(R(kw, 8, 136), pA(h, 2), -0.5, 0.5, A.is_gt, A.subtract)
            stage[0] = ("kn1", t, h)
            for e in (0, 1):
                mm(R(bank, e, 256, 2, 72), R(kw, 64 * e, 64 * e + 72), M("IDB"))
            lin(PLAN["k2"][h], R(k2, 0, 256, 1, 72), R(bank, 0, 256, 1, 72), 1.0, 0.0)
        for c in range(4):
            whole = PLAN["kq"][h] == "H"
            for q in () if PLAN["fd"] == "W" else ((0, 1) if c == 0 else ()) if whole else ((c // 2,) if c % 2 == 0 else ()):
                stage[0] = ("kn%d" % q, t, h)
                bank, o = ("pb%d" % (4 + 2 * h), 128 * q) if whole else ("pb%d" % (4 + 2 * h + q), 0)
                for e in (0, 1):
                    def blk(n, j):
                        return R("WV", 144 * n + 64 - 8 * j, 144 * n + 136 - 8 * j)
                    msum(R(bank, o + e, o + 128, 2, 72),
                         [(blk(2, 8) if k == 0 else blk(3, 8) if k == 15 else blk(0, k - 8 * e), R(v, 16 + 1024 * q + k, 1040 + 1024 * q, 16)) for k in range(7 * e, 8 + 8 * e)]
                         + [(blk(1, k - 8 * e), R(mn, 1024 * q + k, 1024 * q + 1024, 16)) for k in range(1 + 7 * e, 8 + 8 * e)])
                if whole and q == 0:
                    continue
                o, i = (R(k2, 0, 256, 1, 72), R(bank, 0, 256, 1, 72)) if whole else (R(k2, 128 * q, 128 * q + 128, 1, 72), R(bank, 0, 128, 1, 72))
                if PLAN["kn"] == "S":
                    act(o, i, F.Sign, TB[:4] + (72,))
                else:
                    ts(o, i, TB[:4] + (72,), 0.5, A.is_gt, A.subtract)
            stage[0] = ("z%d" % c, t, h)
            b = "pb%d" % (lane[0] % 2)
            if c == 2 and PLAN["fd"] == "W":
                b = "pb%d" % (4 + 2 * h)
            else:
                lane[0] += 1
            for j in range(8):
                mm(R(b, j, 512, 8), R("BK", 128 * j, 128 * j + 128, 1, 72), R(k2, 64 * c, 64 * c + 64, 1, 72))
            d0 = R(b, 0, 512)
            if PLAN["mk"][h][c] == "S":
                act(R(mk, 512 * c, 512 * c + 512), d0, F.Copy)
                d0 = R(mk, 512 * c, 512 * c + 512)
            scan(R("ZZ", 2048 * h + 512 * c, 2048 * h + 512 * c + 512), d0, R(v, 16 + 512 * c, 528 + 512 * c), A.mult, A.max)
        stage[0] = ("count", t, h)
        msum(pB(h, 3), marks("NBO", h))
        msum(pB(h, 2), marks("TRI", h))
        msum(pB(h, 0), marks("TRD", h))
        sm = R("SM%d%d" % (t, h), 0, 128)
        act(sm, pB(h, 3), F.Copy, 8.0, acc=R("AC", h, h + 1) if t < VISITS - 1 else None)
        nm = int(PLAN["nm"][h])
        for j in range(nm):
            c = j if h else nm - 1 - j
            lin(PLAN["cl"][h], R("CW%d" % h, 128 * c, 128 * c + 128), pB(h, 2), 1.0, CBS[j])
        if PLAN["s9"] == "S":
            act(hb(h, S9), pB(h, 0), F.Sign, Q2)
        else:
            ts(hb(h, S9), pB(h, 0), Q2, 0.5, A.is_gt, A.subtract)
        dst, rid, pid = addr(-1)
        m = bits(topo.engines(core, dst)[:8])
        rm = "RM%d%d" % (t, h)
        snd = add("G", lambda: g.remote_dma(out_ap=T[rm][:], in_ap=ap(sm), remote_sem=T.sem["rm%d%d" % (t, h)], local_sem=T.sem["sent"], pid=pid, routing_id=rid, dma_engine_mask=m),
                  [sm], [], 1000.0, dma="sent", lat=NET)
        sends[0] += 8
        for s in range(0, 8, nm):
            stage[0] = ("mask%d" % min(s, 1), t, h)
            ts(mask(h, s, nm), R("CW%d" % h, 0, 128 * nm), 101 + s, None, A.is_equal)
        stage[0] = ("run", t, h)
        msum(pC(h, 2), [x[::-1] for x in marks("SH32", h)] + [(M("ON"), M("PAT"))])
        msum(pC(h, 3), [x[::-1] for x in marks("SH", h)])
        scan(hb(h, GG), pC(h, 2), M("C3"), A.add, A.max)
        hold = pC(h, 1)
        scan(hold, pC(h, 3), hf(h, NM), A.mult, A.max)
        if PLAN["fu"] == "W":
            lin(PLAN["kc"][h], hf(h, KC), hb(h, GG), 9776.0, -360240.0 - 65534.0)
        else:
            mm(pC(h, 2), hb(h, GG), M("IDB"))
            lin(PLAN["kc"][h], hf(h, KC), pC(h, 2), 9776.0, -360240.0 - 65534.0)
            lin(PLAN["gl"][h], hb(h, GL), pC(h, 2), 1.0, 0.0)
        stage[0] = ("p1", t, h)
        if t == 0:
            tt(hi(h, A1), hold, hb(h, GG), A.mult)
        else:
            tt(hf(h, AG), hold, hb(h, GG), A.mult)
            ts(hi(h, A1), hf(h, AG), R("AF", t, t + 1), None, A.add)
        ts(hi(h, A2), hi(h, A1), 0x3FFC, None, A.bitwise_and)
        if PLAN["fu"] == "W":
            ts(hold, hi(h, A2), 1024, 1, A.mult, A.add)
        else:
            ts(hf(h, PW), hi(h, A2), 1024, 1, A.mult, A.add)
            mm(pC(h, 3), hf(h, PW), M("IDF"))
        return snd

    def places(t, h, snd):
        stage[0] = ("places", t, h)
        rm = "RM%d%d" % (t, h)
        msum(pB(h, 2), marks("TRD", h) + [(M("I50"), hb(h, S9)), (M("IDB"), R(rm, 0, 128))], waits=[("rm%d%d" % (t, h), 8)], after=[snd])
        no = int(PLAN["no"][h])
        for j in range(no):
            lin(PLAN["ov"][h], R("CW%d" % h, 512 + 128 * j, 640 + 128 * j), pB(h, 2), 1.0, CDS[j])
        for j in range(0, 4, no):
            ts(mask(h, 8 + j, no), R("CW%d" % h, 512, 512 + 128 * no), OVC[j], None, A.is_equal)

    def middle(t, h, q):
        stage[0] = ("u%d" % q, t, h)
        if PLAN["fu"] == "W":
            if q == 0:
                names_h(t, h, q, (0, 128), pA(h, 1), pA(h, 0), pB(h, 1))
        elif PLAN["uq"][h] == "Q":
            names_h(t, h, q, (64 * q, 64 * q + 64), *[R("pb%d" % (4 + 2 * h + q), c, c + 64) for c in (128, 192, 256)])
        elif q == 0:
            names_h(t, h, q, (0, 128), pB(h, 1), pB(h, 0), pB(h, 2))
        distances(t, h, q)

    def names_h(t, h, q, w, u, sq, y):
        z0 = 2048 * h + 16 * w[0]
        word = PLAN["fu"] == "W"
        if word:
            msum(u, [(M("N16"), M("WX"))] + [(R(u[0], u[1] + k, u[2], 16), R("ZZ", z0 + k, z0 + 2048, 16), R("WV", 32, 40)) for k in range(16)])
        else:
            msum(u, [(win("ZU", k), R("ZZ", z0 + k, z0 + 16 * (w[1] - w[0]), 16)) for k in range(16)])
        if PLAN["um"][h] == "S":
            act(hb(h, RU, *w), u, F.Copy, RUB)
        else:
            ts(hb(h, RU, *w), u, RUB, None, A.add)
        tt(hf(h, RY, *w), u, hb(h, RU, *w), A.subtract)
        if PLAN["hm"][h] == "J":
            act(hf(h, FN, *w), hf(h, RY, *w), F.Square, SQB, 4096.0)
            stage[0] = ("h%d" % q, t, h)
            msum(y, [x[::-1] if word else x for x in ((M("IDF"), hf(h, KC, *w)), (M("IDF"), hf(h, FN, *w)))])
            ts(hi(h, B1, *w), y, 65534, None, A.add)
            ts(hi(h, B2, *w), hi(h, B1, *w), 5, 4095, A.logical_shift_right, A.bitwise_and)
            cp(R("HU%d" % h, *w), hi(h, B2, *w))
            stage[0] = ("y%d" % q, t, h)
            tt(hf(h, YY, *w), hf(h, FN, *w), hf(h, KC, *w), A.add)
            return
        act(sq, hf(h, RY, *w), F.Square, SQB, 4096.0)
        stage[0] = ("h%d" % q, t, h)
        tt(hf(h, YY, *w), sq, hf(h, KC, *w), A.add)
        hu = R("HU%d" % h, *w)
        if PLAN["hm"][h] == "I":
            if word:
                mm(y, hf(h, YY), M("IDF"))
            ts(hi(h, B1, *w), y if word else hf(h, YY, *w), 65534, None, A.add)
            ts(hi(h, B2, *w), hi(h, B1, *w), 5, 4095, A.logical_shift_right, A.bitwise_and)
            cp(hu, hi(h, B2, *w))
        else:
            if PLAN["hm"][h] == "S":
                act(hf(h, RY, *w), hf(h, YY, *w), F.Copy, 12582912.0, 2.0 ** -17)
                act(hb(h, RQ, *w), hf(h, RY, *w), F.Copy, -12582912.0)
            else:
                ts(hf(h, RY, *w), hf(h, YY, *w), 2.0 ** -17, 12582912.0, A.mult, A.add)
                ts(hb(h, RQ, *w), hf(h, RY, *w), -12582912.0, None, A.add)
            msum(y, [x[::-1] if word else x for x in ((M("IDF"), hf(h, YY, *w)), (M("I17"), hb(h, RQ, *w)))])
            ts(hu, y, 2.0 ** -5, (65534 - 15.5) / 32, A.mult, A.add)

    def distances(t, h, q):
        for c in (2 * q, 2 * q + 1):
            a, b = 2048 * h + 512 * c, 2048 * h + 512 * c + 512
            x = (table(t), R("HU%d" % h, 32 * c, 32 * c + 32))
            stage[0] = ("gh%d" % c, t, h)
            if PLAN["hw"][h][q] == "W" and PLAN["gh"][h][2 * q:2 * q + 2] == "SS":
                if c % 2 == 0:
                    xh = R("XH%d" % h, 512 * c, 512 * c + 1024)
                    act(xh, (table(t), R("HU%d" % h, 32 * c, 32 * c + 64)), F.Copy)
                    stage[0] = ("df%d" % c, t, h)
                    scan(R("XD", a, b + 512), xh, R("ZZ", a, b + 512), A.max, A.subtract)
            elif PLAN["gh"][h][c] == "S":
                xh = R("XH%d" % h, 512 * c, 512 * c + 512)
                act(xh, x, F.Copy)
                stage[0] = ("df%d" % c, t, h)
                scan(R("XD", a, b), xh, R("ZZ", a, b), A.max, A.subtract)
            elif PLAN["gh"][h][c] == "T":
                act(R("XD", a, b), x, F.Copy)
                pb = R("pb%d" % (lane[0] % 2), 0, 512)
                lane[0] += 1
                stage[0] = ("ab%d" % c, t, h)
                msum(pb, [(M("NIB"), R("ZZ", a, b)), (M("IDB"), R("XD", a, b))])
                act(R("AE%d" % h, 512 * c, 512 * c + 512), pb, F.Abs, 16.0)
                continue
            else:
                tt(R("XD", a, b), x, R("ZZ", a, b), A.subtract)
            stage[0] = ("ab%d" % c, t, h)
            if PLAN["aw"][h][q] == "N" or "T" in PLAN["gh"][h][2 * q:2 * q + 2]:
                act(R("AE%d" % h, 512 * c, 512 * c + 512), R("XD", a, b), F.Abs, 16.0)
            elif c % 2:
                act(R("AE%d" % h, 512 * c - 512, 512 * c + 512), R("XD", a - 512, b), F.Abs, 16.0)

    def first(t):
        stage[0] = ("fe", t, 1)
        fe, tg, uf, ac = [R("pb%d" % (j // 2), 16 * j, 16 + 16 * j) for j in range(4)]
        msum(fe, [(win("ZK", k), R("MO", 896 + k, 1152, 16)) for k in range(16)])
        ui, u, u15, at, y, hh = [R("UA", 16 * j, 16 * j + 16) for j in range(6)]
        e0, kc, u1, sq, none, tg = [R("UF", 16 * j, 16 * j + 16) for j in range(6)]
        tt(e0, fe, R("BS", 0, 16), A.add)
        ts(none, fe, 1, JUNK, A.is_lt, A.mult)
        if PLAN["early"]:
            ts(kc, fe, 19552, -31 * 19552, A.mult, A.add)
        ts(R("FE", 0, 16), e0, -32, None, A.add)
        tt(tg, none, R("BS", 0, 16), A.add)
        stage[0] = ("zf", t, 1)
        act(R("ZF", 0, 256), (R("ZZ", 0, 4096), R("FE", 0, 16)), F.Copy, -16.0)
        msum(uf, [(win("ZW", k), R("ZF", k, 256, 16)) for k in range(16)])
        cp(ui, uf)
        if PLAN["early"]:
            ts(u, ui, 4095, None, A.bitwise_and)
            ts(u1, u, 1184, None, A.add)
            tt(sq, u1, u, A.mult)
            tt(y, sq, kc, A.add)
            ts(hh, y, 5, 4095, A.logical_shift_right, A.bitwise_and)
            cp(R("HF", 0, 16), hh)
        ts(u15, ui, 15, None, A.bitwise_and)
        tt(at, tg, u15, A.add)
        cp(R("TG", 16 * (t % 2), 16 * (t % 2) + 16), at)
        if t < VISITS - 1:
            stage[0] = ("runs", t, 1)
            a1 = R(ac[0], ac[1], ac[1] + 1)
            msum(a1, [(M("O16"), R("AC", h, h + 1)) for h in (0, 1)])
            cp(R("AI", 0, 1), a1)
            ts(R("AI", 1, 2), R("AI", 0, 1), 1020, None, A.bitwise_and)
            cp(R("AF", t + 1, t + 2), R("AI", 1, 2))
        if PLAN["early"]:
            mean(t)

    def mean(t):
        stage[0] = ("wr", t, 1)
        if PLAN["early"]:
            mm(R("pb1", 256, 512), M("IH"), R("ZF", 0, 256))
            act(R("SU", 0, 256), (table(t), R("HF", 0, 16)), F.Copy, -0.25, 0.5)
        else:
            kind = [x == "T" for x in "".join(PLAN["gh"])]
            cut = [c for c in range(9) if c in (0, 8) or kind[c] != kind[c - 1]]
            for c0, c1 in zip(cut, cut[1:]):
                mm(R("pb1", 256 + 32 * c0, 256 + 32 * c1), M("IH" if kind[c0] else "IDB"), R("ZF", 32 * c0, 32 * c1))
                act(R("SU", 32 * c0, 32 * c1), (R("XD", 0, 4096), R("FE", 2 * c0, 2 * c1)), F.Copy, -0.25 if kind[c0] else 7.75, 0.5)
        tt(R("SV", 256 * (t % 2), 256 * (t % 2) + 256), R("pb1", 256, 512), R("SU", 0, 256), A.add)
        if NX == 2:
            write(t, t + 1)

    def write(t, to):
        cp((R("X%d" % (to % NX), 0, JUNK + 4096), R("TG", 16 * (t % 2), 16 * (t % 2) + 16)), R("SV", 256 * (t % 2), 256 * (t % 2) + 256))

    def second(t, h, q):
        stage[0] = ("d%d" % q, t, h)
        if PLAN["fu"] == "W":
            if q:
                d = pA(h, 2)
                msum(d, [(M("ON"), M("C512"))] + [(R(d[0], d[1] + k, d[2], 16), R("AE%d" % h, k, 2048, 16), R("WV", 40, 48)) for k in range(16)])
                tt(d, d, hb(h, GG), A.mult)
                tt(hi(h, B1), d, hf(h, YY), A.add)
                ts(hi(h, B2), hi(h, B1), 5, 4095, A.arith_shift_right, A.bitwise_and)
                tt(hf(h, PW), pC(h, 1), hi(h, B2), A.add)
            return
        w = (64 * q, 64 * q + 64)
        d = R("pb%d" % (4 + 2 * h + q), 320, 384)
        if PLAN["se"][h] == "H":
            d = R("pb%d" % (4 + 2 * h), 256 + 64 * q, 320 + 64 * q)
        msum(d, [(M("ON"), M("C512")[:2] + (M("C512")[1] + 64, 1, 128))] + [(win("Z32", k), R("AE%d" % h, 1024 * q + k, 1024 * q + 1024, 16)) for k in range(16)])
        if PLAN["se"][h] == "H":
            if q == 0:
                return
            d, w = pA(h, 2), (0, 128)
        tt(d, d, hb(h, GL, *w), A.mult)
        tt(hi(h, B1, *w), d, hf(h, YY, *w), A.add)
        ts(hi(h, B2, *w), hi(h, B1, *w), 5, 4095, A.arith_shift_right, A.bitwise_and)
        tt(hf(h, PL, *w) if PLAN["pl"][h] == "T" else R("pb%d" % (2 + h), 128 + w[0], 128 + w[1]), R("pb%d" % (2 + h), 384 + w[0], 384 + w[1]), hi(h, B2, *w), A.add)

    def back(t, h):
        stage[0] = ("back", t, h)
        np_ = int(PLAN["np"][h])
        if PLAN["fu"] == "W":
            twice = PLAN["pl"][h] == "T"
            if twice:
                mm(pA(h, 3), hf(h, PW), M("IDF"))
            for j in range(np_):
                mm(pC(h, 1 + j), hf(h, PW), M("IDF"))
            lin(PLAN["pl"][h].replace("T", "S"), hf(h, PL), pA(h, 3) if twice else pC(h, 1), 1.0, 0.0)
        elif PLAN["pl"][h] == "T":
            for j in range(np_):
                mm(pC(h, 1 + j), M("IDF"), hf(h, PL))
        else:
            lin(PLAN["pl"][h], hf(h, PL), pC(h, 1), 1.0, 0.0)
            if np_ == 2:
                lin(PLAN["pl"][h], pC(h, 2), pC(h, 1), 1.0, 0.0)
        for j in range(np_):
            mm(pA(h, j), M("DUP"), hf(h, PL))
        last = t == VISITS - 1
        o = pB(h, 3)
        one = PLAN["sn"] == 1 and not last
        gr = ("slots", t, h) if one else None
        if one:
            mm(R(o[0], o[1], o[1] + 64), M("ON"), R("CM", M("MON")[1], M("MON")[1] + 64), True, False, gr)
        for s in (list(range(8, 12)) + list(range(8)) if last else range(12)):
            c = s if h or s >= 8 else 7 - s
            pr = R("PD%d" % h, 128 * c, 128 * c + 128)
            if s % np_ == 0:
                c0 = c - c % np_
                src = R("pb%d" % (2 + h), 128, 128 + 128 * np_) if s < 8 else R("pb%d" % (4 + 2 * h), 0, 128 * np_)
                tt(R("PD%d" % h, 128 * c0, 128 * (c0 + np_)), src, mask(h, s, np_), A.mult)
            if s < 8:
                mm(R(o[0], o[1] + s, o[1] + 64, 8), pr, R("SGF", 0, 8) if last else R("SGF", 7, 15), not one, not one, gr)
            else:
                mm(R(o[0], o[1] + 56 + s, o[1] + 128, 4), pr, R("SGD", 0, 16) if last else R("SGD", 14, 30), not one, not one or s == 11, gr)
        sn = "SN%d%d" % (t, h)
        stage[0] = ("send", t, h)
        if one:
            lin(PLAN["sc"][h], R(sn, 0, 128), o, 1.0, 0.0)
        else:
            lin(PLAN["sc"][h], R(sn, 0, 64), R(o[0], o[1], o[1] + 64), 1.0, -1.0)
            lin(PLAN["sc"][h], R(sn, 64, 128), R(o[0], o[1] + 64, o[1] + 128), 1.0, 0.0)
        ro, rv, rx = "RO%d%d" % (t, h), "RV%d%d" % (t, h), "rx%d%d" % (t, h)
        d1, r1, p1 = addr(1)
        d2, r2, p2 = addr(2)
        e1, e2 = topo.engines(core, d1), topo.engines(core, d2)
        sends[0] += 8
        if last:
            m = bits(e1[:8])
            return add("G", lambda: g.remote_dma(out_ap=T[rv][:], in_ap=ap(R(sn, 64, 128)), remote_sem=T.sem[rx], local_sem=T.sem["sent"], pid=p1, routing_id=r1, dma_engine_mask=m),
                       [R(sn, 64, 128)], [], 1000.0, dma="sent", lat=NET)
        m1, m2 = bits(e1[:4]), bits([e for e in e2 if e not in e1[:4]][:4])

        def fused():
            return g.remote_dma_fused([
                RemoteDMATransfer(dst_ids=[DstId(rid=r1, pnc=p1)], dma_engine_mask=m1, remote_sem=T.sem[rx], src=ap(R(sn, 0, 64)), dst=T[ro][:]),
                RemoteDMATransfer(dst_ids=[DstId(rid=r2, pnc=p2)], dma_engine_mask=m2, remote_sem=T.sem[rx], src=ap(R(sn, 64, 128)), dst=T[rv][:]),
            ], local_sem=T.sem["sent"])
        return add("G", fused, [R(sn, 0, 128)], [], 1200.0, dma="sent", lat=NET)

    arr = {}

    def arrive(t, h):
        if t == 0:
            stage[0] = ("load", 0, h)
            start_words(h)
        else:
            stage[0] = ("join", t, h)
            q = "%d%d" % (t - 1, h)
            join(h, R("RO" + q, 0, 64), R("RV" + q, 0, 64), [("rx" + q, 8)], [arr[h]])
            offsets(h)
    for t in range(VISITS):
        arrive(t, 0)
        s0 = front(t, 0)
        for q in (0, 1):
            middle(t, 0, q)
        arrive(t, 1)
        s1 = front(t, 1)
        for q in (0, 1):
            second(t, 0, q)
        places(t, 0, s0)
        arr[0] = back(t, 0)
        first(t)
        for q in (0, 1):
            middle(t, 1, q)
        if not PLAN["early"]:
            mean(t)
        if t < VISITS - 1 or NX == 1:
            stage[0] = ("wr2", t, 1)
            write(t, t)
        for q in (0, 1):
            second(t, 1, q)
        places(t, 1, s1)
        arr[1] = back(t, 1)
    stage[0] = ("wr", VISITS - 1, 1)
    add("Q", lambda: g.sync.dma_start(T.yx[:], ap(R("X%d" % (VISITS % NX), 0, 4096))), [R("X%d" % (VISITS % NX), 0, 4096)], [], 100.0, dma="dm10", lat=8000.0)
    for h in (0, 1):
        stage[0] = ("join", VISITS, h)
        q = "%d%d" % (VISITS - 1, h)
        join(h, R("SN" + q, 0, 64), R("RV" + q, 0, 64), [("rx" + q, 8)], [arr[h]])
        cp(hf(h, NM), hi(h, NMI))
        mm(pB(h, 0), hf(h, NM), M("IDF"))
        ts(hb(h, LV), pB(h, 0), DEAD, None, A.is_lt)
        tt(R("YL", 128 * h, 128 * h + 128), pB(h, 0), hb(h, LV), A.mult)
        mm(R("pb%d" % (4 + 2 * h), 0, 128, 1, 8), R("SGB", 0, 8), hb(h, LV))
        act(R("YN", 128 * h, 128 * h + 128, 1, 8), R("pb%d" % (4 + 2 * h), 0, 128, 1, 8), F.Copy)
    dma("Q", ("yl", None), R("YL", 0, 256))
    dma("S", ("yn", None), R("YN", 0, 256, 1, 8))
    return ops, sends[0]


def _pass(ops, links, prio, at):
    n = len(ops)
    npred = [0] * n
    for i in range(n):
        for (k, lg) in links[i]:
            npred[k] += 1
    ready = {e: [] for e in "VSTGQ"}
    for i in range(n):
        if npred[i] == 0:
            ready[ops[i]["eng"]].append(i)
    free = {e: 0.0 for e in ready}
    order = []
    start = [0.0] * n
    while len(order) < n:
        t0, e = min((max(free[e], min(at[i] for i in ready[e])), e) for e in ready if ready[e])
        i = max(ready[e], key=lambda k: (prio[k] - PLAN["wait"] * max(0.0, at[k] - t0), -k))
        t0 = max(t0, at[i])
        ready[e].remove(i)
        start[i] = t0
        order.append(i)
        free[e] = t0 + ops[i]["cost"]
        for (k, lg) in links[i]:
            at[k] = max(at[k], t0 + lg)
            npred[k] -= 1
            if npred[k] == 0:
                ready[ops[k]["eng"]].append(k)
    return order, start, max(start[i] + ops[i]["cost"] + (ops[i]["lat"] or 0.0) for i in range(n))


def schedule(ops):
    n = len(ops)
    succ = [[] for _ in range(n)]
    pred = [[] for _ in range(n)]
    for i in range(n):
        b = ops[i]
        for j, hard in b["deps"].items():
            a = ops[j]
            if not hard and j not in b["after"]:
                lg = a["cost"] if a["eng"] == b["eng"] else 0.0
            elif a["lat"] is not None:
                lg = a["cost"] + a["lat"]
            else:
                lg = a["cost"] + (OWN if a["eng"] == b["eng"] else HOP)
            succ[j].append((i, lg))
            pred[i].append((j, lg - a["cost"] + b["cost"]))
    prio = [0.0] * n
    for i in range(n - 1, -1, -1):
        prio[i] = max([ops[i]["cost"] + (ops[i]["lat"] or 0.0)] + [prio[k] + lg for (k, lg) in succ[i]])
    for i in range(n):
        s = ops[i]["stage"]
        prio[i] += 1e6 if s[0] == "load" and ops[i]["eng"] != "S" else 100.0 * RANK[0].get("%s%d" % (s[0], s[2]), 0)
    more = [1e6 if o["stage"][0] == "load" and o["eng"] != "S" else 100.0 * RANK[1].get("%s%d" % (o["stage"][0], o["stage"][2]), 0) for o in ops]
    best = now = _pass(ops, succ, prio, [0.0] * n)
    for _ in range(PLAN["turns"]):
        back = _pass(ops, pred, [now[1][i] + ops[i]["cost"] + (ops[i]["lat"] or 0.0) for i in range(n)], [o["lat"] or 0.0 for o in ops])
        now = _pass(ops, succ, [back[1][i] + ops[i]["cost"] + more[i] for i in range(n)], [0.0] * n)
        if now[2] < best[2]:
            best = now
    return best


def rank_program(g, core, T, topo):
    if T.rank_of(core) is None:
        return
    ops, nsent = build(g, T, topo, core)
    order, start, free = schedule(ops)
    queue = {"V": g.vector, "S": g.scalar, "T": g.tensor, "G": g, "Q": g.sync}
    need = set()
    place = {i: p for p, i in enumerate(order)}
    for i in order:
        late = {}
        for j, hard in ops[i]["deps"].items():
            if hard and not ops[j]["dma"] and place[j] > place.get(late.get(ops[j]["eng"]), -1):
                late[ops[j]["eng"]] = j
        need.update(late.values())
    count = {e: 0 for e in queue}
    mark = {}
    know = {e: {} for e in queue}
    snap = {}
    for i in order:
        o = ops[i]
        e = o["eng"]
        want = {}
        for j, hard in o["deps"].items():
            if not hard or j not in mark:
                continue
            s, v = mark[j]
            if know[e].get(s, 0) < v:
                want.setdefault(s, []).append((v, j))
        todo = sorted(((max(l)[0], s, max(l)[1]) for s, l in want.items()), key=lambda x: -start[x[2]])
        for v, s, j in todo:
            if know[e].get(s, 0) >= v:
                continue
            queue[e].wait_ge(T.sem[s], v)
            know[e][s] = v
            for s2, v2 in snap[j].items():
                if know[e].get(s2, 0) < v2:
                    know[e][s2] = v2
        for (s, v) in o["waits"]:
            queue[e].wait_ge(T.sem[s], v)
        ins = o["fn"]()
        snap[i] = dict(know[e])
        if o["dma"] and o["dma"] != "sent":
            ins.then_inc(T.sem[o["dma"]], 16)
            mark[i] = (o["dma"], 16)
        elif i in need:
            count[e] += 1
            ins.then_inc(T.sem["e" + e], 1)
            mark[i] = ("e" + e, count[e])
    for e in ENGS:
        if count[e]:
            g.wait_ge(T.sem["e" + e], count[e])
    g.wait_ge(T.sem["sent"], nsent)
    for o in ops:
        if o["dma"] and o["dma"] != "sent":
            g.wait_ge(T.sem[o["dma"]], 16)
